import numpy as np, ml_dtypes
CORES = [6,15,38,47]
N = 4
BF = ml_dtypes.bfloat16
S, F, L, RO, A, TH, BYG = 4096, 1024, 256, 4, 960, 9, 0
def whole(x, hi):
    return np.minimum(x.astype(np.int64), hi)
def parts(rng):
    a = rng.choice(np.array([0.2, 0.3, 0.4, 0.5]), (N, 8, 1, 1)).astype(np.float32)
    t = whole(256 * rng.random((N, 8, 16, S), dtype=np.float32) ** a, 255)
    t = np.where(rng.random((N, 8, 1, S)) < 0.25, 255, t)
    return t, rng.integers(0, 255, (N, 8, 16, F)), rng.integers(0, S, (N, 8, 16, F)), rng.integers(0, S, (N, 8, 16, F))
def pack(t, z, eh, ef):
    return {"tab": t.reshape(N, 128, S).astype(np.float32).astype(BF), "zf": z.reshape(N, 128, F).astype(np.float32).astype(BF),
            "eh": np.ascontiguousarray(eh.reshape(N, 128, F)).astype(np.int32), "ef": np.ascontiguousarray(ef.reshape(N, 128, F)).astype(np.int32)}
def setup_inputs(rng):
    return pack(*parts(rng))
def setup_inputs_full(rng):
    t, z, eh, ef = parts(rng)
    for g in (0, 5):
        t[:, g] = 255; eh[:, g] = rng.integers(F, S, (N, 16, F)); ef[:, g] = rng.integers(F, S, (N, 16, F))
        eh[:, g, 0] = np.argsort(rng.random((N, F)), axis=1)
    f = np.arange(F); c = F - A; see = (f >= A - c) & (f < A)
    m = np.flatnonzero(see)
    for g in (2, 7):
        p = np.argsort(rng.random((N, S // 2)), axis=1)[:, :L]
        t[:, g] = 255; eh[:, g] = rng.integers(S // 2, S - 64, (N, 16, F)); ef[:, g] = rng.integers(S // 2, S - 64, (N, 16, F))
        z[:, g] = np.where(f < L, rng.integers(160, 255, (N, 16, F)), np.where(see, rng.integers(100, 160, (N, 16, F)), rng.integers(0, 100, (N, 16, F))))
        eh[:, g, 0] = np.where(see, eh[:, g, 0], p[:, f % L])
        for r in range(N):
            q = (r + 1 + (2 + BYG * g) % (N - 1)) % N
            a, b = m[1::4], m[3::4]
            ef[r, g, rng.integers(0, 16, len(a)), a] = p[q, L - c - 1]
            ef[r, g, rng.integers(0, 16, len(b)), b] = np.max(p[q])
    return pack(t, z, eh, ef)
def setup_inputs_ties(rng):
    t, z, eh, ef = parts(rng)
    pat = np.array([0, 0, 2, 3, 5, TH - 2, TH - 2, TH - 2, TH - 1, TH - 1, TH - 1, TH - 1, TH, TH, TH, 16])
    place = np.argsort(rng.random((N, 4, 16, S), dtype=np.float32), axis=2)
    t[:, :4] = np.where(place < pat[np.arange(S) % 16], 0, 255)
    for x in (eh, ef):
        top = rng.choice(np.array([8, 12, 12, 12, 15, 16]), (N, 4, 1, F))
        x[:, :4] = 16 * rng.integers(0, S // 16, (N, 4, 16, F)) + (rng.random((N, 4, 16, F)) * top).astype(np.int64)
    v = np.array([0, 1, 127, 128, 254, 255])
    t[:, 4:] = rng.choice(v, (N, 4, 16, S), p=[0.04, 0.04, 0.1, 0.12, 0.3, 0.4]); z[:, 4:] = rng.choice(v[:5], (N, 4, 16, F))
    return pack(t, z, eh, ef)
def setup_inputs_alike(rng):
    t, z, eh, ef = parts(rng); few = np.array([0, S - 1, S // 2, 3])
    eh[:, 0] = rng.choice(few, (N, 16, F)); eh[:, 1] = rng.integers(0, S, (N, 1, F))
    t[:, 2] = 255; eh[:, 2] = rng.integers(0, S, (N, 1, 1))
    eh[:, 3] = S - 1 - rng.integers(0, 12, (N, 16, F)); ef[:, 3] = S - 1 - rng.integers(0, 12, (N, 16, F))
    ef[:, 4] = rng.choice(few, (N, 16, F))
    for x in (z, eh, ef): x[:, 5, :, 1::2] = x[:, 5, :, 0::2]
    return pack(t, z, eh, ef)
def setup_inputs_hard(rng):
    t, z, eh, ef = parts(rng)
    t[:, 0] = 0; t[rng.integers(0, N), 1] = 0; t[:, 2] = 255
    z[:, 3] = 0; t[:, 3] = np.maximum(t[:, 3], 1)
    z[:, 4] = 254; t[:, 4] = np.where(rng.random((N, 16, S)) < 0.8, 255, t[:, 4])
    return pack(t, z, eh, ef)
def setup_inputs_spread(rng):
    u = np.float32(2) ** -rng.integers(-2, 6, (N, 8, 1, S)).astype(np.float32); v = np.float32(2) ** rng.integers(-2, 5, (N, 8, 1, F)).astype(np.float32)
    t = whole(256 * rng.random((N, 8, 16, S), dtype=np.float32) ** u, 255); z = whole(255 * rng.random((N, 8, 16, F), dtype=np.float32) ** v, 254)
    e = [whole(S * rng.random((N, 8, 16, F)) ** (2.0 ** rng.integers(0, 3, (N, 8, 16, 1))), S - 1) for i in range(2)]
    return pack(t, z, e[0], e[1])
def check_inputs(d):
    bad = []
    for k, hi in (("tab", 255), ("zf", 254), ("eh", S - 1), ("ef", S - 1)):
        v = np.asarray(d[k]).astype(np.float64)
        if not (np.min(v) >= 0 and np.max(v) <= hi): bad.append("range of " + k)
        if not np.all(v == np.floor(v)): bad.append("whole numbers in " + k)
    return bad
def reference(tab, zf, eh, ef):
    t = tab.astype(np.float32).astype(np.int32).reshape(N, 8, 16, S); z = zf.astype(np.float32).astype(np.int32).reshape(N, 8, 16, F)
    home = eh.astype(np.int64).reshape(N, 8, 16, F); far = ef.astype(np.int64).reshape(N, 8, 16, F)
    d = np.zeros((N, 8, F), np.int64); oc = np.full((N, 8, S), -1, np.int64); free = np.ones((N, 8, F), bool)
    for step in range(RO):
        old = np.array(t)
        turn = (np.arange(F) + A * step) % F
        for r in range(N):
            for g in range(8):
                q = (r + 1 + (step + BYG * g) % (N - 1)) % N
                ln = turn[free[r, g][turn]][:L]
                zl = z[r, g][:, ln]
                sh = (home[r, g][:, ln] + d[r, g, ln]) & (S - 1); sf = (far[r, g][:, ln] + d[r, g, ln]) & (S - 1)
                ph = np.sum(old[r, g][:, sh] <= zl[:, None, :], axis=0); pf = np.sum(old[q, g][:, sf] <= zl[:, None, :], axis=0)
                k = np.argmax(ph, axis=0)
                worst = np.maximum(np.max(ph, axis=0), np.max(pf, axis=0)); go = worst < TH
                d[r, g, ln] += np.where(go, 0, worst)
                cl = np.flatnonzero(go)
                s, first = np.unique(sh[k, np.arange(L)][cl], return_index=True)
                w = cl[first]; was = oc[r, g, s]; was = was[was >= 0]
                d[r, g, was] += 1; free[r, g, was] = True
                t[r, g][:, s] = zl[:, w]; oc[r, g, s] = ln[w]; free[r, g, ln[w]] = False
    return {"yt": t.reshape(N, 128, S).astype(np.float32).astype(BF), "yo": oc.astype(np.float32), "yd": d.astype(np.float32)}

@@ -1,0 +1,532 @@
+from concourse.mybir import AluOpType, ActivationFunctionType
+
+OP = AluOpType
+AF = ActivationFunctionType
+NB2 = 4
+NBV = 12 - NB2
+ZS = 8
+W1 = 131072.0
+BASE = 640
+WT = 4096 + 1024
+SB = "sbuf"
+F32, B16, F16, I32, U16 = "float32", "bfloat16", "float16", "int32", "uint16"
+SCRATCH = {}
+for _names, _w, _d in (
+        ("TAB", WT, B16), ("OCC", WT, F32), ("ST", 1024 + WT, B16), ("EHT EFT", 1024, I32), ("ZFT", 1024, B16),
+        ("IOT YD", 1024, F32), ("JM", 768, F32), ("QX", 144, F32), ("Q4", 128, F32), ("TMPF", 1024, F32), ("KCF JR M0 MI SCM SH SF WA WB YS Y1 Y2", 256, F32),
+        ("PJ", 4, I32), ("PC", 8, F32), ("CI", 96, I32), ("CLA", 16, U16), ("CLB", 12, U16), ("DW C1", 48, I32), ("CJ2 WS", 192, F32),
+        ("XV XS", 144, B16), ("X1", 144, F16), ("BO", 128, F16), ("BO16 BOB NID PID ZT1 ZT2", 128, B16), ("RO", 2048, B16), ("EX", 1024, B16),
+        ("KC JRI", 256, B16), ("M0H", 768, F16), ("HH EE CO", 3072, B16), ("HF", 8, F32), ("SEH SEF", 192, U16), ("DL STN BN", 256, B16),
+        ("EHO EFO", 256, U16), ("EI EM FI FM", 192, I32), ("ZX", 256 * NBV, B16), ("GB0 GB1", 1024, B16),
+        ("IW", 64, I32), ("WF", 256, F32), ("KW NG INC", 16, B16), ("OH MSK SR", 256, F16), ("BL", 16, U16),
+        ("FB VB", 784, F16), ("VW", 768, F16), ("VC", 8, F32), ("II", 288, I32), ("LU", 48, U16),
+        ("ZL0 ZL1 ZL2 ZL3 RZ1 RZ2 RZ3", 256, B16), ("EHH0 EHH1 EHH2 EHH3", 256, F16), ("LW0 LW1 LW2 LW3", BASE + 1024, F32),
+        ("FL0 FL1 FL2 FL3 WL0 WL1 WL2 WL3 RL1 RL2 RL3", 16, U16), ("FT0", 4096, B16), ("FT1 FT2 FT3", WT, B16)):
+    for _n in _names.split():
+        SCRATCH[_n] = (SB, [128, _w], _d)
+for _n, _w in (("CH", NBV), ("CF", NBV), ("S1H", 4), ("S1F", 4), ("S2H", 4), ("S2F", 4)):
+    SCRATCH[_n] = (SB, [128, _w, 256], B16)
+for _n in ("KH", "KF", "D0", "D1", "SRP", "KRP", "SWP"):
+    SCRATCH[_n] = ("psum", [128, 512], F32)
+SCRATCH["ZTP"] = ("psum", [128, 1024], B16)
+SEMAPHORES = ["cv", "cs", "cp", "cg"] + ["ld%d" % _i for _i in range(12)] + ["sn%d" % _i for _i in range(4)] + ["loc%d" % _i for _i in range(16)]
+SEMAPHORES += ["rz%d" % _i for _i in range(4)] + ["rl%d" % _i for _i in range(4)] + ["out%d" % _i for _i in range(8)]
+WIDX = {n: 16 * i for i, n in enumerate("SW NSW SD DTT WM GO NO WN GSD ND XW YW WN2 DT0 DT2".split())}
+
+
+def make(g, T):
+    eng = {"v": g.vector, "s": g.scalar, "p": g.tensor, "g": g, "y": g.sync}
+    sem = {"v": "cv", "s": "cs", "p": "cp", "g": "cg"}
+    cnt = {"v": 0, "s": 0, "p": 0, "g": 0}
+    know = {e: {} for e in eng}
+    acc, total = {}, {}
+
+    def learn(e, tok):
+        for k, v in tok[3].items():
+            know[e][k] = max(v, know[e].get(k, 0))
+        know[e][tok[0]] = max(tok[1], know[e].get(tok[0], 0))
+
+    def psum(b):
+        return b in SCRATCH and SCRATCH[b][0] == "psum"
+
+    def needs(owner, reads, writes):
+        out = []
+        for mode, lst in (("r", reads), ("w", writes)):
+            for (b, lo, hi) in lst:
+                ps = psum(b)
+                for (l2, h2, m2, tok) in acc.get(b, []):
+                    if not ps and (h2 <= lo or hi <= l2):
+                        continue
+                    if mode == "r" and m2 == "r" and not ps:
+                        continue
+                    if tok[2] == owner and not (mode == "r" and m2 == "w"):
+                        continue
+                    out.append(tok)
+        return out
+
+    def waits(e, toks):
+        for tok in sorted(toks, key=lambda x: (-len(x[3]), -x[1])):
+            if know[e].get(tok[0], 0) < tok[1]:
+                top = max([x for x in toks if x[0] == tok[0]], key=lambda x: x[1])
+                eng[e].wait_ge(T.sem[top[0]], top[1])
+                learn(e, top)
+
+    def note(tok, reads, writes):
+        for (b, lo, hi) in writes:
+            lst = acc.setdefault(b, [])
+            if not psum(b):
+                lst[:] = [x for x in lst if not (lo <= x[0] and x[1] <= hi)]
+            else:
+                lst[:] = [x for x in lst if not (x[3][2] == tok[2] and x[2] == "w" and lo <= x[0] and x[1] <= hi)]
+            lst.append((lo, hi, "w", tok))
+        for (b, lo, hi) in reads:
+            lst = acc.setdefault(b, [])
+            lst[:] = [x for x in lst if not (x[2] == "r" and x[3][0] == tok[0] and lo <= x[0] and x[1] <= hi)]
+            lst.append((lo, hi, "r", tok))
+
+    def op(e, reads, writes, fn):
+        waits(e, needs(e, reads, writes))
+        cnt[e] += 1
+        fn(eng[e]).then_inc(T.sem[sem[e]], 1)
+        total[sem[e]] = cnt[e]
+        note((sem[e], cnt[e], e, dict(know[e])), reads, writes)
+
+    def dma(e, s, reads, writes, fn):
+        waits(e, needs("dma" + s, reads, writes))
+        fn(eng[e]).then_inc(T.sem[s], 16)
+        total[s] = total.get(s, 0) + 16
+        note((s, total[s], "dma" + s, dict(know[e])), reads, writes)
+
+    def send(s, n, reads, fn):
+        waits("g", needs("rem" + s, reads, []))
+        fn(g)
+        total[s] = total.get(s, 0) + n
+        note((s, total[s], "rem" + s, dict(know["g"])), reads, [])
+
+    def land(s, n, b, lo, hi):
+        total[s] = total.get(s, 0) + n
+        acc.setdefault(b, []).append((lo, hi, "w", (s, total[s], "net" + s, {})))
+
+    def finish():
+        for s, v in total.items():
+            if know["g"].get(s, 0) < v:
+                g.wait_ge(T.sem[s], v)
+    return op, dma, send, land, finish
+
+
+def rank_program(g, core, T, topo):
+    rank = T.rank_of(core)
+    if rank is None:
+        return
+    op, dma, send, land, finish = make(g, T)
+    cores = T.cores
+
+    def put(dst_buf, lo, hi, src_buf, peer, rsem, lsem):
+        dst = cores[peer]
+        rid, pid, _se = topo.addr(dst)
+        send(lsem, len(topo.engines(core, dst)), [(src_buf, lo, hi)],
+             lambda e: e.remote_dma(T[dst_buf][:, lo:hi], T[src_buf][:, lo:hi], T.sem[rsem], T.sem[lsem], pid, rid, topo.mask(core, dst)))
+
+    def asker(t):
+        return (rank - 1 - t % 3) % 4
+
+    def nin(t):
+        return len(topo.engines(cores[(rank + 1 + t % 3) % 4], core))
+
+    def A(x):
+        return T[x[0]][:, x[1]:x[2]]
+
+    def w(n, a=0, b=16):
+        return ("WF", WIDX[n] + a, WIDX[n] + b)
+
+    def ts(o, i, s1, o0, s2=None, o1=None, ia=None, more=()):
+        rd = [i] + list(more)
+        src = A(i) if ia is None else ia
+        if o1 is None:
+            op("v", rd, [o], lambda e: e.tensor_scalar(A(o), src, s1, None, o0))
+        else:
+            op("v", rd, [o], lambda e: e.tensor_scalar(A(o), src, s1, s2, o0, o1))
+
+    def tt(o, a, b, f, ia=None, ib=None, more=(), oa=None):
+        op("v", [a, b] + list(more), [o], lambda e: e.tensor_tensor(A(o) if oa is None else oa, A(a) if ia is None else ia, A(b) if ib is None else ib, f))
+
+    def cp(o, i, ia=None, oa=None, more=(), e="v"):
+        src, out = A(i) if ia is None else ia, A(o) if oa is None else oa
+        if e == "v":
+            op("v", [i] + list(more), [o], lambda e: e.tensor_copy(out, src))
+        else:
+            op("s", [i] + list(more), [o], lambda e: e.activation(out, src, AF.Copy))
+
+    def gather(o, win, lst, e="v", bias=None):
+        if bias is None:
+            cp(o, win, ia=A(win).indirect(A(lst)), more=[lst], e=e)
+        else:
+            op("s", [win, lst], [o], lambda e: e.activation(A(o), A(win).indirect(A(lst)), AF.Identity, bias=bias))
+
+    def scatter(win, lst, i, more=()):
+        cp(win, i, oa=A(win).indirect(A(lst)), more=[lst, win] + list(more))
+
+    def scan(o, d0, d1, init, o0, o1):
+        op("v", [d0, d1], [o], lambda e: e.tensor_tensor_scan(A(o), A(d0), A(d1), init, o0, o1))
+
+    def mm(o, l, r, start, stop, oa=None, la=None, ra=None):
+        op("p", [l, r], [o], lambda e: e.matmul(A(o) if oa is None else oa, A(l) if la is None else la, A(r) if ra is None else ra, start, stop))
+
+    def iota(o, pattern, base, cm=0):
+        op("g", [], [o], lambda e: e.iota(A(o), pattern, base, cm, allow_small_or_imprecise_dtypes=True))
+
+    def memset(o, v):
+        op("v", [], [o], lambda e: e.memset(A(o), v))
+
+    def load(n, dst, lo, hi, src, a, b):
+        dma("y", "ld%d" % n, [], [(dst, lo, hi)], lambda e: e.dma_start(T[dst][:, lo:hi], T[src][:, a:b]))
+    load(0, "EHT", 192, 448, "eh", 0, 256)
+    load(1, "ZFT", 192, 448, "zf", 0, 256)
+    load(2, "TAB", 0, 2048, "tab", 0, 2048)
+    load(3, "TAB", 2048, 4096, "tab", 2048, 4096)
+    load(4, "EFT", 192, 448, "ef", 0, 256)
+    for k, (dst, src) in enumerate((("EHT", "eh"), ("ZFT", "zf"), ("EFT", "ef"))):
+        load(5 + 2 * k, dst, 0, 192, src, 832, 1024)
+        load(6 + 2 * k, dst, 448, 1024, src, 256, 832)
+    for t in range(4):
+        land("sn%d" % t, nin(t) * (2 if t == 0 else 1), "FT%d" % t, 0, 4096)
+    for t in range(1, 4):
+        land("rz%d" % t, nin(t), "RZ%d" % t, 0, 256)
+        land("rl%d" % t, nin(t), "RL%d" % t, 0, 16)
+
+    pc = ("PC", 0, 4)
+    iota(("PJ", 0, 1), [[0, 1]], 0, 1)
+    iota(("CI", 0, 16), [[-16, 16]], 255)
+    iota(("CI", 32, 44), [[-16, 12]], 191)
+    iota(("QX", 0, 144), [[1, 144]], -15)
+    iota(("Q4", 0, 128), [[16, 8], [0, 16]], 0)
+    iota(("KCF", 0, 256), [[0, 16], [-8192, 16]], 122880)
+    ts(("PJ", 2, 3), ("PJ", 0, 1), 15, OP.bitwise_and)
+    ts(("PJ", 3, 4), ("PJ", 0, 1), 4, OP.arith_shift_right)
+    cp(("PC", 0, 1), ("PJ", 2, 3))
+    cp(("PC", 1, 2), ("PJ", 0, 1))
+    ts(("PC", 2, 3), ("PJ", 3, 4), 16.0, OP.mult)
+    ts(("PC", 3, 4), ("PJ", 2, 3), -1.0, OP.mult, 15.0, OP.add)
+    PI_, PP, PG, P15 = T.PC[:, 0:1], T.PC[:, 1:2], T.PC[:, 2:3], T.PC[:, 3:4]
+    ts(("CLA", 0, 16), ("CI", 0, 16), PI_, OP.subtract, more=[pc])
+    ts(("CLB", 0, 12), ("CI", 32, 44), PI_, OP.subtract, more=[pc])
+    memset(("HF", 0, 1), 0.5)
+    qx = ("QX", 15, 143)
+    ts(("NID", 0, 128), qx, PP, OP.is_equal, -1.0, OP.mult, more=[pc])
+    ts(("PID", 0, 128), qx, PP, OP.is_equal, more=[pc])
+    for n, f in (("XV", W1), ("XS", W1 / 2)):
+        ts((n, 0, 144), ("QX", 0, 144), PG, OP.is_equal, f, OP.mult, more=[pc])
+    ts(("BO16", 0, 128), ("Q4", 0, 128), PG, OP.is_equal, 0.0625, OP.mult, more=[pc])
+    cp(("KC", 0, 16 * NBV), ("KCF", 0, 16 * NBV))
+    ts(("KC", 16 * NBV, 256), ("KCF", 16 * NBV, 256), 8 * W1, OP.add)
+    gather(("ZL0", 0, 256), ("ZFT", 192, 448), ("CLA", 0, 16), e="s")
+    gather(("EHO", 0, 256), ("EHT", 192, 448), ("CLA", 0, 16))
+    iota(("TMPF", 0, 1024), [[1, 64], [0, 16]], 0)
+    ts(("EX", 0, 1024), ("TMPF", 0, 1024), PP, OP.is_equal, more=[pc])
+    iota(("LW0", BASE, BASE + 256), [[-1, 256]], 447)
+    iota(("JM", 0, 768), [[0, 48], [1, 16]], 0)
+    iota(("JR", 0, 256), [[1, 256]], 0)
+    for h in range(2):
+        put("FT0", 2048 * h, 2048 * h + 2048, "TAB", asker(0), "sn0", "loc0")
+    put("FT1", 0, 4096, "TAB", asker(1), "sn1", "loc1")
+    put("RZ1", 0, 256, "ZL0", asker(1), "rz1", "loc4")
+    iota(("CI", 48, 96), [[16, 48]], 65)
+    iota(("OCC", 0, WT), [[1, WT]], 1024)
+    iota(("IOT", 0, 1024), [[1, 1024]], 0)
+    iota(("CJ2", 0, 192), [[-2, 192]], 382)
+    for t in range(1, 4):
+        iota(("LW%d" % t, BASE + 192, BASE + 256), [[-1, 64]], 255 - 64 * t)
+
+    def constants_1():
+        for (o, i, f) in ((("M0", 0, 256), ("JM", 0, 256), OP.not_equal), (("MI", 0, 256), ("JM", 0, 256), OP.is_equal)):
+            ts(o, i, PI_, f, more=[pc])
+        ts(("SCM", 0, 256), ("JM", 0, 256), 0.5, OP.is_gt)
+        ts(("BOB", 0, 128), ("Q4", 0, 128), PG, OP.is_equal, more=[pc])
+        for c in range(16):
+            ts(("RO", 128 * c, 128 * c + 128), ("BOB", 0, 128), T.MI[:, c:c + 1], OP.mult, more=[("MI", 0, 256)])
+        ts(("JRI", 0, 256), ("JR", 0, 256), PI_, OP.subtract, more=[pc])
+        ts(("BO", 0, 128), ("Q4", 0, 128), PG, OP.is_equal, more=[pc])
+        ts(("X1", 0, 144), ("QX", 0, 144), PG, OP.is_equal, more=[pc])
+        ts(("EHH0", 0, 256), ("EHO", 0, 256), -2048.0, OP.add)
+
+    def constants_s():
+        for m in range(16):
+            lo, n, a = (256 * m, 256, 0) if m < 8 else (2048 + 128 * (m - 8), 128, 128)
+            op("s", [("JRI", a, 256)], [("HH", lo, lo + n)], lambda e: e.activation(T.HH[:, lo:lo + n], T.JRI[:, a:a + n], AF.Sign, bias=16.0 * m + 0.5, scale=-1.0))
+
+    def constants_2():
+        memset(("EE", 0, 3072), 1.0)
+        memset(("ST", 0, 1024), 0.0)
+        memset(("DL", 0, 256), 0.0)
+        ts(("DW", 0, 48), ("CI", 48, 96), PI_, OP.add, more=[pc])
+        ts(("C1", 0, 48), ("DW", 0, 48), float(BASE + 191), OP.add)
+        ts(w("DT0"), ("DW", 0, 16), float(4096 - 65), OP.add)
+        ts(("FL0", 0, 16), ("CLA", 0, 16), 192.0, OP.add)
+        for (o, tab) in (("SEH", "EHT"), ("SEF", "EFT")):
+            gather((o, 0, 192), (tab, 0, 192), ("CLB", 0, 12))
+        for t in range(1, 4):
+            x, l = 64 * (t - 1), ("CLB", 4 * t - 4, 4 * t)
+            ts(("EHH%d" % t, 192, 256), ("SEH", x, x + 64), -2048.0, OP.add)
+            gather(("ZL%d" % t, 192, 256), ("ZFT", 0, 192), l, e="s")
+            cp(("FL%d" % t, 12, 16), l)
+        ts(("M0H", 0, 768), ("JM", 0, 768), PI_, OP.not_equal, more=[pc])
+
+    gbn = [0]
+
+    def zt(t, j0, j1, dst):
+        n, zl = j1 - j0, "ZL%d" % t
+        op("p", [(zl, j0, j1), ("PID", 0, 128)], [("ZTP", 0, 128)], lambda e: e.transpose(T.ZTP[0:n, 0:128], T[zl][:, j0:j1], T.PID[:, :]))
+        cp((dst, 0, 128), ("ZTP", 0, 128), ia=T.ZTP[0:n, 0:128], oa=T[dst][0:n, :], e="s")
+
+    def s_gather(win, lst, c0, c1):
+        gb = "GB%d" % (gbn[0] % 2)
+        gbn[0] += 1
+        gather((gb, 0, 16 * (c1 - c0)), (win, 0, 4096), (lst, c0, c1), e="s")
+        return gb
+
+    def s_diff(gb, ztb, nl):
+        for h in range(nl // 32):
+            x = 512 * h
+            mm(("D%d" % h, 0, 512), (ztb, 0, 128), ("EX", x, x + 512), True, False, la=T[ztb][0:nl, :], ra=T.EX[0:nl, x:x + 512])
+        for h in range(nl // 32):
+            x = 512 * h
+            mm(("D%d" % h, 0, 512), ("NID", 0, 128), (gb, x, x + 512), False, True)
+
+    def s_sign(dst, nl):
+        for m in range(nl // 16):
+            d, x = "D%d" % (m // 2), 256 * (m % 2)
+            op("s", [(d, x, x + 256), ("HF", 0, 1)], [(dst, 256 * m, 256 * m + 256)], lambda e: e.activation(T[dst][:, m, :], T[d][:, x:x + 256], AF.Sign, bias=T.HF[:, 0:1]))
+
+    def sums(key, src, b0, b1, m0, xw, last):
+        for c in range(16):
+            mm((key, 16 * (m0 + b0), 16 * (m0 + b1)), (xw, 0, 144), (src, 256 * b0, 256 * b1), False, last and c == 15,
+               la=T[xw][:, 15 - c:143 - c], ra=T[src][:, b0:b1, 16 * c:16 * c + 16])
+
+    def key_open(key):
+        mm((key, 0, 256), ("BO16", 0, 128), ("KC", 0, 256), True, False)
+
+    def v_block(dst, win, lst, b):
+        l, x = (lst, 16 * b, 16 * b + 16), (256 * b, 256 * b + 256)
+        tt((dst, x[0], x[1]), (win, 0, 4096), ("ZX", x[0], x[1]), OP.is_le, ia=T[win][:, 0:4096].indirect(A(l)), more=[l], oa=T[dst][:, b, :])
+
+    def spread(src, dst, start=True):
+        for c in range(16):
+            mm((dst, 0, 256), ("RO", 128 * c, 128 * c + 128), (src, 0, 16), start, start or c == 15, oa=T[dst][:, c:256:16])
+
+    nb2j = 192 - 16 * NB2
+
+    def fresh(t):
+        return ("EHO", "EFO", 192) if t == 0 else ("SEH", "SEF", 64 * (t - 1))
+
+    def fresh_home(t):
+        lst, _f, c0 = fresh(t)
+        zt(t, 192, 256, "ZT1")
+        gb = s_gather("TAB", lst, c0, c0 + 64)
+        s_diff(gb, "ZT1", 64)
+        s_sign("S1H", 64)
+        key_open("KH")
+        sums("KH", "S1H", 0, 4, 12, "XS", False)
+
+    def fresh_foreign(t):
+        _h, lst, c0 = fresh(t)
+        gb = s_gather("FT%d" % t, lst, c0, c0 + 64)
+        key_open("KF")
+        s_diff(gb, "ZT1", 64)
+        s_sign("S1F", 64)
+        sums("KF", "S1F", 0, 4, 12, "XS", False)
+
+    def expand(t):
+        for kk in range(16):
+            cp(("ZX", 0, 256 * NBV), ("ZL%d" % t, 0, 16 * NBV), oa=T.ZX[:, kk:256 * NBV:16], e="s" if kk < ZS else "v")
+
+    def step_main(t):
+        ft, half = "FT%d" % t, (NBV + 1) // 2
+        if t:
+            expand(t)
+        for b in range(NBV):
+            v_block("CH", "TAB", "EHO", b)
+        zt(t, nb2j, 192, "ZT2")
+        ga = s_gather("TAB", "EHO", nb2j, 192)
+        if t:
+            gb = s_gather(ft, "EFO", nb2j, 192)
+        s_diff(ga, "ZT2", 16 * NB2)
+        s_sign("S2H", 16 * NB2)
+        sums("KH", "CH", 0, half, 0, "XV", False)
+        sums("KH", "S2H", 0, NB2, NBV, "XS", False)
+        sums("KH", "CH", half, NBV, 0, "XV", True)
+        if t == 0:
+            gather(("EFO", 0, 256), ("EFT", 192, 448), ("CLA", 0, 16))
+            constants_1()
+            constants_s()
+            claim_slots_1(t)
+            fresh_foreign(0)
+            gb = s_gather(ft, "EFO", nb2j, 192)
+        s_diff(gb, "ZT2", 16 * NB2)
+        s_sign("S2F", 16 * NB2)
+        for b in range(half):
+            v_block("CF", ft, "EFO", b)
+        if t:
+            claim_slots_1(t)
+        sums("KF", "CF", 0, half, 0, "XV", False)
+        for b in range(half, NBV):
+            v_block("CF", ft, "EFO", b)
+        if t == 0:
+            constants_2()
+        claim_slots_2(t)
+        sums("KF", "S2F", 0, NB2, NBV, "XS", False)
+        sums("KF", "CF", half, NBV, 0, "XV", True)
+
+    def claim_slots_1(t):
+        scan(("SH", 0, 256), ("SCM", 0, 256), ("KH", 0, 256), 0.0, OP.mult, OP.max)
+        cp(("IW", 0, 16), ("SH", 0, 256), ia=T.SH[:, 15:256:16])
+        ts(("IW", 16, 32), ("IW", 0, 16), 13, OP.arith_shift_right, 15, OP.bitwise_and)
+        cp(("KW", 0, 16), ("IW", 16, 32))
+        spread("KW", "KRP")
+
+    def claim_slots_2(t):
+        ts(("OH", 0, 256), ("KRP", 0, 256), P15, OP.is_equal, more=[pc])
+        tt(("MSK", 0, 256), ("OH", 0, 256), ("EHH%d" % t, 0, 256), OP.mult)
+        mm(("SRP", 0, 256), ("BO", 0, 128), ("MSK", 0, 256), True, False)
+        for i in range(16):
+            mm(("SWP", 0, 16), ("X1", 15 - i, 143 - i), ("MSK", 0, 256), i == 0, i == 15, ra=T.MSK[:, i:256:16])
+        op("s", [("SWP", 0, 16)], [w("NSW")], lambda e: e.activation(A(w("NSW")), T.SWP[:, 0:16], AF.Copy, scale=-1.0))
+        ts(w("DTT"), w("DT0"), float(256 * t), OP.add)
+        ts(w("DT2"), w("DT0"), float(256 * t - 2048), OP.add)
+
+    def step_claims(t):
+        wl = ("WL%d" % t, 0, 16)
+        cp(w("SW"), ("SWP", 0, 16))
+        tt(w("SD"), w("SW"), w("DT2"), OP.subtract)
+        scan(("SF", 0, 256), ("SCM", 0, 256), ("KF", 0, 256), 0.0, OP.mult, OP.max)
+        tt(w("WM"), ("SH", 0, 256), ("SF", 0, 256), OP.max, ia=T.SH[:, 15:256:16], ib=T.SF[:, 15:256:16])
+        ts(("NG", 0, 16), w("WM"), 9 * W1, OP.is_ge, 8192.0, OP.mult)
+        spread("NG", "SRP", False)
+        ts(w("GO"), w("WM"), 9 * W1, OP.is_lt)
+        ts(w("NO"), w("WM"), 9 * W1, OP.is_ge)
+        cp(("IW", 32, 48), w("WM"))
+        tt(w("GSD"), w("GO"), w("SD"), OP.mult)
+        ts(("IW", 48, 64), ("IW", 32, 48), 17, OP.arith_shift_right)
+        cp(("SR", 0, 256), ("SRP", 0, 256))
+        for m in (0, 15, 1, 14, 2, 13, 3, 12, 11, 10, 9, 8, 4, 5, 6, 7):
+            end = 256 * m + 256 if m < 8 else 2048 + 128 * (m - 7)
+            o, i = ("EE", end - 256 + 16 * m, end), (16 * m, 256)
+            if m < 4:
+                op("s", [("SRP", i[0], 256), w("NSW")], [o], lambda e: e.activation(A(o), T.SRP[:, i[0]:256], AF.Abs, bias=A(w("NSW", m, m + 1))))
+            else:
+                ts(o, ("SR", i[0], 256), A(w("SW", m, m + 1)), OP.not_equal, more=[w("SW")])
+        tt(w("WN"), ("IW", 48, 64), w("NO"), OP.mult)
+        for (lo, hi, st, a) in ((2048, 3072, 128, 8), (0, 2048, 256, 0)):
+            scan(("CO", lo, hi), ("EE", lo, hi), ("HH", lo, hi), 1.0, OP.min, OP.max)
+        for (lo, hi, st, a) in ((2048, 3072, 128, 8), (0, 2048, 256, 0)):
+            ts(w("ND", a, a + 8), ("CO", lo, hi), 0.25, OP.is_gt, ia=T.CO[:, lo + st - 1:hi:st])
+        tt(w("XW"), w("ND"), w("GSD"), OP.mult)
+        tt(w("WN2"), w("ND"), w("GO"), OP.mult)
+        tt(w("YW"), w("XW"), w("DTT"), OP.add)
+        ts(w("WN2"), w("WN2"), 128.0, OP.mult)
+        cp(wl, w("YW"))
+        tt(("INC", 0, 16), w("WN"), w("WN2"), OP.add)
+        spread("INC", "KRP")
+        scatter(("TAB", 0, WT), wl, ("ZL%d" % t, 0, 256))
+
+    def out_table(h):
+        dma("y", "out%d" % h, [("TAB", 2048 * h, 2048 * h + 2048)], [("yt", 2048 * h, 2048 * h + 2048)],
+            lambda e: e.dma_start(T.yt[:, 2048 * h:2048 * h + 2048], T.TAB[:, 2048 * h:2048 * h + 2048]))
+
+    def step_state(t):
+        wl, fl = ("WL%d" % t, 0, 16), ("FL%d" % t, 0, 16)
+        st, st0 = ("ST", 0, 1024 + WT), ("ST", 0, 1024)
+        if t:
+            tt(("WA", 0, 256), ("OCC", 0, WT), ("MI", 0, 256), OP.mult, ia=T.OCC[:, :].indirect(A(wl)), more=[wl])
+        if t == 3:
+            out_table(0)
+            occ(t)
+            dma("y", "out2", [("OCC", 0, 4096)], [("YS", 0, 256)], lambda e: e.dma_start(T.YS[:, :], T.OCC[0:128:16, 0:4096]))
+            out_table(1)
+        if t:
+            scan(("WB", 0, 256), ("M0", 0, 256), ("WA", 0, 256), 0.0, OP.mult, OP.add)
+            cp(("BL", 0, 16), ("WB", 0, 256), ia=T.WB[:, 15:256:16])
+            gather(("BN", 0, 256), st, ("BL", 0, 16), e="s", bias=-127.0)
+        tt(("STN", 0, 256), ("KRP", 0, 256), ("DL", 0, 256), OP.add)
+        scatter(st0, fl, ("STN", 0, 256))
+        if t:
+            scatter(st, ("BL", 0, 16), ("BN", 0, 256))
+
+    def occ(t):
+        scatter(("OCC", 0, WT), ("WL%d" % t, 0, 16), ("LW%d" % t, BASE, BASE + 256), more=[("WA", 0, 256)])
+
+    def step_select(t):
+        U, lo = 256 * t, 256 - 64 * t
+        new, n = lo + U, 16 * t
+        lw, fl, zl = "LW%d" % t, ("FL%d" % t, 0, 12), ("ZL%d" % t, 0, 192)
+        if t == 1:
+            ts(("FB", 0, 1), ("DL", 0, 1), 0.0, OP.mult)
+        ts(("FB", U + 1, U + 2), ("DL", 0, 1), 0.0, OP.mult, -1.0, OP.add)
+        ts(("FB", 1, U + 1), ("ST", lo, lo + U), 128.0, OP.is_lt, -1.0, OP.mult)
+        scan(("VB", 0, U + 1), ("FB", 1, U + 2), ("FB", 0, U + 1), 2000.0, OP.add, OP.add)
+        scan(("VW", 0, U), ("M0H", 0, U), ("VB", 0, U), 0.0, OP.mult, OP.max)
+        ts(("VC", 0, 1), ("VB", U, U + 1), float(2 * new - 1999), OP.add)
+
+        def I(k):
+            return ("II", 48 * k, 48 * k + n)
+        ts(I(0), ("VW", 0, U), -1.0, OP.mult, 2000.0, OP.add, ia=T.VW[:, 15:U:16])
+        ts((lw, BASE, BASE + 192), ("CJ2", 0, 192), T.VC[:, 0:1], OP.add, 0.5, OP.mult, more=[("VC", 0, 1)])
+        ts(I(1), I(0), 1, OP.bitwise_and)
+        ts(I(2), I(0), 1, OP.arith_shift_right)
+        tt(I(3), I(1), ("DW", 0, n), OP.mult)
+        tt(I(4), ("C1", 0, n), I(2), OP.subtract)
+        tt(I(5), I(4), I(3), OP.subtract)
+        cp(("LU", 0, n), I(5))
+        scatter((lw, 0, BASE + 1024), ("LU", 0, n), ("IOT", lo, lo + U))
+        scan(("WS", 0, 192), ("M0", 0, 192), (lw, BASE, BASE + 192), 0.0, OP.mult, OP.max)
+        cp(fl, ("WS", 0, 192), ia=T.WS[:, 15:192:16])
+        occ(t - 1)
+        gather(("DL", 0, 192), ("ST", 0, 1024), fl, e="s")
+        gather(zl, ("ZFT", 0, 1024), fl, e="s")
+        for (tab, a, b, o) in (("EHT", "EI", "EM", "EHO"), ("EFT", "FI", "FM", "EFO")):
+            tt((a, 0, 192), (tab, 0, 1024), ("DL", 0, 192), OP.add, ia=T[tab][:, :].indirect(A(fl)), more=[fl])
+            ts((b, 0, 192), (a, 0, 192), 4095, OP.bitwise_and)
+            cp((o, 0, 192), (b, 0, 192))
+        ts(("EHH%d" % t, 0, 192), ("EM", 0, 192), -2048.0, OP.add)
+
+    memset(("WA", 0, 256), 0.0)
+    expand(0)
+    fresh_home(0)
+    for t in range(4):
+        if t:
+            step_select(t)
+            if t < 3:
+                put("RZ%d" % (t + 1), 0, 256, "ZL%d" % t, asker(t + 1), "rz%d" % (t + 1), "loc%d" % (4 + t))
+        step_main(t)
+        step_claims(t)
+        u = t + 1
+        if t < 3:
+            dst = cores[asker(u)]
+            rid, pid, _se = topo.addr(dst)
+            send("loc%d" % (8 + t), len(topo.engines(core, dst)), [("WL%d" % t, 0, 16)],
+                 lambda e: e.remote_dma(T["RL%d" % u][:, :], T["WL%d" % t][:, :], T.sem["rl%d" % u], T.sem["loc%d" % (8 + t)], pid, rid, topo.mask(core, dst)))
+        if t < 2:
+            put("FT%d" % (t + 2), 0, 4096, "TAB", asker(t + 2), "sn%d" % (t + 2), "loc%d" % (12 + t))
+        if t == 0:
+            iota(("ST", 1024, 1024 + WT), [[0, WT]], 0)
+        step_state(t)
+        if t < 3:
+            fresh_home(u)
+            scatter(("FT%d" % u, 0, WT), ("RL%d" % u, 0, 16), ("RZ%d" % u, 0, 256))
+            fresh_foreign(u)
+    ts(("GB0", 0, 1024), ("ST", 0, 1024), 128.0, OP.is_ge, -128.0, OP.mult)
+    for h in range(2):
+        d, x = ("D%d" % h, 0, 512), (512 * h, 512 * h + 512)
+        mm(d, ("PID", 0, 128), ("ST", x[0], x[1]), True, False)
+        mm(d, ("PID", 0, 128), ("GB0", x[0], x[1]), False, True)
+        cp(("YD", x[0], x[1]), d, e="s")
+    ys, y1, y2 = ("YS", 0, 256), ("Y1", 0, 256), ("Y2", 0, 256)
+    ts(y1, ys, 192.0, OP.is_lt, 1024.0, OP.mult)
+    ts(y2, ys, 1024.0, OP.is_lt)
+    tt(y1, ys, y1, OP.add)
+    ts(y1, y1, -191.0, OP.add)
+    tt(y1, y1, y2, OP.mult)
+    ts(y1, y1, -1.0, OP.add)
+    dma("y", "out5", [y1], [("yo", 0, 4096)], lambda e: e.dma_start(T.yo[:, :], T.Y1[:, :]))
+    dma("s", "out3", [("YD", 192, 1024)], [("yd", 0, 832)], lambda e: e.dma_start(T.yd[:, 0:832], T.YD[0:128:16, 192:1024]))
+    dma("s", "out4", [("YD", 0, 192)], [("yd", 832, 1024)], lambda e: e.dma_start(T.yd[:, 832:1024], T.YD[0:128:16, 0:192]))
+    finish()

@@ -1,37 +1,37 @@
 from concourse.mybir import AluOpType, ActivationFunctionType
+from concourse.bass import DstId, RemoteDMATransfer
 
 OP = AluOpType
 AF = ActivationFunctionType
-NB2 = 4
-NBV = 12 - NB2
-ZS = 8
-W1 = 131072.0
-BASE = 640
-WT = 4096 + 1024
+W1 = 65536.0
+BIG = 8192.0
+OFF = 2048.0 + BIG
+WT = 4096 + 256
 SB = "sbuf"
 F32, B16, F16, I32, U16 = "float32", "bfloat16", "float16", "int32", "uint16"
 SCRATCH = {}
 for _names, _w, _d in (
-        ("TAB", WT, B16), ("OCC", WT, F32), ("ST", 1024 + WT, B16), ("EHT EFT", 1024, I32), ("ZFT", 1024, B16),
-        ("IOT YD", 1024, F32), ("JM", 768, F32), ("QX", 144, F32), ("Q4", 128, F32), ("TMPF", 1024, F32), ("KCF JR M0 MI SCM SH SF WA WB YS Y1 Y2", 256, F32),
-        ("PJ", 4, I32), ("PC", 8, F32), ("CI", 96, I32), ("CLA", 16, U16), ("CLB", 12, U16), ("DW C1", 48, I32), ("CJ2 WS", 192, F32),
-        ("XV XS", 144, B16), ("X1", 144, F16), ("BO", 128, F16), ("BO16 BOB NID PID ZT1 ZT2", 128, B16), ("RO", 2048, B16), ("EX", 1024, B16),
-        ("KC JRI", 256, B16), ("M0H", 768, F16), ("HH EE CO", 3072, B16), ("HF", 8, F32), ("SEH SEF", 192, U16), ("DL STN BN", 256, B16),
-        ("EHO EFO", 256, U16), ("EI EM FI FM", 192, I32), ("ZX", 256 * NBV, B16), ("GB0 GB1", 1024, B16),
-        ("IW", 64, I32), ("WF", 256, F32), ("KW NG INC", 16, B16), ("OH MSK SR", 256, F16), ("BL", 16, U16),
-        ("FB VB", 784, F16), ("VW", 768, F16), ("VC", 8, F32), ("II", 288, I32), ("LU", 48, U16),
-        ("ZL0 ZL1 ZL2 ZL3 RZ1 RZ2 RZ3", 256, B16), ("EHH0 EHH1 EHH2 EHH3", 256, F16), ("LW0 LW1 LW2 LW3", BASE + 1024, F32),
-        ("FL0 FL1 FL2 FL3 WL0 WL1 WL2 WL3 RL1 RL2 RL3", 16, U16), ("FT0", 4096, B16), ("FT1 FT2 FT3", WT, B16)):
+        ("TAB FT1 FT2 FT3", WT, B16), ("OCC", WT, F32), ("ST ZFT YA", 1024, B16), ("EHT EFT", 1024, I32), ("IOT FN", 1024, F32),
+        ("PJ", 4, I32), ("PC", 16, F32), ("CI", 48, F32), ("QX", 160, F32), ("Q4 T1 T2", 128, F32), ("JM RS SCM SH SF CS FR1 FR2 FR3", 256, F32),
+        ("JR MB WS", 192, F32), ("DW", 48, F32), ("HF", 8, F32), ("EX EXI GB0 GB1 DB", 512, B16), ("KC CM STN QZ PM", 256, B16),
+        ("XV X0 XD", 144, B16), ("XP XO", 144, F16), ("BE BD", 160, F16), ("BO BO8 TRI NID PID ZT ZTF ZTQ", 128, B16), ("BO0 PIH BOH", 128, F16),
+        ("RO", 2048, F16), ("ZX", 2048, B16), ("ZXQ", 2560, B16), ("SR OG", 256, F16), ("AB FB VB", 768, F16), ("LW", 1536, F32),
+        ("EHO EFO QE", 256, U16), ("SEH SEF", 192, U16), ("EI EM FI FM", 192, I32), ("IW", 64, I32), ("WF", 256, F32), ("WH", 32, F16),
+        ("RP SP", 16, F32), ("LF", 48, F32), ("LU", 48, U16), ("SL BL TL FL", 16, U16), ("YD", 64, F32),
+        ("ZL1 ZL2 ZL3 RZ1 RZ2 RZ3", 256, B16), ("WL0 WL1 WL2 WL3 RL1 RL2 RL3", 16, U16)):
     for _n in _names.split():
         SCRATCH[_n] = (SB, [128, _w], _d)
-for _n, _w in (("CH", NBV), ("CF", NBV), ("S1H", 4), ("S1F", 4), ("S2H", 4), ("S2F", 4)):
-    SCRATCH[_n] = (SB, [128, _w, 256], B16)
-for _n in ("KH", "KF", "D0", "D1", "SRP", "KRP", "SWP"):
+for _n in ("CH", "CF", "EE"):
+    SCRATCH[_n] = (SB, [128, 16, 256], B16)
+for _n in ("EP", "TR"):
+    SCRATCH[_n] = (SB, [128, 8, 32], F16)
+for _n in ("KH", "KF", "D0", "D1", "ZP", "PA", "PB", "CN"):
     SCRATCH[_n] = ("psum", [128, 512], F32)
-SCRATCH["ZTP"] = ("psum", [128, 1024], B16)
-SEMAPHORES = ["cv", "cs", "cp", "cg"] + ["ld%d" % _i for _i in range(12)] + ["sn%d" % _i for _i in range(4)] + ["loc%d" % _i for _i in range(16)]
-SEMAPHORES += ["rz%d" % _i for _i in range(4)] + ["rl%d" % _i for _i in range(4)] + ["out%d" % _i for _i in range(8)]
-WIDX = {n: 16 * i for i, n in enumerate("SW NSW SD DTT WM GO NO WN GSD ND XW YW WN2 DT0 DT2".split())}
+SEMAPHORES = ["cv", "cs", "cp", "cg", "qu", "rp", "hl"] + ["ld%d" % _i for _i in range(12)] + ["sn%d" % _i for _i in range(4)] + ["loc%d" % _i for _i in range(12)]
+SEMAPHORES += ["rz%d" % _i for _i in range(4)] + ["rl%d" % _i for _i in range(4)] + ["out%d" % _i for _i in range(4)]
+SEMAPHORES += ["h%d%d" % (_t, _q) for _t in range(1, 4) for _q in range(4)]
+WIDX = {n: 16 * i for i, n in enumerate("SW WM NG WN WIN T1 T2 OC X0 X1 X Y0 Y FW TF".split())}
+PCOL = {n: i for i, n in enumerate("I P G P32 M0 M1 EV OD WP WD N1 F0 F1 LO HI".split())}
 
 
 def make(g, T):
@@ -49,7 +49,7 @@ def make(g, T):
     def psum(b):
         return b in SCRATCH and SCRATCH[b][0] == "psum"
 
-    def needs(owner, reads, writes):
+    def needs(owner, reads, writes, part=None):
         out = []
         for mode, lst in (("r", reads), ("w", writes)):
             for (b, lo, hi) in lst:
@@ -59,7 +59,9 @@ def make(g, T):
                         continue
                     if mode == "r" and m2 == "r" and not ps:
                         continue
-                    if tok[2] == owner and not (mode == "r" and m2 == "w"):
+                    if tok[2] == owner and ((mode == "r" and m2 == "r") or (mode == "w" and owner == "p")):
+                        continue
+                    if part and mode == m2 == "w" and tok[4:] == (part,):
                         continue
                     out.append(tok)
         return out
@@ -75,7 +77,7 @@ def make(g, T):
         for (b, lo, hi) in writes:
             lst = acc.setdefault(b, [])
             if not psum(b):
-                lst[:] = [x for x in lst if not (lo <= x[0] and x[1] <= hi)]
+                lst[:] = [x for x in lst if not (lo <= x[0] and x[1] <= hi) or (x[3][2] != tok[2] and tok[4:] != (None,) and x[3][4:] == tok[4:] != ())]
             else:
                 lst[:] = [x for x in lst if not (x[3][2] == tok[2] and x[2] == "w" and lo <= x[0] and x[1] <= hi)]
             lst.append((lo, hi, "w", tok))
@@ -84,15 +86,17 @@ def make(g, T):
             lst[:] = [x for x in lst if not (x[2] == "r" and x[3][0] == tok[0] and lo <= x[0] and x[1] <= hi)]
             lst.append((lo, hi, "r", tok))
 
-    def op(e, reads, writes, fn):
-        waits(e, needs(e, reads, writes))
+    def op(e, reads, writes, fn, part=None):
+        waits(e, needs(e, reads, writes, part))
         cnt[e] += 1
         fn(eng[e]).then_inc(T.sem[sem[e]], 1)
         total[sem[e]] = cnt[e]
-        note((sem[e], cnt[e], e, dict(know[e])), reads, writes)
+        note((sem[e], cnt[e], e, dict(know[e]), part), reads, writes)
 
-    def dma(e, s, reads, writes, fn):
+    def dma(e, s, reads, writes, fn, after=None):
         waits(e, needs("dma" + s, reads, writes))
+        if after:
+            eng[e].wait_ge(T.sem[after], total[after])
         fn(eng[e]).then_inc(T.sem[s], 16)
         total[s] = total.get(s, 0) + 16
         note((s, total[s], "dma" + s, dict(know[e])), reads, writes)
@@ -101,70 +105,111 @@ def make(g, T):
         waits("g", needs("rem" + s, reads, []))
         fn(g)
         total[s] = total.get(s, 0) + n
-        note((s, total[s], "rem" + s, dict(know["g"])), reads, [])
+        for r in reads:
+            acc[r[0]] = [x for x in acc.get(r[0], []) if x[3][0] != s]
+        lo = {}
+        for r in sent.setdefault(s, []) + list(reads):
+            lo[r] = 1
+        sent[s] = list(lo)
+        note((s, total[s], "rem" + s, dict(know["g"])), sent[s], [])
 
     def land(s, n, b, lo, hi):
-        total[s] = total.get(s, 0) + n
-        acc.setdefault(b, []).append((lo, hi, "w", (s, total[s], "net" + s, {})))
+        total[s] = n
+        acc.setdefault(b, []).append((lo, hi, "w", (s, n, "net" + s, {})))
 
     def finish():
         for s, v in total.items():
             if know["g"].get(s, 0) < v:
                 g.wait_ge(T.sem[s], v)
+    sent = {}
     return op, dma, send, land, finish
+
+
+def bits(engines):
+    return sum(1 << e for e in engines)
+
+
+def helpers(topo, cores, rank):
+    me = cores[rank]
+    free = [c for c in topo.cores_of(me) if c != me and all(topo.may_write(c, o) for o in cores if o != me)]
+    return [[c for c in free if topo.die(c) != topo.die(me)][0], [c for c in free if topo.die(c) == topo.die(me)][0]]
+
+
+def hand_on(g, core, T, topo):
+    for rank in range(4):
+        two = helpers(topo, T.cores, rank)
+        if core not in two:
+            continue
+        n = 0
+        for t in range(1, 4):
+            dst = T.cores[(rank - 1 - t % 3) % 4]
+            rid, pid, _se = topo.addr(dst)
+            for q in range(two.index(core), 4, 2):
+                x = T["FT%d" % t][:, 1024 * q:1024 * q + 1024]
+                g.wait_ge(T.sem["h%d%d" % (t, q)], len(topo.engines(T.cores[rank], core)))
+                g.remote_dma(x, x, T.sem["sn%d" % t], T.sem["hl"], pid, rid, topo.mask(core, dst))
+                n += len(topo.engines(core, dst))
+        g.wait_ge(T.sem["hl"], n)
 
 
 def rank_program(g, core, T, topo):
     rank = T.rank_of(core)
     if rank is None:
-        return
+        return hand_on(g, core, T, topo)
     op, dma, send, land, finish = make(g, T)
     cores = T.cores
-
-    def put(dst_buf, lo, hi, src_buf, peer, rsem, lsem):
-        dst = cores[peer]
-        rid, pid, _se = topo.addr(dst)
-        send(lsem, len(topo.engines(core, dst)), [(src_buf, lo, hi)],
-             lambda e: e.remote_dma(T[dst_buf][:, lo:hi], T[src_buf][:, lo:hi], T.sem[rsem], T.sem[lsem], pid, rid, topo.mask(core, dst)))
-
-    def asker(t):
-        return (rank - 1 - t % 3) % 4
-
-    def nin(t):
-        return len(topo.engines(cores[(rank + 1 + t % 3) % 4], core))
+    mine = helpers(topo, cores, rank)
 
     def A(x):
         return T[x[0]][:, x[1]:x[2]]
 
+    def put(o, i, dst, rsem, lsem):
+        rid, pid, _se = topo.addr(dst)
+        send(lsem, len(topo.engines(core, dst)), [i], lambda e: e.remote_dma(A(o), A(i), T.sem[rsem], T.sem[lsem], pid, rid, topo.mask(core, dst)))
+
+    def asker(t):
+        return cores[(rank - 1 - t % 3) % 4]
+
+    def seen(t):
+        return (rank + 1 + t % 3) % 4
+
+    def snapshot(t):
+        for q in range(4):
+            put(("FT%d" % t, 1024 * q, 1024 * q + 1024), ("TAB", 1024 * q, 1024 * q + 1024), mine[q % 2], "h%d%d" % (t, q), "loc%d" % t)
+
     def w(n, a=0, b=16):
         return ("WF", WIDX[n] + a, WIDX[n] + b)
 
-    def ts(o, i, s1, o0, s2=None, o1=None, ia=None, more=()):
+    pc = ("PC", 0, 16)
+
+    def P(n):
+        return T.PC[:, PCOL[n]:PCOL[n] + 1]
+
+    def ts(o, i, s1, o0, s2=None, o1=None, ia=None, oa=None, more=(), part=None):
         rd = [i] + list(more)
-        src = A(i) if ia is None else ia
+        src, out = A(i) if ia is None else ia, A(o) if oa is None else oa
         if o1 is None:
-            op("v", rd, [o], lambda e: e.tensor_scalar(A(o), src, s1, None, o0))
+            op("v", rd, [o], lambda e: e.tensor_scalar(out, src, s1, None, o0), part)
         else:
-            op("v", rd, [o], lambda e: e.tensor_scalar(A(o), src, s1, s2, o0, o1))
+            op("v", rd, [o], lambda e: e.tensor_scalar(out, src, s1, s2, o0, o1), part)
 
     def tt(o, a, b, f, ia=None, ib=None, more=(), oa=None):
         op("v", [a, b] + list(more), [o], lambda e: e.tensor_tensor(A(o) if oa is None else oa, A(a) if ia is None else ia, A(b) if ib is None else ib, f))
 
-    def cp(o, i, ia=None, oa=None, more=(), e="v"):
+    def cp(o, i, ia=None, oa=None, more=(), e="v", bias=None, part=None):
         src, out = A(i) if ia is None else ia, A(o) if oa is None else oa
         if e == "v":
-            op("v", [i] + list(more), [o], lambda e: e.tensor_copy(out, src))
+            op("v", [i] + list(more), [o], lambda e: e.tensor_copy(out, src), part)
+        elif bias is None:
+            op("s", [i] + list(more), [o], lambda e: e.activation(out, src, AF.Copy), part)
         else:
-            op("s", [i] + list(more), [o], lambda e: e.activation(out, src, AF.Copy))
+            op("s", [i] + list(more), [o], lambda e: e.activation(out, src, AF.Identity, bias=bias))
 
     def gather(o, win, lst, e="v", bias=None):
-        if bias is None:
-            cp(o, win, ia=A(win).indirect(A(lst)), more=[lst], e=e)
-        else:
-            op("s", [win, lst], [o], lambda e: e.activation(A(o), A(win).indirect(A(lst)), AF.Identity, bias=bias))
+        cp(o, win, ia=A(win).indirect(A(lst)), more=[lst], e=e, bias=bias)
 
-    def scatter(win, lst, i, more=()):
-        cp(win, i, oa=A(win).indirect(A(lst)), more=[lst, win] + list(more))
+    def scatter(win, lst, i):
+        cp(win, i, oa=A(win).indirect(A(lst)), more=[lst, win])
 
     def scan(o, d0, d1, init, o0, o1):
         op("v", [d0, d1], [o], lambda e: e.tensor_tensor_scan(A(o), A(d0), A(d1), init, o0, o1))
@@ -178,355 +223,444 @@ def rank_program(g, core, T, topo):
     def memset(o, v):
         op("v", [], [o], lambda e: e.memset(A(o), v))
 
-    def load(n, dst, lo, hi, src, a, b):
-        dma("y", "ld%d" % n, [], [(dst, lo, hi)], lambda e: e.dma_start(T[dst][:, lo:hi], T[src][:, a:b]))
-    load(0, "EHT", 192, 448, "eh", 0, 256)
+    def ends(b, n=256):
+        return T[b][:, 15:n:16]
+
+    def load(n, dst, lo, hi, src, a, b, after=None):
+        dma("y", "ld%d" % n, [], [(dst, lo, hi)], lambda e: e.dma_start(T[dst][:, lo:hi], T[src][:, a:b]), after)
+    load(0, "EFT", 192, 448, "ef", 0, 256)
     load(1, "ZFT", 192, 448, "zf", 0, 256)
     load(2, "TAB", 0, 2048, "tab", 0, 2048)
+    load(4, "EHT", 192, 448, "eh", 0, 256)
     load(3, "TAB", 2048, 4096, "tab", 2048, 4096)
-    load(4, "EFT", 192, 448, "ef", 0, 256)
-    for k, (dst, src) in enumerate((("EHT", "eh"), ("ZFT", "zf"), ("EFT", "ef"))):
-        load(5 + 2 * k, dst, 0, 192, src, 832, 1024)
-        load(6 + 2 * k, dst, 448, 1024, src, 256, 832)
-    for t in range(4):
-        land("sn%d" % t, nin(t) * (2 if t == 0 else 1), "FT%d" % t, 0, 4096)
+    far = len(topo.engines(asker(0), core))
+    land("qu", far, "QE", 0, 256)
+    land("qu", far, "QZ", 0, 256)
+    land("rp", len(topo.engines(cores[seen(0)], core)), "RP", 0, 16)
     for t in range(1, 4):
-        land("rz%d" % t, nin(t), "RZ%d" % t, 0, 256)
-        land("rl%d" % t, nin(t), "RL%d" % t, 0, 16)
+        n = len(topo.engines(cores[seen(t)], core))
+        land("sn%d" % t, sum(2 * len(topo.engines(h, core)) for h in helpers(topo, cores, seen(t))), "FT%d" % t, 0, 4096)
+        land("rz%d" % t, n, "RZ%d" % t, 0, 256)
+        land("rl%d" % t, n, "RL%d" % t, 0, 16)
 
-    pc = ("PC", 0, 4)
+    z0 = ("ZFT", 192, 448)
     iota(("PJ", 0, 1), [[0, 1]], 0, 1)
-    iota(("CI", 0, 16), [[-16, 16]], 255)
-    iota(("CI", 32, 44), [[-16, 12]], 191)
-    iota(("QX", 0, 144), [[1, 144]], -15)
+    iota(("QX", 0, 160), [[1, 160]], -16)
+    iota(("EXI", 0, 512), [[1, 32], [0, 16]], 0)
     iota(("Q4", 0, 128), [[16, 8], [0, 16]], 0)
-    iota(("KCF", 0, 256), [[0, 16], [-8192, 16]], 122880)
-    ts(("PJ", 2, 3), ("PJ", 0, 1), 15, OP.bitwise_and)
-    ts(("PJ", 3, 4), ("PJ", 0, 1), 4, OP.arith_shift_right)
-    cp(("PC", 0, 1), ("PJ", 2, 3))
-    cp(("PC", 1, 2), ("PJ", 0, 1))
-    ts(("PC", 2, 3), ("PJ", 3, 4), 16.0, OP.mult)
-    ts(("PC", 3, 4), ("PJ", 2, 3), -1.0, OP.mult, 15.0, OP.add)
-    PI_, PP, PG, P15 = T.PC[:, 0:1], T.PC[:, 1:2], T.PC[:, 2:3], T.PC[:, 3:4]
-    ts(("CLA", 0, 16), ("CI", 0, 16), PI_, OP.subtract, more=[pc])
-    ts(("CLB", 0, 12), ("CI", 32, 44), PI_, OP.subtract, more=[pc])
-    memset(("HF", 0, 1), 0.5)
-    qx = ("QX", 15, 143)
-    ts(("NID", 0, 128), qx, PP, OP.is_equal, -1.0, OP.mult, more=[pc])
-    ts(("PID", 0, 128), qx, PP, OP.is_equal, more=[pc])
-    for n, f in (("XV", W1), ("XS", W1 / 2)):
-        ts((n, 0, 144), ("QX", 0, 144), PG, OP.is_equal, f, OP.mult, more=[pc])
-    ts(("BO16", 0, 128), ("Q4", 0, 128), PG, OP.is_equal, 0.0625, OP.mult, more=[pc])
-    cp(("KC", 0, 16 * NBV), ("KCF", 0, 16 * NBV))
-    ts(("KC", 16 * NBV, 256), ("KCF", 16 * NBV, 256), 8 * W1, OP.add)
-    gather(("ZL0", 0, 256), ("ZFT", 192, 448), ("CLA", 0, 16), e="s")
-    gather(("EHO", 0, 256), ("EHT", 192, 448), ("CLA", 0, 16))
-    iota(("TMPF", 0, 1024), [[1, 64], [0, 16]], 0)
-    ts(("EX", 0, 1024), ("TMPF", 0, 1024), PP, OP.is_equal, more=[pc])
-    iota(("LW0", BASE, BASE + 256), [[-1, 256]], 447)
-    iota(("JM", 0, 768), [[0, 48], [1, 16]], 0)
-    iota(("JR", 0, 256), [[1, 256]], 0)
-    for h in range(2):
-        put("FT0", 2048 * h, 2048 * h + 2048, "TAB", asker(0), "sn0", "loc0")
-    put("FT1", 0, 4096, "TAB", asker(1), "sn1", "loc1")
-    put("RZ1", 0, 256, "ZL0", asker(1), "rz1", "loc4")
-    iota(("CI", 48, 96), [[16, 48]], 65)
-    iota(("OCC", 0, WT), [[1, WT]], 1024)
+    iota(("KC", 0, 256), [[0, 16], [-256, 16]], 3968)
+    iota(("JM", 0, 256), [[0, 16], [1, 16]], 0)
+    memset(("HF", 0, 1), 200.0)
+    memset(("ST", 0, 1024), 0.0)
+    for k in range(4):
+        cp(("OCC", 1024 * k, 1024 * k + 1024), ("ST", 0, 1024), e="s", bias=-1.0)
+
+    def col(n, i, s1, o0, s2=None, o1=None):
+        ts(("PC", PCOL[n], PCOL[n] + 1), i, s1, o0, s2, o1)
+
+    def c(n):
+        return ("PC", PCOL[n], PCOL[n] + 1)
+    ts(("PJ", 1, 2), ("PJ", 0, 1), 15, OP.bitwise_and)
+    ts(("PJ", 2, 3), ("PJ", 0, 1), 31, OP.bitwise_and)
+    cp(c("P"), ("PJ", 0, 1))
+    cp(c("I"), ("PJ", 1, 2))
+    cp(c("P32"), ("PJ", 2, 3))
+    tt(c("G"), c("P"), c("I"), OP.subtract)
+    col("M0", c("I"), 0.0, OP.is_equal)
+    col("M1", c("I"), 1.0, OP.is_equal)
+    col("EV", c("P32"), 16.0, OP.is_lt)
+    col("OD", c("P32"), 16.0, OP.is_ge)
+    cp(("EFO", 0, 256), ("EFT", 192, 448))
+    dst = cores[seen(0)]
+    rid, pid, _se = topo.addr(dst)
+    en = topo.engines(core, dst)
+    send("loc0", len(en), [("EFO", 0, 256), z0], lambda e: e.remote_dma_fused(
+        [RemoteDMATransfer(dst_ids=[DstId(rid=rid, pnc=pid)], dma_engine_mask=bits(m), remote_sem=T.sem["qu"], src=A(i), dst=A(o))
+         for (m, i, o) in ((en[:len(en) // 2], ("EFO", 0, 256), ("QE", 0, 256)), (en[len(en) // 2:], z0, ("QZ", 0, 256)))], local_sem=T.sem["loc0"]))
+    qx = ("QX", 16, 144)
+    ts(("NID", 0, 128), qx, P("P"), OP.is_equal, -1.0, OP.mult, more=[pc])
+    ts(("PID", 0, 128), qx, P("P"), OP.is_equal, more=[pc])
+    ts(("EX", 0, 512), ("EXI", 0, 512), P("P32"), OP.is_equal, more=[pc])
+    ts(("XV", 0, 144), ("QX", 0, 144), P("G"), OP.is_equal, W1, OP.mult, more=[pc])
+    ts(("BO", 0, 128), ("Q4", 0, 128), P("G"), OP.is_equal, more=[pc])
+    cp(("EHO", 0, 256), ("EHT", 192, 448))
+    iota(("CI", 0, 48), [[16, 48]], 0)
+    iota(("JR", 0, 192), [[1, 192]], 0)
     iota(("IOT", 0, 1024), [[1, 1024]], 0)
-    iota(("CJ2", 0, 192), [[-2, 192]], 382)
-    for t in range(1, 4):
-        iota(("LW%d" % t, BASE + 192, BASE + 256), [[-1, 64]], 255 - 64 * t)
 
     def constants_1():
-        for (o, i, f) in ((("M0", 0, 256), ("JM", 0, 256), OP.not_equal), (("MI", 0, 256), ("JM", 0, 256), OP.is_equal)):
-            ts(o, i, PI_, f, more=[pc])
+        for n, f in (("BE", "EV"), ("BD", "OD")):
+            ts((n, 0, 160), ("QX", 0, 160), P("P"), OP.is_equal, P(f), OP.mult, more=[pc])
         ts(("SCM", 0, 256), ("JM", 0, 256), 0.5, OP.is_gt)
-        ts(("BOB", 0, 128), ("Q4", 0, 128), PG, OP.is_equal, more=[pc])
-        for c in range(16):
-            ts(("RO", 128 * c, 128 * c + 128), ("BOB", 0, 128), T.MI[:, c:c + 1], OP.mult, more=[("MI", 0, 256)])
-        ts(("JRI", 0, 256), ("JR", 0, 256), PI_, OP.subtract, more=[pc])
-        ts(("BO", 0, 128), ("Q4", 0, 128), PG, OP.is_equal, more=[pc])
-        ts(("X1", 0, 144), ("QX", 0, 144), PG, OP.is_equal, more=[pc])
-        ts(("EHH0", 0, 256), ("EHO", 0, 256), -2048.0, OP.add)
-
-    def constants_s():
-        for m in range(16):
-            lo, n, a = (256 * m, 256, 0) if m < 8 else (2048 + 128 * (m - 8), 128, 128)
-            op("s", [("JRI", a, 256)], [("HH", lo, lo + n)], lambda e: e.activation(T.HH[:, lo:lo + n], T.JRI[:, a:a + n], AF.Sign, bias=16.0 * m + 0.5, scale=-1.0))
+        ts(("BOH", 0, 128), ("Q4", 0, 128), P("G"), OP.is_equal, more=[pc])
+        ts(("T2", 0, 128), ("JM", 0, 128), P("I"), OP.is_equal, more=[pc])
+        ts(("T1", 0, 128), ("JM", 0, 128), P("I"), OP.is_gt, more=[pc])
+        for k in range(16):
+            ts(("RO", 128 * k, 128 * k + 128), ("BOH", 0, 128), T.T2[:, k:k + 1], OP.mult, more=[("T2", 0, 128)])
+        ts(("PIH", 0, 128), qx, P("P"), OP.is_equal, more=[pc])
+        ts(("BO8", 0, 128), ("BO", 0, 128), BIG, OP.mult)
+        tt(("T1", 0, 128), ("T1", 0, 128), ("T2", 0, 128), OP.subtract)
+        ts(("CM", 0, 256), ("JM", 0, 256), P("I"), OP.not_equal, 131072.0, OP.mult, more=[pc])
+        tt(("TRI", 0, 128), ("T1", 0, 128), ("BO8", 0, 128), OP.mult)
+        memset(("RS", 0, 256), -20000.0)
+        ts(("RS", 0, 256), ("CI", 0, 16), P("I"), OP.add, 4096.0 - OFF, OP.add, oa=T.RS[:, 0:256:16], more=[pc, ("RS", 0, 256)])
 
     def constants_2():
-        memset(("EE", 0, 3072), 1.0)
-        memset(("ST", 0, 1024), 0.0)
-        memset(("DL", 0, 256), 0.0)
-        ts(("DW", 0, 48), ("CI", 48, 96), PI_, OP.add, more=[pc])
-        ts(("C1", 0, 48), ("DW", 0, 48), float(BASE + 191), OP.add)
-        ts(w("DT0"), ("DW", 0, 16), float(4096 - 65), OP.add)
-        ts(("FL0", 0, 16), ("CLA", 0, 16), 192.0, OP.add)
-        for (o, tab) in (("SEH", "EHT"), ("SEF", "EFT")):
-            gather((o, 0, 192), (tab, 0, 192), ("CLB", 0, 12))
-        for t in range(1, 4):
-            x, l = 64 * (t - 1), ("CLB", 4 * t - 4, 4 * t)
-            ts(("EHH%d" % t, 192, 256), ("SEH", x, x + 64), -2048.0, OP.add)
-            gather(("ZL%d" % t, 192, 256), ("ZFT", 0, 192), l, e="s")
-            cp(("FL%d" % t, 12, 16), l)
-        ts(("M0H", 0, 768), ("JM", 0, 768), PI_, OP.not_equal, more=[pc])
+        col("WP", c("M1"), -2048.0, OP.mult, P("M0"), OP.add)
+        col("WD", c("M1"), -128.0, OP.mult, P("M0"), OP.add)
+        col("N1", c("I"), 1.0, OP.not_equal)
+        col("F0", c("M0"), 832.0, OP.mult)
+        col("F1", c("M0"), -192.0, OP.mult)
+        col("LO", c("M1"), 127.0, OP.mult)
+        col("HI", c("M1"), -128.0, OP.mult, 256.0, OP.add)
+        for n, f in (("X0", "M0"), ("XO", "M1"), ("XP", "WP"), ("XD", "WD")):
+            ts((n, 0, 144), ("QX", 0, 144), P("G"), OP.is_equal, P(f), OP.mult, more=[pc])
+        ts(("BO0", 0, 128), ("Q4", 0, 128), P("G"), OP.is_equal, P("M0"), OP.mult, more=[pc])
+        ts(("MB", 0, 192), ("JM", 0, 192), P("I"), OP.is_equal, 60000.0, OP.mult, more=[pc])
+        ts(("AB", 0, 768), ("ST", 0, 768), P("N1"), OP.add, more=[pc])
+        ts(("DW", 0, 48), ("CI", 0, 48), P("I"), OP.add, 768.0 - 2047.0, OP.add, more=[pc])
+        memset(("DB", 0, 64), 0.0)
 
-    gbn = [0]
+    def constants_3():
+        ts(("FN", 0, 192), ("IOT", 0, 192), P("F0"), OP.add, more=[pc])
+        ts(("FN", 192, 1024), ("IOT", 192, 1024), P("F1"), OP.add, more=[pc])
+        cp(("SEH", 0, 192), ("EHT", 0, 192))
+        cp(("SEF", 0, 192), ("EFT", 0, 192))
 
-    def zt(t, j0, j1, dst):
-        n, zl = j1 - j0, "ZL%d" % t
-        op("p", [(zl, j0, j1), ("PID", 0, 128)], [("ZTP", 0, 128)], lambda e: e.transpose(T.ZTP[0:n, 0:128], T[zl][:, j0:j1], T.PID[:, :]))
-        cp((dst, 0, 128), ("ZTP", 0, 128), ia=T.ZTP[0:n, 0:128], oa=T[dst][0:n, :], e="s")
+    def turn(o, z):
+        n = z[2] - z[1]
+        mm(("ZP", 0, 128), z, ("PID", 0, 128), True, True, oa=T.ZP[0:n, 0:128])
+        cp((o, 0, 128), ("ZP", 0, 128), ia=T.ZP[0:n, 0:128], oa=T[o][0:n, :], e="s")
 
-    def s_gather(win, lst, c0, c1):
-        gb = "GB%d" % (gbn[0] % 2)
-        gbn[0] += 1
-        gather((gb, 0, 16 * (c1 - c0)), (win, 0, 4096), (lst, c0, c1), e="s")
-        return gb
+    def expand(o, z, on_s):
+        n = 16 * (z[2] - z[1])
+        for k in range(16):
+            cp((o, 0, n), z, oa=T[o][:, k:n:16], e="s" if k < on_s else "v", part=(o,) + z)
 
-    def s_diff(gb, ztb, nl):
-        for h in range(nl // 32):
-            x = 512 * h
-            mm(("D%d" % h, 0, 512), (ztb, 0, 128), ("EX", x, x + 512), True, False, la=T[ztb][0:nl, :], ra=T.EX[0:nl, x:x + 512])
-        for h in range(nl // 32):
-            x = 512 * h
-            mm(("D%d" % h, 0, 512), ("NID", 0, 128), (gb, x, x + 512), False, True)
+    units = [0]
+    waiting = []
 
-    def s_sign(dst, nl):
-        for m in range(nl // 16):
-            d, x = "D%d" % (m // 2), 256 * (m % 2)
-            op("s", [(d, x, x + 256), ("HF", 0, 1)], [(dst, 256 * m, 256 * m + 256)], lambda e: e.activation(T[dst][:, m, :], T[d][:, x:x + 256], AF.Sign, bias=T.HF[:, 0:1]))
+    def s_unit(dst, m, win, lst, col0, zt, row):
+        u = units[0] % 2
+        units[0] += 1
+        d, gb = ("D%d" % u, 0, 512), ("GB%d" % u, 0, 512)
+        mm(d, (zt, 0, 128), ("EX", 0, 512), True, False, la=T[zt][row:row + 32, :], ra=T.EX[row:row + 32, :])
+        gather(gb, (win, 0, 4096), (lst, col0, col0 + 32), e="s")
+        mm(d, ("NID", 0, 128), gb, False, True)
+        s_step()
+        waiting.append((dst, m, d[0]))
 
-    def sums(key, src, b0, b1, m0, xw, last):
-        for c in range(16):
-            mm((key, 16 * (m0 + b0), 16 * (m0 + b1)), (xw, 0, 144), (src, 256 * b0, 256 * b1), False, last and c == 15,
-               la=T[xw][:, 15 - c:143 - c], ra=T[src][:, b0:b1, 16 * c:16 * c + 16])
+    def s_step():
+        while waiting:
+            dst, m, d = waiting.pop()
+            for h in range(2):
+                op("s", [(d, 0, 512), ("HF", 0, 1)], [(dst, 256 * (m + h), 256 * (m + h) + 256)],
+                   lambda e: e.activation(T[dst][:, m + h, :], T[d][:, 256 * h:256 * h + 256], AF.Sigmoid, bias=T.HF[:, 0:1], scale=400.0))
+
+    def v_block(dst, m, win, lst, col0, zx, b):
+        l, x = (lst, col0, col0 + 16), (zx, 256 * b, 256 * b + 256)
+        tt((dst, 256 * m, 256 * m + 256), (win, 0, 4096), x, OP.is_le, ia=T[win][:, 0:4096].indirect(A(l)), more=[l], oa=T[dst][:, m, :])
 
     def key_open(key):
-        mm((key, 0, 256), ("BO16", 0, 128), ("KC", 0, 256), True, False)
+        mm((key, 0, 256), ("BO", 0, 128), ("KC", 0, 256), True, False)
 
-    def v_block(dst, win, lst, b):
-        l, x = (lst, 16 * b, 16 * b + 16), (256 * b, 256 * b + 256)
-        tt((dst, x[0], x[1]), (win, 0, 4096), ("ZX", x[0], x[1]), OP.is_le, ia=T[win][:, 0:4096].indirect(A(l)), more=[l], oa=T[dst][:, b, :])
+    def sums(key, src, m0, m1, last=False):
+        for k in range(16):
+            mm((key, 16 * m0, 16 * m1), ("XV", 0, 144), (src, 256 * m0, 256 * m1), False, last and k == 15,
+               la=T.XV[:, 16 - k:144 - k], ra=T[src][:, m0:m1, 16 * k:16 * k + 16])
 
-    def spread(src, dst, start=True):
-        for c in range(16):
-            mm((dst, 0, 256), ("RO", 128 * c, 128 * c + 128), (src, 0, 16), start, start or c == 15, oa=T[dst][:, c:256:16])
+    def slots_in(parts):
+        ep, tr = ("EP", 0, 256), ("TR", 0, 256)
+        for (src, b0, b1, h) in parts:
+            ts(ep, src, -2048.0, OP.add, oa=T.EP[:, b0:b1, 16 * h:16 * h + 16], part=parts)
+        op("v", [ep], [tr], lambda e: e.transpose(T.TR[:, :, :], T.EP[:, :, :]))
 
-    nb2j = 192 - 16 * NB2
+    def slots_mm():
+        for (h2, h, l, a) in ((0, 0, "BE", 16), (0, 1, "BE", 0), (1, 1, "BD", 16), (1, 0, "BD", 32)):
+            mm(("KH", 128 * h2, 128 * h2 + 128), (l, a, a + 128), ("TR", 0, 256), False, False, ra=T.TR[:, :, 16 * h:16 * h + 16])
 
-    def fresh(t):
-        return ("EHO", "EFO", 192) if t == 0 else ("SEH", "SEF", 64 * (t - 1))
+    def spread(src, start):
+        for k in range(16):
+            mm(("PA", 0, 256), ("RO", 128 * k, 128 * k + 128), src, start, start or k == 15, oa=T.PA[:, k:256:16])
 
-    def fresh_home(t):
-        lst, _f, c0 = fresh(t)
-        zt(t, 192, 256, "ZT1")
-        gb = s_gather("TAB", lst, c0, c0 + 64)
-        s_diff(gb, "ZT1", 64)
-        s_sign("S1H", 64)
-        key_open("KH")
-        sums("KH", "S1H", 0, 4, 12, "XS", False)
+    def pick(x, src, n, stop=True):
+        for k in range(16):
+            mm(("PB", 0, n), (x, 16 - k, 144 - k), src, k == 0, stop and k == 15, ra=T[src[0]][:, src[1] + k:src[2]:16])
 
-    def fresh_foreign(t):
-        _h, lst, c0 = fresh(t)
-        gb = s_gather("FT%d" % t, lst, c0, c0 + 64)
-        key_open("KF")
-        s_diff(gb, "ZT1", 64)
-        s_sign("S1F", 64)
-        sums("KF", "S1F", 0, 4, 12, "XS", False)
-
-    def expand(t):
-        for kk in range(16):
-            cp(("ZX", 0, 256 * NBV), ("ZL%d" % t, 0, 16 * NBV), oa=T.ZX[:, kk:256 * NBV:16], e="s" if kk < ZS else "v")
-
-    def step_main(t):
-        ft, half = "FT%d" % t, (NBV + 1) // 2
-        if t:
-            expand(t)
-        for b in range(NBV):
-            v_block("CH", "TAB", "EHO", b)
-        zt(t, nb2j, 192, "ZT2")
-        ga = s_gather("TAB", "EHO", nb2j, 192)
-        if t:
-            gb = s_gather(ft, "EFO", nb2j, 192)
-        s_diff(ga, "ZT2", 16 * NB2)
-        s_sign("S2H", 16 * NB2)
-        sums("KH", "CH", 0, half, 0, "XV", False)
-        sums("KH", "S2H", 0, NB2, NBV, "XS", False)
-        sums("KH", "CH", half, NBV, 0, "XV", True)
-        if t == 0:
-            gather(("EFO", 0, 256), ("EFT", 192, 448), ("CLA", 0, 16))
-            constants_1()
-            constants_s()
-            claim_slots_1(t)
-            fresh_foreign(0)
-            gb = s_gather(ft, "EFO", nb2j, 192)
-        s_diff(gb, "ZT2", 16 * NB2)
-        s_sign("S2F", 16 * NB2)
-        for b in range(half):
-            v_block("CF", ft, "EFO", b)
-        if t:
-            claim_slots_1(t)
-        sums("KF", "CF", 0, half, 0, "XV", False)
-        for b in range(half, NBV):
-            v_block("CF", ft, "EFO", b)
-        if t == 0:
-            constants_2()
-        claim_slots_2(t)
-        sums("KF", "S2F", 0, NB2, NBV, "XS", False)
-        sums("KF", "CF", half, NBV, 0, "XV", True)
-
-    def claim_slots_1(t):
+    def slot_1(t):
         scan(("SH", 0, 256), ("SCM", 0, 256), ("KH", 0, 256), 0.0, OP.mult, OP.max)
-        cp(("IW", 0, 16), ("SH", 0, 256), ia=T.SH[:, 15:256:16])
-        ts(("IW", 16, 32), ("IW", 0, 16), 13, OP.arith_shift_right, 15, OP.bitwise_and)
-        cp(("KW", 0, 16), ("IW", 16, 32))
-        spread("KW", "KRP")
+        cp(("IW", 0, 16), ("SH", 0, 256), ia=ends("SH"))
+        ts(("IW", 16, 32), ("IW", 0, 16), 4095, OP.bitwise_and)
+        ts(("WH", 0, 16), ("IW", 16, 32), -2048.0, OP.add)
+        if t:
+            cp(("SL", 0, 16), ("IW", 16, 32))
+        ts(w("SW"), ("IW", 16, 32), -2048.0, OP.add)
+        spread(("WH", 0, 16), True)
 
-    def claim_slots_2(t):
-        ts(("OH", 0, 256), ("KRP", 0, 256), P15, OP.is_equal, more=[pc])
-        tt(("MSK", 0, 256), ("OH", 0, 256), ("EHH%d" % t, 0, 256), OP.mult)
-        mm(("SRP", 0, 256), ("BO", 0, 128), ("MSK", 0, 256), True, False)
-        for i in range(16):
-            mm(("SWP", 0, 16), ("X1", 15 - i, 143 - i), ("MSK", 0, 256), i == 0, i == 15, ra=T.MSK[:, i:256:16])
-        op("s", [("SWP", 0, 16)], [w("NSW")], lambda e: e.activation(A(w("NSW")), T.SWP[:, 0:16], AF.Copy, scale=-1.0))
-        ts(w("DTT"), w("DT0"), float(256 * t), OP.add)
-        ts(w("DT2"), w("DT0"), float(256 * t - 2048), OP.add)
+    def slot_2():
+        cp(("SR", 0, 256), ("PA", 0, 256))
+        mm(("CN", 0, 256), ("PID", 0, 128), ("CM", 0, 256), True, False)
+        mm(("CN", 0, 256), ("PIH", 0, 128), ("SR", 0, 256), False, False)
 
-    def step_claims(t):
+    def owner_1():
+        gather(("OG", 0, 256), ("OCC", 0, 4096), ("SL", 0, 16))
+
+    def owner_2():
+        pick("XO", ("OG", 0, 256), 16)
+        cp(("BL", 0, 16), ("PB", 0, 16))
+        ts(w("OC"), ("PB", 0, 16), 0.0, OP.is_ge)
+        tt(w("Y0"), ("PB", 0, 16), w("FW"), OP.subtract)
+        tt(w("Y"), w("Y0"), w("OC"), OP.mult)
+
+    def owner_3():
+        gather(("DB", 256, 512), ("ST", 0, 1024), ("BL", 0, 16), e="s", bias=-127.0)
+        pick("X0", ("DB", 0, 512), 32)
+
+    def owner_4():
+        ts(w("X0"), ("PB", 0, 16), 128.0, OP.add)
+        tt(w("X1"), ("PB", 16, 32), w("X0"), OP.subtract)
+        tt(w("X0"), w("X1"), w("OC"), OP.mult)
+        ts(w("X"), w("X0"), 128.0, OP.add)
+
+    def mark(t):
+        memset(("ST", 192 - 64 * t, 256 - 64 * t), 128.0)
+        scatter(("ST", 0, 1024), ("FL", 0, 12), ("PM", 0, 192))
+
+    def lanes(t):
+        return z0 if t == 0 else ("ZL%d" % t, 0, 256)
+
+    def claims(t):
         wl = ("WL%d" % t, 0, 16)
-        cp(w("SW"), ("SWP", 0, 16))
-        tt(w("SD"), w("SW"), w("DT2"), OP.subtract)
-        scan(("SF", 0, 256), ("SCM", 0, 256), ("KF", 0, 256), 0.0, OP.mult, OP.max)
-        tt(w("WM"), ("SH", 0, 256), ("SF", 0, 256), OP.max, ia=T.SH[:, 15:256:16], ib=T.SF[:, 15:256:16])
-        ts(("NG", 0, 16), w("WM"), 9 * W1, OP.is_ge, 8192.0, OP.mult)
-        spread("NG", "SRP", False)
-        ts(w("GO"), w("WM"), 9 * W1, OP.is_lt)
-        ts(w("NO"), w("WM"), 9 * W1, OP.is_ge)
+        if t:
+            scan(("SF", 0, 256), ("SCM", 0, 256), ("KF", 0, 256), 0.0, OP.mult, OP.max)
+            tt(w("WM"), ("SH", 0, 256), ("SF", 0, 256), OP.max, ia=ends("SH"), ib=ends("SF"))
+        else:
+            tt(w("WM"), ("SH", 0, 256), ("RP", 0, 16), OP.max, ia=ends("SH"))
+        ts(w("NG"), w("WM"), 9 * W1, OP.is_ge, BIG, OP.mult)
         cp(("IW", 32, 48), w("WM"))
-        tt(w("GSD"), w("GO"), w("SD"), OP.mult)
-        ts(("IW", 48, 64), ("IW", 32, 48), 17, OP.arith_shift_right)
-        cp(("SR", 0, 256), ("SRP", 0, 256))
-        for m in (0, 15, 1, 14, 2, 13, 3, 12, 11, 10, 9, 8, 4, 5, 6, 7):
-            end = 256 * m + 256 if m < 8 else 2048 + 128 * (m - 7)
-            o, i = ("EE", end - 256 + 16 * m, end), (16 * m, 256)
-            if m < 4:
-                op("s", [("SRP", i[0], 256), w("NSW")], [o], lambda e: e.activation(A(o), T.SRP[:, i[0]:256], AF.Abs, bias=A(w("NSW", m, m + 1))))
-            else:
-                ts(o, ("SR", i[0], 256), A(w("SW", m, m + 1)), OP.not_equal, more=[w("SW")])
-        tt(w("WN"), ("IW", 48, 64), w("NO"), OP.mult)
-        for (lo, hi, st, a) in ((2048, 3072, 128, 8), (0, 2048, 256, 0)):
-            scan(("CO", lo, hi), ("EE", lo, hi), ("HH", lo, hi), 1.0, OP.min, OP.max)
-        for (lo, hi, st, a) in ((2048, 3072, 128, 8), (0, 2048, 256, 0)):
-            ts(w("ND", a, a + 8), ("CO", lo, hi), 0.25, OP.is_gt, ia=T.CO[:, lo + st - 1:hi:st])
-        tt(w("XW"), w("ND"), w("GSD"), OP.mult)
-        tt(w("WN2"), w("ND"), w("GO"), OP.mult)
-        tt(w("YW"), w("XW"), w("DTT"), OP.add)
-        ts(w("WN2"), w("WN2"), 128.0, OP.mult)
-        cp(wl, w("YW"))
-        tt(("INC", 0, 16), w("WN"), w("WN2"), OP.add)
-        spread("INC", "KRP")
-        scatter(("TAB", 0, WT), wl, ("ZL%d" % t, 0, 256))
-
-    def out_table(h):
-        dma("y", "out%d" % h, [("TAB", 2048 * h, 2048 * h + 2048)], [("yt", 2048 * h, 2048 * h + 2048)],
-            lambda e: e.dma_start(T.yt[:, 2048 * h:2048 * h + 2048], T.TAB[:, 2048 * h:2048 * h + 2048]))
-
-    def step_state(t):
-        wl, fl = ("WL%d" % t, 0, 16), ("FL%d" % t, 0, 16)
-        st, st0 = ("ST", 0, 1024 + WT), ("ST", 0, 1024)
+        for m in range(16):
+            n = 256 - 16 * m
+            ts(("EE", 256 * m, 256 * m + n), ("SR", 16 * m, 256), A(w("SW", m, m + 1)), OP.subtract, A(w("NG", m, m + 1)), OP.is_equal,
+               oa=T.EE[:, m, 0:n], more=[w("SW"), w("NG")])
+            if m < 15:
+                mm(("CN", 16 * m + 16, 256), ("BO8", 0, 128), ("EE", 256 * m, 256 * m + n), False, False, ra=T.EE[:, m, 16:n])
+            if m % 4 == 3:
+                mm(("CN", 16 * m - 48, 16 * m + 16), ("TRI", 0, 128), ("EE", 256 * m - 768, 256 * m + 256), False, m == 15, ra=T.EE[:, m - 3:m + 1, 0:16])
+        ts(("IW", 48, 64), ("IW", 32, 48), 16, OP.arith_shift_right)
         if t:
-            tt(("WA", 0, 256), ("OCC", 0, WT), ("MI", 0, 256), OP.mult, ia=T.OCC[:, :].indirect(A(wl)), more=[wl])
-        if t == 3:
-            out_table(0)
-            occ(t)
-            dma("y", "out2", [("OCC", 0, 4096)], [("YS", 0, 256)], lambda e: e.dma_start(T.YS[:, :], T.OCC[0:128:16, 0:4096]))
-            out_table(1)
+            owner_4()
+            mm(("PA", 0, 256), ("PID", 0, 128), ("DB", 0, 256), True, False)
+        tt(w("WN"), ("IW", 48, 64), w("NG"), OP.min)
+        cs = ("CS", 0, 256)
+        scan(cs, ("RS", 0, 256), ("CN", 0, 256), -20000.0, OP.max, OP.min)
         if t:
-            scan(("WB", 0, 256), ("M0", 0, 256), ("WA", 0, 256), 0.0, OP.mult, OP.add)
-            cp(("BL", 0, 16), ("WB", 0, 256), ia=T.WB[:, 15:256:16])
-            gather(("BN", 0, 256), st, ("BL", 0, 16), e="s", bias=-127.0)
-        tt(("STN", 0, 256), ("KRP", 0, 256), ("DL", 0, 256), OP.add)
-        scatter(st0, fl, ("STN", 0, 256))
+            ts(w("WIN"), cs, 4096.0 - OFF, OP.is_lt, ia=ends("CS"))
+            ts(wl, cs, OFF, OP.add, ia=ends("CS"))
+            tt(w("T1"), w("WIN"), w("X"), OP.mult)
+            tt(w("T2"), w("WIN"), w("Y"), OP.mult)
+        else:
+            ts(w("T1"), cs, 4096.0 - OFF, OP.is_lt, 128.0, OP.mult, ia=ends("CS"))
+            ts(wl, cs, OFF, OP.add, ia=ends("CS"))
+        tt(("WH", 16, 32), w("T1"), w("WN"), OP.add)
+        spread(("WH", 16, 32), t == 0)
+        if t < 3:
+            put(("RL%d" % (t + 1), 0, 16), wl, asker(t + 1), "rl%d" % (t + 1), "loc%d" % (8 + t))
         if t:
-            scatter(st, ("BL", 0, 16), ("BN", 0, 256))
+            tt(w("TF"), w("T2"), w("FW"), OP.add)
+        scatter(("TAB", 0, WT), wl, lanes(t))
+        if t < 2:
+            snapshot(t + 2)
+        if t:
+            cp(("TL", 0, 16), w("TF"))
+            cp(("STN", 0, 256), ("PA", 0, 256), e="s")
+            scatter(("ST", 0, 1024), ("TL", 0, 16), ("STN", 0, 256))
+        else:
+            cp(("ST", 192, 448), ("PA", 0, 256), e="s")
 
     def occ(t):
-        scatter(("OCC", 0, WT), ("WL%d" % t, 0, 16), ("LW%d" % t, BASE, BASE + 256), more=[("WA", 0, 256)])
+        scatter(("OCC", 0, WT), ("WL%d" % t, 0, 16), ("FR%d" % t, 0, 256) if t else ("FN", 192, 448))
 
-    def step_select(t):
-        U, lo = 256 * t, 256 - 64 * t
-        new, n = lo + U, 16 * t
-        lw, fl, zl = "LW%d" % t, ("FL%d" % t, 0, 12), ("ZL%d" % t, 0, 192)
-        if t == 1:
-            ts(("FB", 0, 1), ("DL", 0, 1), 0.0, OP.mult)
-        ts(("FB", U + 1, U + 2), ("DL", 0, 1), 0.0, OP.mult, -1.0, OP.add)
-        ts(("FB", 1, U + 1), ("ST", lo, lo + U), 128.0, OP.is_lt, -1.0, OP.mult)
-        scan(("VB", 0, U + 1), ("FB", 1, U + 2), ("FB", 0, U + 1), 2000.0, OP.add, OP.add)
-        scan(("VW", 0, U), ("M0H", 0, U), ("VB", 0, U), 0.0, OP.mult, OP.max)
-        ts(("VC", 0, 1), ("VB", U, U + 1), float(2 * new - 1999), OP.add)
+    def fresh_1(t):
+        a = 192 - 64 * t
+        turn("ZTF", ("ZFT", a, a + 64))
+        cp(("ZL%d" % t, 0, 64), ("ZFT", a, a + 64), e="s")
+        cp(("FR%d" % t, 0, 64), ("FN", a, a + 64), e="s")
 
-        def I(k):
-            return ("II", 48 * k, 48 * k + n)
-        ts(I(0), ("VW", 0, U), -1.0, OP.mult, 2000.0, OP.add, ia=T.VW[:, 15:U:16])
-        ts((lw, BASE, BASE + 192), ("CJ2", 0, 192), T.VC[:, 0:1], OP.add, 0.5, OP.mult, more=[("VC", 0, 1)])
-        ts(I(1), I(0), 1, OP.bitwise_and)
-        ts(I(2), I(0), 1, OP.arith_shift_right)
-        tt(I(3), I(1), ("DW", 0, n), OP.mult)
-        tt(I(4), ("C1", 0, n), I(2), OP.subtract)
-        tt(I(5), I(4), I(3), OP.subtract)
-        cp(("LU", 0, n), I(5))
-        scatter((lw, 0, BASE + 1024), ("LU", 0, n), ("IOT", lo, lo + U))
-        scan(("WS", 0, 192), ("M0", 0, 192), (lw, BASE, BASE + 192), 0.0, OP.mult, OP.max)
-        cp(fl, ("WS", 0, 192), ia=T.WS[:, 15:192:16])
+    def fresh_2(t, dst, win, lst, u):
+        s_unit(dst, 2 * u, win, lst, 192 - 64 * t + 32 * u, "ZTF", 32 * u)
+
+    def select(t):
+        U, lo, n = 256 * t, 256 - 64 * t, 16 * t
+        ft, fl = "FT%d" % t, ("FL", 0, 12)
+        key_open("KH")
+        fresh_2(t, "CH", "TAB", "SEH", 0)
+        fresh_2(t, "CH", "TAB", "SEH", 1)
+        ts(("FB", 0, U), ("ST", lo, lo + U), 128.0, OP.is_lt)
+        scan(("VB", 0, U), ("AB", 0, U), ("FB", 0, U), 0.0, OP.mult, OP.add)
+        mm(("PB", 48, 49), ("BO0", 0, 128), ("VB", U - 1, U), True, True)
+        pick("XP", ("VB", 0, U), n)
+        scatter((ft, 0, WT), ("RL%d" % t, 0, 16), ("RZ%d" % t, 0, 256))
+        key_open("KF")
+        fresh_2(t, "CF", ft, "SEF", 0)
+        tt(("LF", 0, n), ("PB", 0, n), ("DW", 0, n), OP.min)
+        ts(("LW", 0, 192), ("JR", 0, 192), T.PB[:, 48:49], OP.subtract, float(lo + U), OP.add, more=[("PB", 48, 49)])
+        ts(("LU", 0, n), ("LF", 0, n), 2047.0, OP.add)
+        scatter(("LW", 0, 1536), ("LU", 0, n), ("IOT", lo, lo + U))
+        sums("KH", "CH", 0, 4)
+        fresh_2(t, "CF", ft, "SEF", 1)
+        s_step()
+        sums("KF", "CF", 0, 4)
+        scan(("WS", 0, 192), ("MB", 0, 192), ("LW", 0, 192), 0.0, OP.max, OP.min)
+        cp(fl, ("WS", 0, 192), ia=ends("WS", 192))
+
+    def entries(tab, a, b, o):
+        fl = ("FL", 0, 12)
+        tt((a, 0, 192), (tab, 0, 1024), ("DB", 64, 256), OP.add, ia=T[tab][:, :].indirect(A(fl)), more=[fl])
+        ts((b, 0, 192), (a, 0, 192), 4095, OP.bitwise_and)
+        cp((o, 0, 192), (b, 0, 192))
+
+    def penalties(t):
+        ft, fl, zl, a = "FT%d" % t, ("FL", 0, 12), "ZL%d" % t, 192 - 64 * t
+        gather(("DB", 64, 256), ("ST", 0, 1024), fl)
+        gather((zl, 64, 256), ("ZFT", 0, 1024), fl, e="s")
+        if t < 3:
+            put(("RZ%d" % (t + 1), 0, 256), (zl, 0, 256), asker(t + 1), "rz%d" % (t + 1), "loc%d" % (4 + t))
+        entries("EHT", "EI", "EM", "EHO")
+        turn("ZT", (zl, 64, 192))
+        expand("ZX", (zl, 128, 256), 8)
+
+        def vh(m):
+            v_block("CH", m, "TAB", "EHO", 16 * m - 64, "ZX", m - 8)
+
+        def vf(m):
+            v_block("CF", m, ft, "EFO", 16 * m - 64, "ZX", m - 8)
+
+        def sh(m):
+            s_unit("CH", m, "TAB", "EHO", 16 * m - 64, "ZT", 16 * m - 64)
+
+        def sf(m):
+            s_unit("CF", m, ft, "EFO", 16 * m - 64, "ZT", 16 * m - 64)
+        sh(4)
+        vh(15)
+        vh(14)
+        sh(6)
+        entries("EFT", "FI", "FM", "EFO")
+        vh(13)
+        vh(12)
+        sums("KH", "CH", 12, 16)
+        sf(4)
+        slots_in(((("EHT", a, a + 64), 0, 4, 0), (("EM", 0, 64), 4, 8, 0), (("EM", 64, 192), 0, 8, 1)))
+        sums("KH", "CH", 4, 8)
+        slots_mm()
+        for m in (11, 10, 9, 8):
+            vh(m)
+        sf(6)
+        sums("KH", "CH", 8, 12, True)
         occ(t - 1)
-        gather(("DL", 0, 192), ("ST", 0, 1024), fl, e="s")
-        gather(zl, ("ZFT", 0, 1024), fl, e="s")
-        for (tab, a, b, o) in (("EHT", "EI", "EM", "EHO"), ("EFT", "FI", "FM", "EFO")):
-            tt((a, 0, 192), (tab, 0, 1024), ("DL", 0, 192), OP.add, ia=T[tab][:, :].indirect(A(fl)), more=[fl])
-            ts((b, 0, 192), (a, 0, 192), 4095, OP.bitwise_and)
-            cp((o, 0, 192), (b, 0, 192))
-        ts(("EHH%d" % t, 0, 192), ("EM", 0, 192), -2048.0, OP.add)
+        sf(8)
+        slot_1(t)
+        cp(w("FW", 4, 16), ("WS", 0, 192), ia=ends("WS", 192))
+        ts(w("FW", 0, 4), ("CI", 0, 4), P("I"), OP.add, float(a), OP.add, more=[pc])
+        owner_1()
+        sums("KF", "CF", 4, 8)
+        sf(10)
+        vf(15)
+        slot_2()
+        vf(14)
+        owner_2()
+        s_step()
+        vf(13)
+        vf(12)
+        sums("KF", "CF", 8, 10)
+        sums("KF", "CF", 14, 16)
+        sums("KF", "CF", 10, 14, True)
+        gather(("FR%d" % t, 64, 256), ("FN", 0, 1024), fl, e="s")
+        owner_3()
+        if t < 3:
+            cp(("PM", 0, 192), ("DB", 64, 256), e="s", bias=128.0)
+            mark(t)
+            fresh_1(t + 1)
 
-    memset(("WA", 0, 256), 0.0)
-    expand(0)
-    fresh_home(0)
+    def penalties_0():
+        turn("ZT", ("ZFT", 192, 320))
+        expand("ZX", ("ZFT", 320, 448), 0)
+        constants_1()
+        slots_in(((("EHT", 192, 320), 0, 8, 0), (("EHT", 320, 448), 0, 8, 1)))
+        snapshot(1)
+        put(("RZ1", 0, 256), z0, asker(1), "rz1", "loc4")
+        for k, (o, i) in enumerate((("EHT", "eh"), ("ZFT", "zf"), ("EFT", "ef"))):
+            load(5 + k, o, 0, 192, i, 832, 1024, "loc1" if k == 0 else None)
+
+        def vh(m):
+            v_block("CH", m, "TAB", "EHO", 16 * m, "ZX", m - 8)
+
+        def vf(m):
+            v_block("CF", m, "TAB", "QE", 16 * m, "ZXQ", m - 6)
+
+        def sh(m):
+            s_unit("CH", m, "TAB", "EHO", 16 * m, "ZT", 16 * m)
+
+        def sf(m):
+            s_unit("CF", m, "TAB", "QE", 16 * m, "ZTQ", 16 * m)
+        key_open("KH")
+        key_open("KF")
+        slots_mm()
+        sh(0)
+        sh(2)
+        for m in (15, 14, 13, 12):
+            vh(m)
+        sums("KH", "CH", 12, 16)
+        turn("ZTQ", ("QZ", 0, 96))
+        expand("ZXQ", ("QZ", 96, 256), 0)
+        sf(0)
+        sums("KH", "CH", 0, 4)
+        for m in (15, 14, 13, 12):
+            vf(m)
+        sf(2)
+        sums("KF", "CF", 12, 16)
+        sf(4)
+        for m in (11, 10, 9, 8):
+            vf(m)
+        sums("KF", "CF", 0, 4)
+        sums("KF", "CF", 8, 12)
+        sh(4)
+        vf(7)
+        vf(6)
+        sums("KF", "CF", 4, 8, True)
+        sh(6)
+        vh(11)
+        vh(10)
+        scan(("SF", 0, 256), ("SCM", 0, 256), ("KF", 0, 256), 0.0, OP.mult, OP.max)
+        cp(("SP", 0, 16), ("SF", 0, 256), ia=ends("SF"))
+        put(("RP", 0, 16), ("SP", 0, 16), asker(0), "rp", "loc11")
+        for k, (o, i) in enumerate((("EHT", "eh"), ("ZFT", "zf"), ("EFT", "ef"))):
+            load(8 + k, o, 448, 1024, i, 256, 832, "loc11" if k == 0 else None)
+        s_step()
+        vh(9)
+        vh(8)
+        sums("KH", "CH", 10, 12)
+        sums("KH", "CH", 4, 10, True)
+        constants_2()
+        slot_1(0)
+        constants_3()
+        slot_2()
+        fresh_1(1)
+
+    penalties_0()
     for t in range(4):
         if t:
-            step_select(t)
-            if t < 3:
-                put("RZ%d" % (t + 1), 0, 256, "ZL%d" % t, asker(t + 1), "rz%d" % (t + 1), "loc%d" % (4 + t))
-        step_main(t)
-        step_claims(t)
-        u = t + 1
-        if t < 3:
-            dst = cores[asker(u)]
-            rid, pid, _se = topo.addr(dst)
-            send("loc%d" % (8 + t), len(topo.engines(core, dst)), [("WL%d" % t, 0, 16)],
-                 lambda e: e.remote_dma(T["RL%d" % u][:, :], T["WL%d" % t][:, :], T.sem["rl%d" % u], T.sem["loc%d" % (8 + t)], pid, rid, topo.mask(core, dst)))
-        if t < 2:
-            put("FT%d" % (t + 2), 0, 4096, "TAB", asker(t + 2), "sn%d" % (t + 2), "loc%d" % (12 + t))
-        if t == 0:
-            iota(("ST", 1024, 1024 + WT), [[0, WT]], 0)
-        step_state(t)
-        if t < 3:
-            fresh_home(u)
-            scatter(("FT%d" % u, 0, WT), ("RL%d" % u, 0, 16), ("RZ%d" % u, 0, 256))
-            fresh_foreign(u)
-    ts(("GB0", 0, 1024), ("ST", 0, 1024), 128.0, OP.is_ge, -128.0, OP.mult)
+            select(t)
+            penalties(t)
+        claims(t)
     for h in range(2):
-        d, x = ("D%d" % h, 0, 512), (512 * h, 512 * h + 512)
-        mm(d, ("PID", 0, 128), ("ST", x[0], x[1]), True, False)
-        mm(d, ("PID", 0, 128), ("GB0", x[0], x[1]), False, True)
-        cp(("YD", x[0], x[1]), d, e="s")
-    ys, y1, y2 = ("YS", 0, 256), ("Y1", 0, 256), ("Y2", 0, 256)
-    ts(y1, ys, 192.0, OP.is_lt, 1024.0, OP.mult)
-    ts(y2, ys, 1024.0, OP.is_lt)
-    tt(y1, ys, y1, OP.add)
-    ts(y1, y1, -191.0, OP.add)
-    tt(y1, y1, y2, OP.mult)
-    ts(y1, y1, -1.0, OP.add)
-    dma("y", "out5", [y1], [("yo", 0, 4096)], lambda e: e.dma_start(T.yo[:, :], T.Y1[:, :]))
-    dma("s", "out3", [("YD", 192, 1024)], [("yd", 0, 832)], lambda e: e.dma_start(T.yd[:, 0:832], T.YD[0:128:16, 192:1024]))
-    dma("s", "out4", [("YD", 0, 192)], [("yd", 832, 1024)], lambda e: e.dma_start(T.yd[:, 832:1024], T.YD[0:128:16, 0:192]))
+        x = (2048 * h, 2048 * h + 2048)
+        dma("y", "out%d" % h, [("TAB", x[0], x[1])], [("yt", x[0], x[1])], lambda e: e.dma_start(T.yt[:, x[0]:x[1]], T.TAB[:, x[0]:x[1]]))
+    ts(("YA", 0, 1024), ("ST", 0, 1024), P("LO"), OP.max, P("HI"), OP.min, more=[pc])
+    for k in range(16):
+        a = (64 * k + 192) % 1024
+        mm(("PB", 0, 64), ("XD", 16 - k, 144 - k), ("YA", a, a + 64), k == 0, k == 15)
+    occ(3)
+    dma("y", "out2", [("OCC", 0, 4096)], [("yo", 0, 4096)], lambda e: e.dma_start(T.yo[:, :], T.OCC[0:128:16, 0:4096]))
+    cp(("YD", 0, 64), ("PB", 0, 64), e="s", bias=16256.0)
+    dma("s", "out3", [("YD", 0, 64)], [("yd", 0, 1024)], lambda e: e.dma_start(T.yd[:, :], T.YD[:, :]))
     finish()

@@ -6,18 +6,25 @@ AF = ActivationFunctionType
 W1 = 65536.0
 BIG = 8192.0
 OFF = 2048.0 + BIG
-WT = 4096 + 256
+LOOK = 4096 + 64
+WT = LOOK + 256
+ON = {"SR": "s", "OG": "s", "DL": "s"}
+SPLIT0, SPLIT = (7, 7), (8, 11)
+ZS = 9
+CYC, PE, GATHER, SCATTER, WAKE, WAKE_SAME, FILL, HOP = 0.00085, 0.00035, 1.56, 3.8, 0.17, 0.17, 0.5, 5.0
+ROUNDS, ORDER = 4, []
 SB = "sbuf"
 F32, B16, F16, I32, U16 = "float32", "bfloat16", "float16", "int32", "uint16"
 SCRATCH = {}
 for _names, _w, _d in (
         ("TAB FT1 FT2 FT3", WT, B16), ("OCC", WT, F32), ("ST ZFT YA", 1024, B16), ("EHT EFT", 1024, I32), ("IOT FN", 1024, F32),
         ("PJ", 4, I32), ("PC", 16, F32), ("CI", 48, F32), ("QX", 160, F32), ("Q4 T1 T2", 128, F32), ("JM RS SCM SH SF CS FR1 FR2 FR3", 256, F32),
-        ("JR MB WS", 192, F32), ("DW", 48, F32), ("HF", 8, F32), ("EX EXI GB0 GB1 DB", 512, B16), ("KC CM STN QZ PM", 256, B16),
-        ("XV X0 XD", 144, B16), ("XP XO", 144, F16), ("BE BD", 160, F16), ("BO BO8 TRI NID PID ZT ZTF ZTQ", 128, B16), ("BO0 PIH BOH", 128, F16),
-        ("RO", 2048, F16), ("ZX", 2048, B16), ("ZXQ", 2560, B16), ("SR OG", 256, F16), ("AB FB VB", 768, F16), ("LW", 1536, F32),
-        ("EHO EFO QE", 256, U16), ("SEH SEF", 192, U16), ("EI EM FI FM", 192, I32), ("IW", 64, I32), ("WF", 256, F32), ("WH", 32, F16),
+        ("JR MB WS", 192, F32), ("DW", 48, F32), ("HF", 8, F32), ("EX EXI GB0 GB1 DB", 512, B16), ("KC KD CM STN QZ PM", 256, B16),
+        ("XV X0 XD", 144, B16), ("XP XO", 144, F16), ("BE BD", 160, F16), ("BO BO8 TRI NID PID ZT ZU ZTF ZTQ", 128, B16), ("BO0 PIH BOH", 128, F16),
+        ("RO", 2048, F16), ("ZX ZXQ", 2560, B16), ("SR OG", 256, F16), ("AB FB VB", 768, F16), ("LW", 1536, F32),
+        ("EHO EFO QE", 256, U16), ("SEH SEF", 192, U16), ("EI EM FI", 192, I32), ("IW", 64, I32), ("WF", 256, F32), ("WH", 48, F16),
         ("RP SP", 16, F32), ("LF", 48, F32), ("LU", 48, U16), ("SL BL TL FL", 16, U16), ("YD", 64, F32),
+        ("SF1 SF2 SF3", 256, F32), ("SQ", 64, F32), ("QF", 192, U16), ("QY", 192, B16), ("ZTG TU", 128, B16),
         ("ZL1 ZL2 ZL3 RZ1 RZ2 RZ3", 256, B16), ("WL0 WL1 WL2 WL3 RL1 RL2 RL3", 16, U16)):
     for _n in _names.split():
         SCRATCH[_n] = (SB, [128, _w], _d)
@@ -27,102 +34,172 @@ for _n in ("EP", "TR"):
     SCRATCH[_n] = (SB, [128, 8, 32], F16)
 for _n in ("KH", "KF", "D0", "D1", "ZP", "PA", "PB", "CN"):
     SCRATCH[_n] = ("psum", [128, 512], F32)
-SEMAPHORES = ["cv", "cs", "cp", "cg", "qu", "rp", "hl"] + ["ld%d" % _i for _i in range(12)] + ["sn%d" % _i for _i in range(4)] + ["loc%d" % _i for _i in range(12)]
-SEMAPHORES += ["rz%d" % _i for _i in range(4)] + ["rl%d" % _i for _i in range(4)] + ["out%d" % _i for _i in range(4)]
+SEMAPHORES = ["cv", "cs", "cp", "cg", "qu", "rp", "hl"] + ["ld%d" % _i for _i in range(12)] + ["loc%d" % _i for _i in range(16)]
+SEMAPHORES += ["%s%d" % (_s, _t) for _s in ("sn", "qf", "rq", "rz", "rl") for _t in range(1, 4)] + ["out%d" % _i for _i in range(4)]
 SEMAPHORES += ["h%d%d" % (_t, _q) for _t in range(1, 4) for _q in range(4)]
-WIDX = {n: 16 * i for i, n in enumerate("SW WM NG WN WIN T1 T2 OC X0 X1 X Y0 Y FW TF".split())}
-PCOL = {n: i for i, n in enumerate("I P G P32 M0 M1 EV OD WP WD N1 F0 F1 LO HI".split())}
+WIDX = {n: 16 * i for i, n in enumerate("SW HG HN FA FC WIN T2 OC X0 X1 X Y0 Y FW TF X2".split())}
+PCOL = {n: i for i, n in enumerate("I P G P32 M0 M1 EV OD WP WD N1 F0 F1 LO HI SG".split())}
 
 
 def make(g, T):
     eng = {"v": g.vector, "s": g.scalar, "p": g.tensor, "g": g, "y": g.sync}
     sem = {"v": "cv", "s": "cs", "p": "cp", "g": "cg"}
-    cnt = {"v": 0, "s": 0, "p": 0, "g": 0}
-    know = {e: {} for e in eng}
-    acc, total = {}, {}
-
-    def learn(e, tok):
-        for k, v in tok[3].items():
-            know[e][k] = max(v, know[e].get(k, 0))
-        know[e][tok[0]] = max(tok[1], know[e].get(tok[0], 0))
+    nodes, acc, total, sender, last, open_batch = [], {}, {}, {}, {}, [None]
 
     def psum(b):
         return b in SCRATCH and SCRATCH[b][0] == "psum"
 
-    def needs(owner, reads, writes, part=None):
-        out = []
+    def add(e, own, reads, writes, fns, hold, dur, s=None, part=None):
+        me = {"id": len(nodes), "e": e, "own": own, "fns": fns, "hold": hold, "dur": dur, "s": s, "part": part, "pre": {}}
+        nodes.append(me)
+        link(me, reads, writes)
+        if e in "gy":
+            if e in last:
+                me["pre"].setdefault(last[e], False)
+            last[e] = me["id"]
+        return me
+
+    def link(me, reads, writes):
         for mode, lst in (("r", reads), ("w", writes)):
             for (b, lo, hi) in lst:
                 ps = psum(b)
-                for (l2, h2, m2, tok) in acc.get(b, []):
-                    if not ps and (h2 <= lo or hi <= l2):
+                for (l2, h2, m2, k) in acc.get(b, []):
+                    x = nodes[k]
+                    if x is me or (not ps and (h2 <= lo or hi <= l2)) or (mode == m2 == "r" and (not ps or x["own"] == me["own"])):
                         continue
-                    if mode == "r" and m2 == "r" and not ps:
+                    if me["part"] and mode == m2 == "w" and x["part"] == me["part"]:
                         continue
-                    if tok[2] == owner and ((mode == "r" and m2 == "r") or (mode == "w" and owner == "p")):
-                        continue
-                    if part and mode == m2 == "w" and tok[4:] == (part,):
-                        continue
-                    out.append(tok)
-        return out
-
-    def waits(e, toks):
-        for tok in sorted(toks, key=lambda x: (-len(x[3]), -x[1])):
-            if know[e].get(tok[0], 0) < tok[1]:
-                top = max([x for x in toks if x[0] == tok[0]], key=lambda x: x[1])
-                eng[e].wait_ge(T.sem[top[0]], top[1])
-                learn(e, top)
-
-    def note(tok, reads, writes):
+                    wait = not (x["own"] == me["own"] == "p" and mode == "w")
+                    me["pre"][k] = wait or me["pre"].get(k, False)
         for (b, lo, hi) in writes:
             lst = acc.setdefault(b, [])
-            if not psum(b):
-                lst[:] = [x for x in lst if not (lo <= x[0] and x[1] <= hi) or (x[3][2] != tok[2] and tok[4:] != (None,) and x[3][4:] == tok[4:] != ())]
-            else:
-                lst[:] = [x for x in lst if not (x[3][2] == tok[2] and x[2] == "w" and lo <= x[0] and x[1] <= hi)]
-            lst.append((lo, hi, "w", tok))
+            lst[:] = [x for x in lst if not (psum(b) or (lo <= x[0] and x[1] <= hi)) or (me["part"] and nodes[x[3]]["part"] == me["part"])]
+            lst.append((lo, hi, "w", me["id"]))
         for (b, lo, hi) in reads:
-            lst = acc.setdefault(b, [])
-            lst[:] = [x for x in lst if not (x[2] == "r" and x[3][0] == tok[0] and lo <= x[0] and x[1] <= hi)]
-            lst.append((lo, hi, "r", tok))
+            acc.setdefault(b, []).append((lo, hi, "r", me["id"]))
 
-    def op(e, reads, writes, fn, part=None):
-        waits(e, needs(e, reads, writes, part))
-        cnt[e] += 1
-        fn(eng[e]).then_inc(T.sem[sem[e]], 1)
-        total[sem[e]] = cnt[e]
-        note((sem[e], cnt[e], e, dict(know[e]), part), reads, writes)
+    def op(e, reads, writes, fn, cost, part=None):
+        b = open_batch[0]
+        if b is not None and e in b:
+            b[e]["fns"].append(fn)
+            b[e]["hold"] += cost
+            b[e]["dur"] += cost
+            link(b[e], reads, writes)
+        else:
+            me = add(e, e, reads, writes, [fn], cost, cost, sem[e], part)
+            if b is not None:
+                b[e] = me
 
-    def dma(e, s, reads, writes, fn, after=None):
-        waits(e, needs("dma" + s, reads, writes))
+    def batch(on):
+        open_batch[0] = {} if on else None
+
+    def dma(e, s, reads, writes, fn, dur, after=None):
+        me = add(e, "dma" + s, reads, writes, [fn], 0.1, dur, s)
+        total[s] = 16
         if after:
-            eng[e].wait_ge(T.sem[after], total[after])
-        fn(eng[e]).then_inc(T.sem[s], 16)
-        total[s] = total.get(s, 0) + 16
-        note((s, total[s], "dma" + s, dict(know[e])), reads, writes)
+            me["pre"][sender[after]] = True
 
-    def send(s, n, reads, fn):
-        waits("g", needs("rem" + s, reads, []))
-        fn(g)
+    def send(s, n, reads, fn, lands, dur):
+        me = add("g", "rem" + s, reads, [], [fn], 0.5 if sender else 2.5, dur, s)
         total[s] = total.get(s, 0) + n
-        for r in reads:
-            acc[r[0]] = [x for x in acc.get(r[0], []) if x[3][0] != s]
-        lo = {}
-        for r in sent.setdefault(s, []) + list(reads):
-            lo[r] = 1
-        sent[s] = list(lo)
-        note((s, total[s], "rem" + s, dict(know["g"])), sent[s], [])
+        sender[s] = sender[lands] = me["id"]
 
-    def land(s, n, b, lo, hi):
+    def land(s, n, b, lo, hi, like, lag):
+        me = add("n", "net" + s, [], [(b, lo, hi)], [], 0.0, lag, s)
+        me["like"] = like
         total[s] = n
-        acc.setdefault(b, []).append((lo, hi, "w", (s, n, "net" + s, {})))
+
+    def order():
+        for x in nodes:
+            x["post"] = []
+            if "like" in x:
+                x["pre"][sender[x["like"]]] = False
+        for x in nodes:
+            for k in x["pre"]:
+                nodes[k]["post"].append(x["id"])
+
+        def step(a, b):
+            if b["e"] == "n":
+                return a["dur"]
+            return a["dur"] + (WAKE_SAME if a["e"] == b["e"] else WAKE) if b["pre"][a["id"]] else a["hold"]
+
+        def run(way, back):
+            pre, post = ("post", "pre") if back else ("pre", "post")
+            left = [len(x[pre]) for x in nodes]
+            ready = [x["dur"] - x["hold"] if back else 0.0 for x in nodes]
+            free = {e: 0.0 for e in "vspgyn"}
+            cand = {e: [x for x in nodes if x["e"] == e and not x[pre]] for e in free}
+            out, start = [], [0.0] * len(nodes)
+            while len(out) < len(nodes):
+                best = None
+                for e, lst in cand.items():
+                    if not lst:
+                        continue
+                    lst.sort(key=lambda x: (-way[x["id"]], x["id"]))
+                    pick = lst[0]
+                    r = ready[pick["id"]]
+                    if e == "n":
+                        pick = min(lst, key=lambda x: ready[x["id"]])
+                    elif r > free[e]:
+                        for y in lst[1:]:
+                            at = max(free[e], ready[y["id"]])
+                            if at < r and at + y["hold"] - r < FILL * (r - at) + max(0.0, y["hold"] - way[pick["id"]] + way[y["id"]]):
+                                pick = y
+                                break
+                    at = max(free[e], ready[pick["id"]])
+                    if best is None or at < best[0]:
+                        best = (at, pick)
+                at, x = best
+                cand[x["e"]].remove(x)
+                free[x["e"]] = at + x["hold"]
+                start[x["id"]] = at
+                out.append(x)
+                for k in x[post]:
+                    y = nodes[k]
+                    ready[k] = max(ready[k], at + (x["hold"] + step(y, x) - y["hold"] if back else step(x, y)))
+                    left[k] -= 1
+                    if not left[k]:
+                        cand[y["e"]].append(y)
+            return out, [start[x["id"]] + x["hold"] for x in nodes], max(start[x["id"]] + x["dur"] for x in nodes)
+        if not ORDER:
+            way, best = [float(x["id"]) for x in nodes], None
+            for _ in range(ROUNDS):
+                way = run(way, True)[1]
+                out, way, end = run(way, False)
+                if best is None or end < best[0]:
+                    best = (end, [x["id"] for x in out])
+            ORDER.extend(best[1])
+        return [nodes[k] for k in ORDER]
 
     def finish():
+        know = {e: {} for e in eng}
+        cnt = {e: 0 for e in sem}
+        for x in order():
+            e = x["e"]
+            if e == "n":
+                x["tok"] = (x["s"], total[x["s"]], {})
+                continue
+            toks = [nodes[k]["tok"] for k, wait in x["pre"].items() if wait]
+            for tok in sorted(toks, key=lambda y: (-len(y[2]), -y[1])):
+                if know[e].get(tok[0], 0) < tok[1]:
+                    top = max([y for y in toks if y[0] == tok[0]], key=lambda y: y[1])
+                    eng[e].wait_ge(T.sem[top[0]], top[1])
+                    for k, v in list(top[2].items()) + [top[:2]]:
+                        know[e][k] = max(v, know[e].get(k, 0))
+            for fn in x["fns"]:
+                if x["own"] == e:
+                    cnt[e] += 1
+                    fn(eng[e]).then_inc(T.sem[sem[e]], 1)
+                    total[sem[e]] = cnt[e]
+                elif x["own"].startswith("dma"):
+                    fn(eng[e]).then_inc(T.sem[x["s"]], 16)
+                else:
+                    fn(eng[e])
+            x["tok"] = (x["s"], total[x["s"]], dict(know[e]))
         for s, v in total.items():
             if know["g"].get(s, 0) < v:
                 g.wait_ge(T.sem[s], v)
-    sent = {}
-    return op, dma, send, land, finish
+    return op, batch, dma, send, land, finish
 
 
 def bits(engines):
@@ -133,6 +210,11 @@ def helpers(topo, cores, rank):
     me = cores[rank]
     free = [c for c in topo.cores_of(me) if c != me and all(topo.may_write(c, o) for o in cores if o != me)]
     return [[c for c in free if topo.die(c) != topo.die(me)][0], [c for c in free if topo.die(c) == topo.die(me)][0]]
+
+
+def inner(topo, cores, rank, helper, t):
+    out = topo.engines(cores[rank], cores[rank - 1]) if t > 3 else []
+    return [e for e in topo.engines(cores[rank], helper) if e not in out]
 
 
 def hand_on(g, core, T, topo):
@@ -146,7 +228,7 @@ def hand_on(g, core, T, topo):
             rid, pid, _se = topo.addr(dst)
             for q in range(two.index(core), 4, 2):
                 x = T["FT%d" % t][:, 1024 * q:1024 * q + 1024]
-                g.wait_ge(T.sem["h%d%d" % (t, q)], len(topo.engines(T.cores[rank], core)))
+                g.wait_ge(T.sem["h%d%d" % (t, q)], len(inner(topo, T.cores, rank, core, t)))
                 g.remote_dma(x, x, T.sem["sn%d" % t], T.sem["hl"], pid, rid, topo.mask(core, dst))
                 n += len(topo.engines(core, dst))
         g.wait_ge(T.sem["hl"], n)
@@ -156,16 +238,17 @@ def rank_program(g, core, T, topo):
     rank = T.rank_of(core)
     if rank is None:
         return hand_on(g, core, T, topo)
-    op, dma, send, land, finish = make(g, T)
+    op, batch, dma, send, land, finish = make(g, T)
     cores = T.cores
     mine = helpers(topo, cores, rank)
 
     def A(x):
         return T[x[0]][:, x[1]:x[2]]
 
-    def put(o, i, dst, rsem, lsem):
+    def put(o, i, dst, rsem, lsem, en=None, more=(), dur=1.5):
         rid, pid, _se = topo.addr(dst)
-        send(lsem, len(topo.engines(core, dst)), [i], lambda e: e.remote_dma(A(o), A(i), T.sem[rsem], T.sem[lsem], pid, rid, topo.mask(core, dst)))
+        en = en or topo.engines(core, dst)
+        send(lsem, len(en), [i] + list(more), lambda e: e.remote_dma(A(o), A(i), T.sem[rsem], T.sem[lsem], pid, rid, bits(en)), rsem, dur)
 
     def asker(t):
         return cores[(rank - 1 - t % 3) % 4]
@@ -173,9 +256,10 @@ def rank_program(g, core, T, topo):
     def seen(t):
         return (rank + 1 + t % 3) % 4
 
-    def snapshot(t):
-        for q in range(4):
-            put(("FT%d" % t, 1024 * q, 1024 * q + 1024), ("TAB", 1024 * q, 1024 * q + 1024), mine[q % 2], "h%d%d" % (t, q), "loc%d" % t)
+    def snapshot(t, quarters=range(4), lsem=None):
+        for n, q in enumerate(quarters):
+            put(("FT%d" % t, 1024 * q, 1024 * q + 1024), ("TAB", 1024 * q, 1024 * q + 1024), mine[q % 2], "h%d%d" % (t, q), lsem or "loc%d" % t,
+                inner(topo, cores, rank, mine[q % 2], t), [("EHT", 0, 192)] if t == 1 else [], 2.5 + 1.5 * n)
 
     def w(n, a=0, b=16):
         return ("WF", WIDX[n] + a, WIDX[n] + b)
@@ -185,63 +269,86 @@ def rank_program(g, core, T, topo):
     def P(n):
         return T.PC[:, PCOL[n]:PCOL[n] + 1]
 
+    def cost(out, sides, each):
+        n = 1
+        for k in out.shape[1:]:
+            n *= k
+        if each is None:
+            each = 0.5 if all(SCRATCH[x[0]][2] in (B16, F16, U16) for x in sides) else 1.0
+        return CYC * max(64, n * each)
+
     def ts(o, i, s1, o0, s2=None, o1=None, ia=None, oa=None, more=(), part=None):
         rd = [i] + list(more)
         src, out = A(i) if ia is None else ia, A(o) if oa is None else oa
         if o1 is None:
-            op("v", rd, [o], lambda e: e.tensor_scalar(out, src, s1, None, o0), part)
+            op("v", rd, [o], lambda e: e.tensor_scalar(out, src, s1, None, o0), cost(out, [o, i], None), part)
         else:
-            op("v", rd, [o], lambda e: e.tensor_scalar(out, src, s1, s2, o0, o1), part)
+            op("v", rd, [o], lambda e: e.tensor_scalar(out, src, s1, s2, o0, o1), cost(out, [o, i], None), part)
 
-    def tt(o, a, b, f, ia=None, ib=None, more=(), oa=None):
-        op("v", [a, b] + list(more), [o], lambda e: e.tensor_tensor(A(o) if oa is None else oa, A(a) if ia is None else ia, A(b) if ib is None else ib, f))
+    def tt(o, a, b, f, ia=None, ib=None, more=(), oa=None, lst=None):
+        out = A(o) if oa is None else oa
+        if lst:
+            ia, more = A(a).indirect(A(lst)), [lst]
+        op("v", [a, b] + list(more), [o], lambda e: e.tensor_tensor(out, A(a) if ia is None else ia, A(b) if ib is None else ib, f),
+           0.055 + cost(out, [], GATHER) if lst else cost(out, [], 2.0))
 
-    def cp(o, i, ia=None, oa=None, more=(), e="v", bias=None, part=None):
+    def act(o, i, f, ia=None, oa=None, more=(), part=None, price=None, **k):
+        src, out = A(i) if ia is None else ia, A(o) if oa is None else oa
+        op("s", [i] + list(more), [o], lambda e: e.activation(out, src, f, **k), price or cost(out, [], 1.0), part)
+
+    def cp(o, i, ia=None, oa=None, more=(), e="v", bias=None, part=None, price=None):
         src, out = A(i) if ia is None else ia, A(o) if oa is None else oa
         if e == "v":
-            op("v", [i] + list(more), [o], lambda e: e.tensor_copy(out, src), part)
+            op("v", [i] + list(more), [o], lambda e: e.tensor_copy(out, src), price or cost(out, [o, i], None), part)
         elif bias is None:
-            op("s", [i] + list(more), [o], lambda e: e.activation(out, src, AF.Copy), part)
+            act(o, i, AF.Copy, ia, oa, more, part, price)
         else:
-            op("s", [i] + list(more), [o], lambda e: e.activation(out, src, AF.Identity, bias=bias))
+            act(o, i, AF.Identity, ia, oa, more, part, price, bias=bias)
 
     def gather(o, win, lst, e="v", bias=None):
-        cp(o, win, ia=A(win).indirect(A(lst)), more=[lst], e=e, bias=bias)
+        cp(o, win, ia=A(win).indirect(A(lst)), more=[lst], e=e, bias=bias, price=0.07 + cost(A(o), [], GATHER))
 
     def scatter(win, lst, i):
-        cp(win, i, oa=A(win).indirect(A(lst)), more=[lst, win])
+        cp(win, i, oa=A(win).indirect(A(lst)), more=[lst], price=0.055 + cost(A(i), [], SCATTER))
 
     def scan(o, d0, d1, init, o0, o1):
-        op("v", [d0, d1], [o], lambda e: e.tensor_tensor_scan(A(o), A(d0), A(d1), init, o0, o1))
+        op("v", [d0, d1], [o], lambda e: e.tensor_tensor_scan(A(o), A(d0), A(d1), init, o0, o1), cost(A(o), [o, d0, d1], None))
 
     def mm(o, l, r, start, stop, oa=None, la=None, ra=None):
-        op("p", [l, r], [o], lambda e: e.matmul(A(o) if oa is None else oa, A(l) if la is None else la, A(r) if ra is None else ra, start, stop))
+        out = A(o) if oa is None else oa
+        op("p", [l, r], [o], lambda e: e.matmul(out, A(l) if la is None else la, A(r) if ra is None else ra, start, stop), cost(out, [], 1.0) * PE / CYC)
 
     def iota(o, pattern, base, cm=0):
-        op("g", [], [o], lambda e: e.iota(A(o), pattern, base, cm, allow_small_or_imprecise_dtypes=True))
+        op("g", [], [o], lambda e: e.iota(A(o), pattern, base, cm, allow_small_or_imprecise_dtypes=True), 0.14 + 2 * CYC * (o[2] - o[1]))
 
     def memset(o, v):
-        op("v", [], [o], lambda e: e.memset(A(o), v))
+        op("v", [], [o], lambda e: e.memset(A(o), v), cost(A(o), [o], None))
 
     def ends(b, n=256):
         return T[b][:, 15:n:16]
 
+    queued = [1.8]
+
     def load(n, dst, lo, hi, src, a, b, after=None):
-        dma("y", "ld%d" % n, [], [(dst, lo, hi)], lambda e: e.dma_start(T[dst][:, lo:hi], T[src][:, a:b]), after)
+        queued[0] = (1.8 if after else queued[0]) + 0.2 + (hi - lo) * (2 if SCRATCH[dst][2] == B16 else 4) / 1750
+        dma("y", "ld%d" % n, [], [(dst, lo, hi)], lambda e: e.dma_start(T[dst][:, lo:hi], T[src][:, a:b]), queued[0], after)
     load(0, "EFT", 192, 448, "ef", 0, 256)
     load(1, "ZFT", 192, 448, "zf", 0, 256)
     load(2, "TAB", 0, 2048, "tab", 0, 2048)
     load(4, "EHT", 192, 448, "eh", 0, 256)
     load(3, "TAB", 2048, 4096, "tab", 2048, 4096)
     far = len(topo.engines(asker(0), core))
-    land("qu", far, "QE", 0, 256)
-    land("qu", far, "QZ", 0, 256)
-    land("rp", len(topo.engines(cores[seen(0)], core)), "RP", 0, 16)
+    land("qu", far, "QE", 0, 256, "qu", 2.0)
+    land("qu", far, "QZ", 0, 256, "qu", 2.0)
+    land("rp", len(topo.engines(cores[seen(0)], core)), "RP", 0, 16, "rp", 1.5)
     for t in range(1, 4):
-        n = len(topo.engines(cores[seen(t)], core))
-        land("sn%d" % t, sum(2 * len(topo.engines(h, core)) for h in helpers(topo, cores, seen(t))), "FT%d" % t, 0, 4096)
-        land("rz%d" % t, n, "RZ%d" % t, 0, 256)
-        land("rl%d" % t, n, "RL%d" % t, 0, 16)
+        a, n = 192 - 64 * t, len(topo.engines(cores[seen(t)], core))
+        land("qf%d" % t, len(topo.engines(asker(t), core)), "QF", a, a + 64, "qf%d" % t, HOP)
+        land("qf%d" % t, len(topo.engines(asker(t), core)), "QY", a, a + 64, "qf%d" % t, HOP)
+        land("rq%d" % t, n, "SF%d" % t, 0, 64, "rq%d" % t, HOP)
+        land("sn%d" % t, sum(2 * len(topo.engines(h, core)) for h in helpers(topo, cores, seen(t))), "FT%d" % t, 0, 4096, "h%d3" % t, 9.0)
+        land("rz%d" % t, n, "RZ%d" % t, 0, 256, "rz%d" % t, HOP)
+        land("rl%d" % t, n, "RL%d" % t, 0, 16, "rl%d" % t, HOP)
 
     z0 = ("ZFT", 192, 448)
     iota(("PJ", 0, 1), [[0, 1]], 0, 1)
@@ -250,82 +357,89 @@ def rank_program(g, core, T, topo):
     iota(("Q4", 0, 128), [[16, 8], [0, 16]], 0)
     iota(("KC", 0, 256), [[0, 16], [-256, 16]], 3968)
     iota(("JM", 0, 256), [[0, 16], [1, 16]], 0)
+    iota(("CI", 0, 48), [[16, 48]], 0)
     memset(("HF", 0, 1), 200.0)
     memset(("ST", 0, 1024), 0.0)
-    for k in range(4):
-        cp(("OCC", 1024 * k, 1024 * k + 1024), ("ST", 0, 1024), e="s", bias=-1.0)
-
-    def col(n, i, s1, o0, s2=None, o1=None):
-        ts(("PC", PCOL[n], PCOL[n] + 1), i, s1, o0, s2, o1)
+    for k in range(8):
+        cp(("OCC", 512 * k, 512 * k + 512), ("ST", 0, 512), e="s", bias=-1.0)
 
     def c(n):
         return ("PC", PCOL[n], PCOL[n] + 1)
+
+    def col(n, i, s1, o0, s2=None, o1=None):
+        ts(c(n), c(i), s1, o0, s2, o1, more=[c("M0")] if n in ("WP", "WD") else [])
     ts(("PJ", 1, 2), ("PJ", 0, 1), 15, OP.bitwise_and)
     ts(("PJ", 2, 3), ("PJ", 0, 1), 31, OP.bitwise_and)
     cp(c("P"), ("PJ", 0, 1))
     cp(c("I"), ("PJ", 1, 2))
     cp(c("P32"), ("PJ", 2, 3))
     tt(c("G"), c("P"), c("I"), OP.subtract)
-    col("M0", c("I"), 0.0, OP.is_equal)
-    col("M1", c("I"), 1.0, OP.is_equal)
-    col("EV", c("P32"), 16.0, OP.is_lt)
-    col("OD", c("P32"), 16.0, OP.is_ge)
-    cp(("EFO", 0, 256), ("EFT", 192, 448))
-    dst = cores[seen(0)]
-    rid, pid, _se = topo.addr(dst)
-    en = topo.engines(core, dst)
-    send("loc0", len(en), [("EFO", 0, 256), z0], lambda e: e.remote_dma_fused(
-        [RemoteDMATransfer(dst_ids=[DstId(rid=rid, pnc=pid)], dma_engine_mask=bits(m), remote_sem=T.sem["qu"], src=A(i), dst=A(o))
-         for (m, i, o) in ((en[:len(en) // 2], ("EFO", 0, 256), ("QE", 0, 256)), (en[len(en) // 2:], z0, ("QZ", 0, 256)))], local_sem=T.sem["loc0"]))
+    col("M0", "I", 0.0, OP.is_equal)
+    col("M1", "I", 1.0, OP.is_equal)
+    col("EV", "P32", 16.0, OP.is_lt)
+    col("OD", "P32", 16.0, OP.is_ge)
+    col("SG", "I", -400.0, OP.mult, -200.0, OP.add)
+    col("F0", "M0", 832.0, OP.mult)
+    col("F1", "M0", -192.0, OP.mult)
+    col("WP", "M1", -2048.0, OP.mult, P("M0"), OP.add)
+    col("WD", "M1", -128.0, OP.mult, P("M0"), OP.add)
+    col("N1", "I", 1.0, OP.not_equal)
+    col("LO", "M1", 127.0, OP.mult)
+    col("HI", "M1", -128.0, OP.mult, 256.0, OP.add)
     qx = ("QX", 16, 144)
-    ts(("NID", 0, 128), qx, P("P"), OP.is_equal, -1.0, OP.mult, more=[pc])
     ts(("PID", 0, 128), qx, P("P"), OP.is_equal, more=[pc])
-    ts(("EX", 0, 512), ("EXI", 0, 512), P("P32"), OP.is_equal, more=[pc])
+    ts(("NID", 0, 128), qx, P("P"), OP.is_equal, -1.0, OP.mult, more=[pc])
     ts(("XV", 0, 144), ("QX", 0, 144), P("G"), OP.is_equal, W1, OP.mult, more=[pc])
+    for n, f in (("BE", "EV"), ("BD", "OD")):
+        ts((n, 0, 160), ("QX", 0, 160), P("P"), OP.is_equal, P(f), OP.mult, more=[pc])
+    ts(("EX", 0, 512), ("EXI", 0, 512), P("P32"), OP.is_equal, more=[pc])
     ts(("BO", 0, 128), ("Q4", 0, 128), P("G"), OP.is_equal, more=[pc])
-    cp(("EHO", 0, 256), ("EHT", 192, 448))
-    iota(("CI", 0, 48), [[16, 48]], 0)
-    iota(("JR", 0, 192), [[1, 192]], 0)
+    ts(("BOH", 0, 128), ("Q4", 0, 128), P("G"), OP.is_equal, more=[pc])
+    act(("TU", 0, 128), ("JM", 0, 128), AF.Sigmoid, more=[pc], price=1.5, bias=P("SG"), scale=400.0)
+    ts(("SCM", 0, 256), ("JM", 0, 256), 0.5, OP.is_gt)
+    ts(("T2", 0, 128), ("JM", 0, 128), P("I"), OP.is_equal, more=[pc])
+    for k in range(16):
+        ts(("RO", 128 * k, 128 * k + 128), ("BOH", 0, 128), T.T2[:, k:k + 1], OP.mult, more=[("T2", 0, 128)])
+    ts(("PIH", 0, 128), qx, P("P"), OP.is_equal, more=[pc])
+    ts(("BO8", 0, 128), ("BO", 0, 128), BIG, OP.mult)
+    tt(("T1", 0, 128), ("TU", 0, 128), ("T2", 0, 128), OP.subtract)
+    ts(("CM", 0, 256), ("JM", 0, 256), P("I"), OP.not_equal, 131072.0, OP.mult, more=[pc])
+    tt(("TRI", 0, 128), ("T1", 0, 128), ("BO8", 0, 128), OP.mult)
+    memset(("RS", 0, 256), -20000.0)
+    ts(("RS", 0, 256), ("CI", 0, 16), P("I"), OP.add, LOOK - OFF, OP.add, oa=T.RS[:, 0:256:16], more=[pc])
+    ts(("AB", 0, 768), ("ST", 0, 768), P("N1"), OP.add, more=[pc])
+    ts(("DW", 0, 48), ("CI", 0, 48), P("I"), OP.add, 768.0 - 2047.0, OP.add, more=[pc])
+    memset(("DB", 0, 256), 0.0)
+    memset(("KD", 0, 256), -W1 / 2)
+    for n, f in (("X0", "M0"), ("XO", "M1"), ("XP", "WP"), ("XD", "WD")):
+        ts((n, 0, 144), ("QX", 0, 144), P("G"), OP.is_equal, P(f), OP.mult, more=[pc])
+    ts(("BO0", 0, 128), ("Q4", 0, 128), P("G"), OP.is_equal, P("M0"), OP.mult, more=[pc])
+    ts(("MB", 0, 192), ("JM", 0, 192), P("I"), OP.is_equal, 60000.0, OP.mult, more=[pc])
+
+    def ask(dst, e_from, e_to, z_from, z_to, rsem, lsem, dur):
+        rid, pid, _se = topo.addr(dst)
+        en = topo.engines(core, dst)
+        parts = ((en[:len(en) // 2], e_from, e_to), (en[len(en) // 2:], z_from, z_to))
+        send(lsem, len(en), [e_from, z_from], lambda e: e.remote_dma_fused(
+            [RemoteDMATransfer(dst_ids=[DstId(rid=rid, pnc=pid)], dma_engine_mask=bits(m), remote_sem=T.sem[rsem], src=A(i), dst=A(o)) for (m, i, o) in parts],
+            local_sem=T.sem[lsem]), rsem, dur)
+
+    def ask_fresh(t):
+        a = 192 - 64 * t
+        ask(cores[seen(t)], ("SEF", a, a + 64), ("QF", a, a + 64), ("ZFT", a, a + 64), ("QY", a, a + 64), "qf%d" % t, "loc7", 2.0)
+    cp(("EFO", 0, 256), ("EFT", 192, 448))
+    ask(cores[seen(0)], ("EFO", 0, 256), ("QE", 0, 256), z0, ("QZ", 0, 256), "qu", "loc0", 6.5)
+    for k, (o, i) in enumerate((("EFT", "ef"), ("ZFT", "zf"), ("EHT", "eh"))):
+        load(5 + k, o, 0, 192, i, 832, 1024, "loc0" if k == 0 else None)
+    for k, (o, i) in enumerate((("ZFT", "zf"), ("EHT", "eh"), ("EFT", "ef"))):
+        load(8 + k, o, 448, 1024, i, 256, 832)
     iota(("IOT", 0, 1024), [[1, 1024]], 0)
-
-    def constants_1():
-        for n, f in (("BE", "EV"), ("BD", "OD")):
-            ts((n, 0, 160), ("QX", 0, 160), P("P"), OP.is_equal, P(f), OP.mult, more=[pc])
-        ts(("SCM", 0, 256), ("JM", 0, 256), 0.5, OP.is_gt)
-        ts(("BOH", 0, 128), ("Q4", 0, 128), P("G"), OP.is_equal, more=[pc])
-        ts(("T2", 0, 128), ("JM", 0, 128), P("I"), OP.is_equal, more=[pc])
-        ts(("T1", 0, 128), ("JM", 0, 128), P("I"), OP.is_gt, more=[pc])
-        for k in range(16):
-            ts(("RO", 128 * k, 128 * k + 128), ("BOH", 0, 128), T.T2[:, k:k + 1], OP.mult, more=[("T2", 0, 128)])
-        ts(("PIH", 0, 128), qx, P("P"), OP.is_equal, more=[pc])
-        ts(("BO8", 0, 128), ("BO", 0, 128), BIG, OP.mult)
-        tt(("T1", 0, 128), ("T1", 0, 128), ("T2", 0, 128), OP.subtract)
-        ts(("CM", 0, 256), ("JM", 0, 256), P("I"), OP.not_equal, 131072.0, OP.mult, more=[pc])
-        tt(("TRI", 0, 128), ("T1", 0, 128), ("BO8", 0, 128), OP.mult)
-        memset(("RS", 0, 256), -20000.0)
-        ts(("RS", 0, 256), ("CI", 0, 16), P("I"), OP.add, 4096.0 - OFF, OP.add, oa=T.RS[:, 0:256:16], more=[pc, ("RS", 0, 256)])
-
-    def constants_2():
-        col("WP", c("M1"), -2048.0, OP.mult, P("M0"), OP.add)
-        col("WD", c("M1"), -128.0, OP.mult, P("M0"), OP.add)
-        col("N1", c("I"), 1.0, OP.not_equal)
-        col("F0", c("M0"), 832.0, OP.mult)
-        col("F1", c("M0"), -192.0, OP.mult)
-        col("LO", c("M1"), 127.0, OP.mult)
-        col("HI", c("M1"), -128.0, OP.mult, 256.0, OP.add)
-        for n, f in (("X0", "M0"), ("XO", "M1"), ("XP", "WP"), ("XD", "WD")):
-            ts((n, 0, 144), ("QX", 0, 144), P("G"), OP.is_equal, P(f), OP.mult, more=[pc])
-        ts(("BO0", 0, 128), ("Q4", 0, 128), P("G"), OP.is_equal, P("M0"), OP.mult, more=[pc])
-        ts(("MB", 0, 192), ("JM", 0, 192), P("I"), OP.is_equal, 60000.0, OP.mult, more=[pc])
-        ts(("AB", 0, 768), ("ST", 0, 768), P("N1"), OP.add, more=[pc])
-        ts(("DW", 0, 48), ("CI", 0, 48), P("I"), OP.add, 768.0 - 2047.0, OP.add, more=[pc])
-        memset(("DB", 0, 64), 0.0)
-
-    def constants_3():
-        ts(("FN", 0, 192), ("IOT", 0, 192), P("F0"), OP.add, more=[pc])
-        ts(("FN", 192, 1024), ("IOT", 192, 1024), P("F1"), OP.add, more=[pc])
-        cp(("SEH", 0, 192), ("EHT", 0, 192))
-        cp(("SEF", 0, 192), ("EFT", 0, 192))
+    iota(("JR", 0, 192), [[1, 192]], 0)
+    cp(("FN", 0, 192), ("IOT", 0, 192), e="s", bias=P("F0"), more=[pc])
+    for a in (192, 608):
+        cp(("FN", a, a + 416), ("IOT", a, a + 416), e="s", bias=P("F1"), more=[pc])
+    cp(("SEH", 0, 192), ("EHT", 0, 192))
+    cp(("SEF", 0, 192), ("EFT", 0, 192))
 
     def turn(o, z):
         n = z[2] - z[1]
@@ -334,95 +448,97 @@ def rank_program(g, core, T, topo):
 
     def expand(o, z, on_s):
         n = 16 * (z[2] - z[1])
+        batch(True)
         for k in range(16):
             cp((o, 0, n), z, oa=T[o][:, k:n:16], e="s" if k < on_s else "v", part=(o,) + z)
+        batch(False)
 
-    units = [0]
-    waiting = []
+    units, tab = [0], ("TAB", 0, 4096)
 
-    def s_unit(dst, m, win, lst, col0, zt, row):
+    def s_unit(dst, m, win, lst, col0, zt, row, n=2):
         u = units[0] % 2
         units[0] += 1
-        d, gb = ("D%d" % u, 0, 512), ("GB%d" % u, 0, 512)
-        mm(d, (zt, 0, 128), ("EX", 0, 512), True, False, la=T[zt][row:row + 32, :], ra=T.EX[row:row + 32, :])
-        gather(gb, (win, 0, 4096), (lst, col0, col0 + 32), e="s")
+        d, gb = ("D%d" % u, 0, 256 * n), ("GB%d" % u, 0, 256 * n)
+        mm(d, (zt, 0, 128), ("EX", 0, 512), True, False, la=T[zt][row:row + 16 * n, :], ra=T.EX[row:row + 16 * n, 0:256 * n])
+        gather(gb, win, (lst, col0, col0 + 16 * n), e="s")
         mm(d, ("NID", 0, 128), gb, False, True)
-        s_step()
-        waiting.append((dst, m, d[0]))
-
-    def s_step():
-        while waiting:
-            dst, m, d = waiting.pop()
-            for h in range(2):
-                op("s", [(d, 0, 512), ("HF", 0, 1)], [(dst, 256 * (m + h), 256 * (m + h) + 256)],
-                   lambda e: e.activation(T[dst][:, m + h, :], T[d][:, 256 * h:256 * h + 256], AF.Sigmoid, bias=T.HF[:, 0:1], scale=400.0))
+        batch(True)
+        for h in range(n):
+            act((dst, 256 * (m + h), 256 * (m + h) + 256), d, AF.Sigmoid, ia=T[d[0]][:, 256 * h:256 * h + 256], oa=T[dst][:, m + h, :],
+                more=[("HF", 0, 1)], bias=T.HF[:, 0:1], scale=400.0)
+        batch(False)
 
     def v_block(dst, m, win, lst, col0, zx, b):
-        l, x = (lst, col0, col0 + 16), (zx, 256 * b, 256 * b + 256)
-        tt((dst, 256 * m, 256 * m + 256), (win, 0, 4096), x, OP.is_le, ia=T[win][:, 0:4096].indirect(A(l)), more=[l], oa=T[dst][:, m, :])
+        tt((dst, 256 * m, 256 * m + 256), win, (zx, 256 * b, 256 * b + 256), OP.is_le, oa=T[dst][:, m, :], lst=(lst, col0, col0 + 16))
 
-    def key_open(key):
-        mm((key, 0, 256), ("BO", 0, 128), ("KC", 0, 256), True, False)
+    def key_open(key, a=0, b=256):
+        mm((key, a, b), ("BO", 0, 128), ("KC" if key == "KH" else "KD", a, b), True, False)
 
     def sums(key, src, m0, m1, last=False):
+        batch(True)
         for k in range(16):
             mm((key, 16 * m0, 16 * m1), ("XV", 0, 144), (src, 256 * m0, 256 * m1), False, last and k == 15,
                la=T.XV[:, 16 - k:144 - k], ra=T[src][:, m0:m1, 16 * k:16 * k + 16])
+        batch(False)
 
     def slots_in(parts):
         ep, tr = ("EP", 0, 256), ("TR", 0, 256)
+        batch(True)
         for (src, b0, b1, h) in parts:
-            ts(ep, src, -2048.0, OP.add, oa=T.EP[:, b0:b1, 16 * h:16 * h + 16], part=parts)
-        op("v", [ep], [tr], lambda e: e.transpose(T.TR[:, :, :], T.EP[:, :, :]))
+            ts(ep, src, -2048.0, OP.add, oa=T.EP[:, b0:b1, 16 * h:16 * h + 16])
+        batch(False)
+        op("v", [ep], [tr], lambda e: e.transpose(T.TR[:, :, :], T.EP[:, :, :]), 128 * CYC)
 
     def slots_mm():
+        batch(True)
         for (h2, h, l, a) in ((0, 0, "BE", 16), (0, 1, "BE", 0), (1, 1, "BD", 16), (1, 0, "BD", 32)):
             mm(("KH", 128 * h2, 128 * h2 + 128), (l, a, a + 128), ("TR", 0, 256), False, False, ra=T.TR[:, :, 16 * h:16 * h + 16])
+        batch(False)
 
-    def spread(src, start):
+    def spread(src, start, stop):
+        batch(True)
         for k in range(16):
-            mm(("PA", 0, 256), ("RO", 128 * k, 128 * k + 128), src, start, start or k == 15, oa=T.PA[:, k:256:16])
+            mm(("PA", 0, 256), ("RO", 128 * k, 128 * k + 128), src, start, start or (stop and k == 15), oa=T.PA[:, k:256:16])
+        batch(False)
 
-    def pick(x, src, n, stop=True):
+    def pick(x, src, n):
+        batch(True)
         for k in range(16):
-            mm(("PB", 0, n), (x, 16 - k, 144 - k), src, k == 0, stop and k == 15, ra=T[src[0]][:, src[1] + k:src[2]:16])
+            mm(("PB", 0, n), (x, 16 - k, 144 - k), src, k == 0, k == 15, ra=T[src[0]][:, src[1] + k:src[2]:16])
+        batch(False)
 
-    def slot_1(t):
+    def slot(t):
         scan(("SH", 0, 256), ("SCM", 0, 256), ("KH", 0, 256), 0.0, OP.mult, OP.max)
         cp(("IW", 0, 16), ("SH", 0, 256), ia=ends("SH"))
         ts(("IW", 16, 32), ("IW", 0, 16), 4095, OP.bitwise_and)
         ts(("WH", 0, 16), ("IW", 16, 32), -2048.0, OP.add)
-        if t:
-            cp(("SL", 0, 16), ("IW", 16, 32))
-        ts(w("SW"), ("IW", 16, 32), -2048.0, OP.add)
-        spread(("WH", 0, 16), True)
-
-    def slot_2():
-        cp(("SR", 0, 256), ("PA", 0, 256))
+        ts(w("HG"), ("SH", 0, 256), 9 * W1, OP.is_ge, 2 * BIG, OP.mult, ia=ends("SH"))
+        tt(w("SW"), ("WH", 0, 16), w("HG"), OP.add)
+        ts(("IW", 32, 48), ("IW", 0, 16), 16, OP.arith_shift_right)
+        tt(w("HN"), ("IW", 32, 48), w("HG"), OP.min)
+        spread(("WH", 0, 16), True, True)
+        cp(("SR", 0, 256), ("PA", 0, 256), e=ON["SR"])
         mm(("CN", 0, 256), ("PID", 0, 128), ("CM", 0, 256), True, False)
         mm(("CN", 0, 256), ("PIH", 0, 128), ("SR", 0, 256), False, False)
-
-    def owner_1():
-        gather(("OG", 0, 256), ("OCC", 0, 4096), ("SL", 0, 16))
-
-    def owner_2():
+        mm(("PA", 0, 256), ("PID", 0, 128), ("DB", 0, 256), True, False)
+        if t == 0:
+            return
+        cp(("SL", 0, 16), ("IW", 16, 32))
+        gather(("OG", 0, 256), ("OCC", 0, 4096), ("SL", 0, 16), e=ON["OG"])
         pick("XO", ("OG", 0, 256), 16)
         cp(("BL", 0, 16), ("PB", 0, 16))
         ts(w("OC"), ("PB", 0, 16), 0.0, OP.is_ge)
         tt(w("Y0"), ("PB", 0, 16), w("FW"), OP.subtract)
         tt(w("Y"), w("Y0"), w("OC"), OP.mult)
-
-    def owner_3():
         gather(("DB", 256, 512), ("ST", 0, 1024), ("BL", 0, 16), e="s", bias=-127.0)
         pick("X0", ("DB", 0, 512), 32)
-
-    def owner_4():
         ts(w("X0"), ("PB", 0, 16), 128.0, OP.add)
         tt(w("X1"), ("PB", 16, 32), w("X0"), OP.subtract)
-        tt(w("X0"), w("X1"), w("OC"), OP.mult)
-        ts(w("X"), w("X0"), 128.0, OP.add)
+        tt(w("X2"), w("X1"), w("OC"), OP.mult)
+        ts(w("X"), w("X2"), 128.0, OP.add)
 
     def mark(t):
+        cp(("PM", 0, 192), ("DB", 64, 256), e="s", bias=128.0)
         memset(("ST", 192 - 64 * t, 256 - 64 * t), 128.0)
         scatter(("ST", 0, 1024), ("FL", 0, 12), ("PM", 0, 192))
 
@@ -432,235 +548,172 @@ def rank_program(g, core, T, topo):
     def claims(t):
         wl = ("WL%d" % t, 0, 16)
         if t:
-            scan(("SF", 0, 256), ("SCM", 0, 256), ("KF", 0, 256), 0.0, OP.mult, OP.max)
-            tt(w("WM"), ("SH", 0, 256), ("SF", 0, 256), OP.max, ia=ends("SH"), ib=ends("SF"))
+            sf, far = ("SF%d" % t, 0, 256), ends("SF%d" % t)
+            scan((sf[0], 64, 256), ("SCM", 64, 256), ("KF", 64, 256), 0.0, OP.mult, OP.max)
         else:
-            tt(w("WM"), ("SH", 0, 256), ("RP", 0, 16), OP.max, ia=ends("SH"))
-        ts(w("NG"), w("WM"), 9 * W1, OP.is_ge, BIG, OP.mult)
-        cp(("IW", 32, 48), w("WM"))
+            sf, far = ("RP", 0, 16), T.RP[:, :]
         for m in range(16):
-            n = 256 - 16 * m
-            ts(("EE", 256 * m, 256 * m + n), ("SR", 16 * m, 256), A(w("SW", m, m + 1)), OP.subtract, A(w("NG", m, m + 1)), OP.is_equal,
-               oa=T.EE[:, m, 0:n], more=[w("SW"), w("NG")])
+            n, x = 256 - 16 * m, 16 * m + 15 if t else m
+            ts(("EE", 256 * m, 256 * m + n), ("SR", 16 * m, 256), A(w("SW", m, m + 1)), OP.subtract, T[sf[0]][:, x:x + 1], OP.is_equal,
+               oa=T.EE[:, m, 0:n], more=[w("SW"), (sf[0], x, x + 1)])
             if m < 15:
                 mm(("CN", 16 * m + 16, 256), ("BO8", 0, 128), ("EE", 256 * m, 256 * m + n), False, False, ra=T.EE[:, m, 16:n])
             if m % 4 == 3:
                 mm(("CN", 16 * m - 48, 16 * m + 16), ("TRI", 0, 128), ("EE", 256 * m - 768, 256 * m + 256), False, m == 15, ra=T.EE[:, m - 3:m + 1, 0:16])
-        ts(("IW", 48, 64), ("IW", 32, 48), 16, OP.arith_shift_right)
-        if t:
-            owner_4()
-            mm(("PA", 0, 256), ("PID", 0, 128), ("DB", 0, 256), True, False)
-        tt(w("WN"), ("IW", 48, 64), w("NG"), OP.min)
+        ts(w("FA"), sf, 1 / W1, OP.mult, 8.0, OP.add, ia=far)
+        tt(w("FC"), w("FA"), sf, OP.min, ib=far)
+        tt(("WH", 32, 48), w("FC"), w("HN"), OP.max)
+        spread(("WH", 32, 48), False, False)
         cs = ("CS", 0, 256)
         scan(cs, ("RS", 0, 256), ("CN", 0, 256), -20000.0, OP.max, OP.min)
+        ts(wl, cs, OFF, OP.add, ia=ends("CS"))
         if t:
             ts(w("WIN"), cs, 4096.0 - OFF, OP.is_lt, ia=ends("CS"))
-            ts(wl, cs, OFF, OP.add, ia=ends("CS"))
-            tt(w("T1"), w("WIN"), w("X"), OP.mult)
+            tt(("WH", 16, 32), w("WIN"), w("X"), OP.mult)
             tt(w("T2"), w("WIN"), w("Y"), OP.mult)
+            tt(w("TF"), w("T2"), w("FW"), OP.add)
+            cp(("TL", 0, 16), w("TF"))
         else:
-            ts(w("T1"), cs, 4096.0 - OFF, OP.is_lt, 128.0, OP.mult, ia=ends("CS"))
-            ts(wl, cs, OFF, OP.add, ia=ends("CS"))
-        tt(("WH", 16, 32), w("T1"), w("WN"), OP.add)
-        spread(("WH", 16, 32), t == 0)
+            ts(("WH", 16, 32), cs, 4096.0 - OFF, OP.is_lt, 128.0, OP.mult, ia=ends("CS"))
+        spread(("WH", 16, 32), False, True)
         if t < 3:
             put(("RL%d" % (t + 1), 0, 16), wl, asker(t + 1), "rl%d" % (t + 1), "loc%d" % (8 + t))
-        if t:
-            tt(w("TF"), w("T2"), w("FW"), OP.add)
         scatter(("TAB", 0, WT), wl, lanes(t))
+        if t < 3:
+            cp(("TAB", 4096, LOOK), ("TAB", 0, LOOK - 4096))
         if t < 2:
             snapshot(t + 2)
         if t:
-            cp(("TL", 0, 16), w("TF"))
             cp(("STN", 0, 256), ("PA", 0, 256), e="s")
             scatter(("ST", 0, 1024), ("TL", 0, 16), ("STN", 0, 256))
         else:
             cp(("ST", 192, 448), ("PA", 0, 256), e="s")
+        scatter(("OCC", 0, WT), wl, ("FR%d" % t, 0, 256) if t else ("FN", 192, 448))
 
-    def occ(t):
-        scatter(("OCC", 0, WT), ("WL%d" % t, 0, 16), ("FR%d" % t, 0, 256) if t else ("FN", 192, 448))
-
-    def fresh_1(t):
+    def fresh(t):
         a = 192 - 64 * t
+        turn("ZTG", ("QY", a, a + 64))
         turn("ZTF", ("ZFT", a, a + 64))
         cp(("ZL%d" % t, 0, 64), ("ZFT", a, a + 64), e="s")
         cp(("FR%d" % t, 0, 64), ("FN", a, a + 64), e="s")
-
-    def fresh_2(t, dst, win, lst, u):
-        s_unit(dst, 2 * u, win, lst, 192 - 64 * t + 32 * u, "ZTF", 32 * u)
+        for (dst, lst, zt) in (("CF", "QF", "ZTG"), ("CH", "SEH", "ZTF")):
+            for u in range(2):
+                s_unit(dst, 2 * u, tab, lst, a + 32 * u, zt, 32 * u)
+        key_open("KF", 0, 64)
+        sums("KF", "CF", 0, 4, True)
+        key_open("KH")
+        sums("KH", "CH", 0, 4)
 
     def select(t):
         U, lo, n = 256 * t, 256 - 64 * t, 16 * t
-        ft, fl = "FT%d" % t, ("FL", 0, 12)
-        key_open("KH")
-        fresh_2(t, "CH", "TAB", "SEH", 0)
-        fresh_2(t, "CH", "TAB", "SEH", 1)
         ts(("FB", 0, U), ("ST", lo, lo + U), 128.0, OP.is_lt)
         scan(("VB", 0, U), ("AB", 0, U), ("FB", 0, U), 0.0, OP.mult, OP.add)
-        mm(("PB", 48, 49), ("BO0", 0, 128), ("VB", U - 1, U), True, True)
+        mm(("PA", 0, 1), ("BO0", 0, 128), ("VB", U - 1, U), True, True)
         pick("XP", ("VB", 0, U), n)
-        scatter((ft, 0, WT), ("RL%d" % t, 0, 16), ("RZ%d" % t, 0, 256))
-        key_open("KF")
-        fresh_2(t, "CF", ft, "SEF", 0)
+        ts(("LW", 0, 192), ("JR", 0, 192), T.PA[:, 0:1], OP.subtract, float(lo + U), OP.add, more=[("PA", 0, 1)])
         tt(("LF", 0, n), ("PB", 0, n), ("DW", 0, n), OP.min)
-        ts(("LW", 0, 192), ("JR", 0, 192), T.PB[:, 48:49], OP.subtract, float(lo + U), OP.add, more=[("PB", 48, 49)])
         ts(("LU", 0, n), ("LF", 0, n), 2047.0, OP.add)
         scatter(("LW", 0, 1536), ("LU", 0, n), ("IOT", lo, lo + U))
-        sums("KH", "CH", 0, 4)
-        fresh_2(t, "CF", ft, "SEF", 1)
-        s_step()
-        sums("KF", "CF", 0, 4)
         scan(("WS", 0, 192), ("MB", 0, 192), ("LW", 0, 192), 0.0, OP.max, OP.min)
-        cp(fl, ("WS", 0, 192), ia=ends("WS", 192))
+        cp(("FL", 0, 12), ("WS", 0, 192), ia=ends("WS", 192))
 
-    def entries(tab, a, b, o):
-        fl = ("FL", 0, 12)
-        tt((a, 0, 192), (tab, 0, 1024), ("DB", 64, 256), OP.add, ia=T[tab][:, :].indirect(A(fl)), more=[fl])
-        ts((b, 0, 192), (a, 0, 192), 4095, OP.bitwise_and)
-        cp((o, 0, 192), (b, 0, 192))
+    def entries(tab, a, o):
+        tt((a, 0, 192), (tab, 0, 1024), ("DB", 64, 256), OP.add, lst=("FL", 0, 12))
+        cp((o, 0, 192), (a, 0, 192))
+
+    def blocks(dst, key, first, split, win, lst, col0, zt, zx, zx0):
+        for m in range(first, split, 2):
+            s_unit(dst, m, win, lst, 16 * (m - col0), *zt(m), min(2, split - m))
+        for m in range(15, split - 1, -1):
+            v_block(dst, m, win, lst, 16 * (m - col0), zx, m - zx0)
+        low, high = first, 16
+        while high - low > 4:
+            if split - low >= high - split:
+                sums(key, dst, low, low + 4)
+                low += 4
+            else:
+                sums(key, dst, high - 4, high)
+                high -= 4
+        sums(key, dst, low, high, True)
 
     def penalties(t):
         ft, fl, zl, a = "FT%d" % t, ("FL", 0, 12), "ZL%d" % t, 192 - 64 * t
-        gather(("DB", 64, 256), ("ST", 0, 1024), fl)
+        gather(("DB", 64, 256), ("ST", 0, 1024), fl, e=ON["DL"])
         gather((zl, 64, 256), ("ZFT", 0, 1024), fl, e="s")
         if t < 3:
             put(("RZ%d" % (t + 1), 0, 256), (zl, 0, 256), asker(t + 1), "rz%d" % (t + 1), "loc%d" % (4 + t))
-        entries("EHT", "EI", "EM", "EHO")
-        turn("ZT", (zl, 64, 192))
-        expand("ZX", (zl, 128, 256), 8)
-
-        def vh(m):
-            v_block("CH", m, "TAB", "EHO", 16 * m - 64, "ZX", m - 8)
-
-        def vf(m):
-            v_block("CF", m, ft, "EFO", 16 * m - 64, "ZX", m - 8)
-
-        def sh(m):
-            s_unit("CH", m, "TAB", "EHO", 16 * m - 64, "ZT", 16 * m - 64)
-
-        def sf(m):
-            s_unit("CF", m, ft, "EFO", 16 * m - 64, "ZT", 16 * m - 64)
-        sh(4)
-        vh(15)
-        vh(14)
-        sh(6)
-        entries("EFT", "FI", "FM", "EFO")
-        vh(13)
-        vh(12)
-        sums("KH", "CH", 12, 16)
-        sf(4)
+        scan(("SQ", 0, 64), ("SCM", 0, 64), ("KF", 0, 64), 0.0, OP.mult, OP.max)
+        put(("SF%d" % t, 0, 64), ("SQ", 0, 64), asker(t), "rq%d" % t, "loc%d" % (11 + t))
+        entries("EHT", "EI", "EHO")
+        entries("EFT", "FI", "EFO")
+        ts(("EM", 0, 192), ("EI", 0, 192), 4095, OP.bitwise_and)
+        expand("ZX", (zl, 16 * min(SPLIT), 256), ZS)
+        turn("ZT", (zl, 64, min(192, 16 * max(SPLIT))))
+        if max(SPLIT) > 12:
+            turn("ZU", (zl, 192, 16 * max(SPLIT)))
+        key_open("KF", 64, 256)
+        scatter((ft, 0, WT), ("RL%d" % t, 0, 16), ("RZ%d" % t, 0, 256))
+        cp((ft, 4096, LOOK), (ft, 0, LOOK - 4096))
         slots_in(((("EHT", a, a + 64), 0, 4, 0), (("EM", 0, 64), 4, 8, 0), (("EM", 64, 192), 0, 8, 1)))
-        sums("KH", "CH", 4, 8)
         slots_mm()
-        for m in (11, 10, 9, 8):
-            vh(m)
-        sf(6)
-        sums("KH", "CH", 8, 12, True)
-        occ(t - 1)
-        sf(8)
-        slot_1(t)
+
+        def zt(m):
+            return ("ZT", 16 * m - 64) if m < 12 else ("ZU", 16 * m - 192)
+        blocks("CH", "KH", 4, SPLIT[0], ("TAB", 0, LOOK), "EHO", 4, zt, "ZX", min(SPLIT))
+        blocks("CF", "KF", 4, SPLIT[1], (ft, 0, LOOK), "EFO", 4, zt, "ZX", min(SPLIT))
         cp(w("FW", 4, 16), ("WS", 0, 192), ia=ends("WS", 192))
         ts(w("FW", 0, 4), ("CI", 0, 4), P("I"), OP.add, float(a), OP.add, more=[pc])
-        owner_1()
-        sums("KF", "CF", 4, 8)
-        sf(10)
-        vf(15)
-        slot_2()
-        vf(14)
-        owner_2()
-        s_step()
-        vf(13)
-        vf(12)
-        sums("KF", "CF", 8, 10)
-        sums("KF", "CF", 14, 16)
-        sums("KF", "CF", 10, 14, True)
         gather(("FR%d" % t, 64, 256), ("FN", 0, 1024), fl, e="s")
-        owner_3()
+        slot(t)
         if t < 3:
-            cp(("PM", 0, 192), ("DB", 64, 256), e="s", bias=128.0)
             mark(t)
-            fresh_1(t + 1)
 
     def penalties_0():
-        turn("ZT", ("ZFT", 192, 320))
-        expand("ZX", ("ZFT", 320, 448), 0)
-        constants_1()
+        h, f = SPLIT0
+        turn("ZT", ("ZFT", 192, 192 + 16 * h))
+        expand("ZX", ("ZFT", 192 + 16 * h, 448), 16)
+        cp(("EHO", 0, 256), ("EHT", 192, 448))
         slots_in(((("EHT", 192, 320), 0, 8, 0), (("EHT", 320, 448), 0, 8, 1)))
-        snapshot(1)
-        put(("RZ1", 0, 256), z0, asker(1), "rz1", "loc4")
-        for k, (o, i) in enumerate((("EHT", "eh"), ("ZFT", "zf"), ("EFT", "ef"))):
-            load(5 + k, o, 0, 192, i, 832, 1024, "loc1" if k == 0 else None)
-
-        def vh(m):
-            v_block("CH", m, "TAB", "EHO", 16 * m, "ZX", m - 8)
-
-        def vf(m):
-            v_block("CF", m, "TAB", "QE", 16 * m, "ZXQ", m - 6)
-
-        def sh(m):
-            s_unit("CH", m, "TAB", "EHO", 16 * m, "ZT", 16 * m)
-
-        def sf(m):
-            s_unit("CF", m, "TAB", "QE", 16 * m, "ZTQ", 16 * m)
+        snapshot(1, (0, 2))
+        ask_fresh(1)
         key_open("KH")
         key_open("KF")
         slots_mm()
-        sh(0)
-        sh(2)
-        for m in (15, 14, 13, 12):
-            vh(m)
-        sums("KH", "CH", 12, 16)
-        turn("ZTQ", ("QZ", 0, 96))
-        expand("ZXQ", ("QZ", 96, 256), 0)
-        sf(0)
+        turn("ZTQ", ("QZ", 0, 16 * f))
+        expand("ZXQ", ("QZ", 16 * f, 256), 0)
+        for m in range(0, 4, 2):
+            s_unit("CH", m, tab, "EHO", 16 * m, "ZT", 16 * m)
         sums("KH", "CH", 0, 4)
-        for m in (15, 14, 13, 12):
-            vf(m)
-        sf(2)
-        sums("KF", "CF", 12, 16)
-        sf(4)
-        for m in (11, 10, 9, 8):
-            vf(m)
-        sums("KF", "CF", 0, 4)
-        sums("KF", "CF", 8, 12)
-        sh(4)
-        vf(7)
-        vf(6)
-        sums("KF", "CF", 4, 8, True)
-        sh(6)
-        vh(11)
-        vh(10)
+        blocks("CF", "KF", 0, f, tab, "QE", 0, lambda m: ("ZTQ", 16 * m), "ZXQ", f)
+        blocks("CH", "KH", 4, h, tab, "EHO", 0, lambda m: ("ZT", 16 * m), "ZX", h)
         scan(("SF", 0, 256), ("SCM", 0, 256), ("KF", 0, 256), 0.0, OP.mult, OP.max)
         cp(("SP", 0, 16), ("SF", 0, 256), ia=ends("SF"))
         put(("RP", 0, 16), ("SP", 0, 16), asker(0), "rp", "loc11")
-        for k, (o, i) in enumerate((("EHT", "eh"), ("ZFT", "zf"), ("EFT", "ef"))):
-            load(8 + k, o, 448, 1024, i, 256, 832, "loc11" if k == 0 else None)
-        s_step()
-        vh(9)
-        vh(8)
-        sums("KH", "CH", 10, 12)
-        sums("KH", "CH", 4, 10, True)
-        constants_2()
-        slot_1(0)
-        constants_3()
-        slot_2()
-        fresh_1(1)
+        snapshot(1, (1, 3), "loc15")
+        put(("RZ1", 0, 256), z0, asker(1), "rz1", "loc4")
+        ask_fresh(2)
+        ask_fresh(3)
+        slot(0)
 
     penalties_0()
     for t in range(4):
         if t:
+            fresh(t)
             select(t)
             penalties(t)
         claims(t)
+    def store(e, n, o, oa, i, ia, dur):
+        dma(e, "out%d" % n, [i], [o], lambda q: q.dma_start(oa, ia), dur)
     for h in range(2):
-        x = (2048 * h, 2048 * h + 2048)
-        dma("y", "out%d" % h, [("TAB", x[0], x[1])], [("yt", x[0], x[1])], lambda e: e.dma_start(T.yt[:, x[0]:x[1]], T.TAB[:, x[0]:x[1]]))
+        a, b = 2048 * h, 2048 * h + 2048
+        store("y", h, ("yt", a, b), T.yt[:, a:b], ("TAB", a, b), T.TAB[:, a:b], 4.2 + 2.4 * h)
     ts(("YA", 0, 1024), ("ST", 0, 1024), P("LO"), OP.max, P("HI"), OP.min, more=[pc])
+    batch(True)
     for k in range(16):
         a = (64 * k + 192) % 1024
         mm(("PB", 0, 64), ("XD", 16 - k, 144 - k), ("YA", a, a + 64), k == 0, k == 15)
-    occ(3)
-    dma("y", "out2", [("OCC", 0, 4096)], [("yo", 0, 4096)], lambda e: e.dma_start(T.yo[:, :], T.OCC[0:128:16, 0:4096]))
+    batch(False)
+    store("y", 2, ("yo", 0, 4096), T.yo[:, :], ("OCC", 0, 4096), T.OCC[0:128:16, 0:4096], 2.5)
     cp(("YD", 0, 64), ("PB", 0, 64), e="s", bias=16256.0)
-    dma("s", "out3", [("YD", 0, 64)], [("yd", 0, 1024)], lambda e: e.dma_start(T.yd[:, :], T.YD[:, :]))
+    store("s", 3, ("yd", 0, 1024), T.yd[:, :], ("YD", 0, 64), T.YD[:, :], 2.0)
     finish()

@@ -1,3 +1,4 @@
+import numpy as np
 from concourse.mybir import AluOpType, ActivationFunctionType
 from concourse.bass import DstId, RemoteDMATransfer
 
@@ -8,22 +9,27 @@ BIG = 8192.0
 OFF = 2048.0 + BIG
 LOOK = 4096 + 64
 WT = LOOK + 256
-ON = {"SR": "s", "OG": "s", "DL": "s"}
-SPLIT0, SPLIT = (7, 7), (8, 11)
-ZS = 9
-CYC, PE, GATHER, SCATTER, WAKE, WAKE_SAME, FILL, HOP = 0.00085, 0.00035, 1.56, 3.8, 0.17, 0.17, 0.5, 5.0
-ROUNDS, ORDER = 4, []
+ON = {"SR": "s", "DL": "sss", "ZL": "sss", "BL": "s", "WL": "v", "TL": "v", "FW": "s", "FT": "s"}
+FINE = 1 / 8192
+EARLY = 3
+SPLIT0, SPLIT = (7, 7), (9, 9)
+ZS, ZQ = 7, 4
+CYC, PE, GATHER, SCATTER, WAKE, WAKE_SAME, FILL, HOP = 0.00085, 0.00035, 1.56, 3.8, 0.18, 0.2, 1.0, 5.0
+FIX, LEAST, SFIX, RATE = 0.0, 64, 0.03, 2200
+CASES = ((0.15, 0.3, -0.03, 0.0, 1.0, 1.0), (0.15, 0.15, 0.035, 0.0, 0.75, 1.0), (0.2, 0.2, 0.0, 1.0, 1.0, 0.7), (0.2, 0.2, 0.0, 0.4, 1.4, 0.8))
+LIST, SEARCH, PIECES = 5.0, 2, (1, 3)
+ROUNDS, TRIES, SWAPS, HEAT, ORDER = 4, 200, 4000, 0.12, []
 SB = "sbuf"
 F32, B16, F16, I32, U16 = "float32", "bfloat16", "float16", "int32", "uint16"
 SCRATCH = {}
 for _names, _w, _d in (
         ("TAB FT1 FT2 FT3", WT, B16), ("OCC", WT, F32), ("ST ZFT YA", 1024, B16), ("EHT EFT", 1024, I32), ("IOT FN", 1024, F32),
-        ("PJ", 4, I32), ("PC", 16, F32), ("CI", 48, F32), ("QX", 160, F32), ("Q4 T1 T2", 128, F32), ("JM RS SCM SH SF CS FR1 FR2 FR3", 256, F32),
-        ("JR MB WS", 192, F32), ("DW", 48, F32), ("HF", 8, F32), ("EX EXI GB0 GB1 DB", 512, B16), ("KC KD CM STN QZ PM", 256, B16),
-        ("XV X0 XD", 144, B16), ("XP XO", 144, F16), ("BE BD", 160, F16), ("BO BO8 TRI NID PID ZT ZU ZTF ZTQ", 128, B16), ("BO0 PIH BOH", 128, F16),
-        ("RO", 2048, F16), ("ZX ZXQ", 2560, B16), ("SR OG", 256, F16), ("AB FB VB", 768, F16), ("LW", 1536, F32),
-        ("EHO EFO QE", 256, U16), ("SEH SEF", 192, U16), ("EI EM FI", 192, I32), ("IW", 64, I32), ("WF", 256, F32), ("WH", 48, F16),
-        ("RP SP", 16, F32), ("LF", 48, F32), ("LU", 48, U16), ("SL BL TL FL", 16, U16), ("YD", 64, F32),
+        ("PJ", 4, I32), ("PC", 24, F32), ("CI", 48, F32), ("QX", 160, F32), ("Q4 T1 T2", 128, F32), ("JM RS SCM SH SF CS FR1 FR2 FR3", 256, F32),
+        ("MB WS", 192, F32), ("JR", 192, B16), ("DW", 48, F32), ("HF", 8, F32), ("EX EXI GB0 GB1 DB", 512, B16), ("KC KD CM STN QZ PM", 256, B16),
+        ("XV X0 XN XD", 144, B16), ("NIH", 128, F16), ("FW", 16, F16), ("XP XO", 144, F16), ("BE BD", 160, F16), ("BO BO8 TRI NID PID ZT ZTF ZTQ", 128, B16), ("BO0 PIH BOH", 128, F16),
+        ("RO", 2048, F16), ("ZX ZXQ", 2560, B16), ("SR OG", 256, F16), ("AB FB VB", 1024, F16), ("LW", 1536, F32),
+        ("EHO EFO QE", 256, U16), ("SEH SEF", 192, U16), ("EI EM FI", 192, I32), ("IW", 64, I32), ("WF", 256, F32), ("WH", 64, F16),
+        ("RP SP", 16, F32), ("LF", 64, F32), ("LU", 48, U16), ("SL BL TL FL", 16, U16), ("YD", 64, F32),
         ("SF1 SF2 SF3", 256, F32), ("SQ", 64, F32), ("QF", 192, U16), ("QY", 192, B16), ("ZTG TU", 128, B16),
         ("ZL1 ZL2 ZL3 RZ1 RZ2 RZ3", 256, B16), ("WL0 WL1 WL2 WL3 RL1 RL2 RL3", 16, U16)):
     for _n in _names.split():
@@ -35,10 +41,10 @@ for _n in ("EP", "TR"):
 for _n in ("KH", "KF", "D0", "D1", "ZP", "PA", "PB", "CN"):
     SCRATCH[_n] = ("psum", [128, 512], F32)
 SEMAPHORES = ["cv", "cs", "cp", "cg", "qu", "rp", "hl"] + ["ld%d" % _i for _i in range(12)] + ["loc%d" % _i for _i in range(16)]
-SEMAPHORES += ["%s%d" % (_s, _t) for _s in ("sn", "qf", "rq", "rz", "rl") for _t in range(1, 4)] + ["out%d" % _i for _i in range(4)]
+SEMAPHORES += ["%s%d" % (_s, _t) for _s in ("sn", "qf", "rq", "rz", "rl") for _t in range(1, 4)] + ["out%d" % _i for _i in range(5)]
 SEMAPHORES += ["h%d%d" % (_t, _q) for _t in range(1, 4) for _q in range(4)]
 WIDX = {n: 16 * i for i, n in enumerate("SW HG HN FA FC WIN T2 OC X0 X1 X Y0 Y FW TF X2".split())}
-PCOL = {n: i for i, n in enumerate("I P G P32 M0 M1 EV OD WP WD N1 F0 F1 LO HI SG".split())}
+PCOL = {n: i for i, n in enumerate("I P G P32 M0 M1 EV OD WP WD N1 F0 F1 LO HI SG MN".split())}
 
 
 def make(g, T):
@@ -50,7 +56,7 @@ def make(g, T):
         return b in SCRATCH and SCRATCH[b][0] == "psum"
 
     def add(e, own, reads, writes, fns, hold, dur, s=None, part=None):
-        me = {"id": len(nodes), "e": e, "own": own, "fns": fns, "hold": hold, "dur": dur, "s": s, "part": part, "pre": {}}
+        me = {"id": len(nodes), "e": e, "own": own, "fns": fns, "hold": hold, "dur": dur, "s": s, "part": part, "pre": {}, "more": 0.0, "name": writes[0][0] if writes else s}
         nodes.append(me)
         link(me, reads, writes)
         if e in "gy":
@@ -80,15 +86,18 @@ def make(g, T):
 
     def op(e, reads, writes, fn, cost, part=None):
         b = open_batch[0]
+        cost, more = cost if isinstance(cost, tuple) else (cost, 0.4 * cost)
         if b is not None and e in b:
-            b[e]["fns"].append(fn)
-            b[e]["hold"] += cost
-            b[e]["dur"] += cost
-            link(b[e], reads, writes)
+            me = b[e]
+            me["fns"].append(fn)
+            me["hold"] += cost
+            me["dur"] += cost
+            link(me, reads, writes)
         else:
             me = add(e, e, reads, writes, [fn], cost, cost, sem[e], part)
             if b is not None:
                 b[e] = me
+        me["more"] += more
 
     def batch(on):
         open_batch[0] = {} if on else None
@@ -162,13 +171,80 @@ def make(g, T):
                         cand[y["e"]].append(y)
             return out, [start[x["id"]] + x["hold"] for x in nodes], max(start[x["id"]] + x["dur"] for x in nodes)
         if not ORDER:
-            way, best = [float(x["id"]) for x in nodes], None
-            for _ in range(ROUNDS):
-                way = run(way, True)[1]
-                out, way, end = run(way, False)
-                if best is None or end < best[0]:
-                    best = (end, [x["id"] for x in out])
-            ORDER.extend(best[1])
+            cases = []
+            for (wake, same, call, slow, link_time, weight) in CASES:
+                hold = [x["hold"] + slow * x["more"] + (call * len(x["fns"]) if x["own"] == "s" else 0.0) for x in nodes]
+                dur = [h if x["own"] == x["e"] else x["dur"] * link_time for x, h in zip(nodes, hold)]
+                edge = [[(k, dur[k] if x["e"] == "n" else dur[k] + (same if nodes[k]["e"] == x["e"] else wake) if wait else hold[k])
+                         for k, wait in x["pre"].items()] for x in nodes]
+                cases.append((hold, dur, edge, weight))
+
+            def others(out):
+                mark = 0.0
+                for (hold, dur, edge, weight) in cases:
+                    free, start, end = {e: 0.0 for e in "vspgyn"}, [0.0] * len(nodes), 0.0
+                    for x in out:
+                        j = x["id"]
+                        at = free[x["e"]]
+                        for k, d in edge[j]:
+                            if start[k] + d > at:
+                                at = start[k] + d
+                        start[j], free[x["e"]] = at, at + hold[j]
+                        end = max(end, at + dur[j])
+                    mark += weight * end
+                return mark
+            ends, best, rng = [float(x["id"]) for x in nodes], None, np.random.RandomState(1)
+            for n in range(ROUNDS + TRIES):
+                if n < ROUNDS:
+                    way = run(ends, True)[1]
+                else:
+                    a, size = rng.uniform(-3.0, best[4]), rng.choice([0.15, 0.4, 1.0])
+                    way = [v + size * float(rng.randn()) if a < e < a + 6.0 else v for v, e in zip(best[2], best[3])]
+                out, ends, end = run(way, False)
+                mark = end + others(out)
+                if best is None or mark <= best[0]:
+                    best = (mark, [x["id"] for x in out], way, ends, end)
+            cases.append(([x["hold"] for x in nodes], [x["dur"] for x in nodes], [[(k, step(nodes[k], x)) for k in x["pre"]] for x in nodes], 1.0))
+
+            def queued(out, case):
+                hold, dur, edge, _w = case
+                lastq, start, why = {}, [0.0] * len(nodes), {}
+                for x in out:
+                    j, q = x["id"], lastq.get(x["e"])
+                    at, by = (start[q] + hold[q], (q, True)) if q is not None else (0.0, None)
+                    for k, d in edge[j]:
+                        if start[k] + d >= at:
+                            at, by = start[k] + d, (k, False)
+                    start[j], why[j], lastq[x["e"]] = at, by, j
+                j, pairs = max(range(len(nodes)), key=lambda k: start[k] + dur[k]), []
+                while why[j]:
+                    if why[j][1] and nodes[j]["e"] in "vsp":
+                        pairs.append((why[j][0], j))
+                    j = why[j][0]
+                return pairs
+            out = [nodes[k] for k in best[1]]
+            mark = others(out)
+            best = (mark, out)
+            for n in range(SWAPS):
+                if n % 4 == 0:
+                    pairs = queued(out, cases[rng.randint(len(cases))])
+                a, b = pairs[rng.randint(len(pairs))]
+                place = {x["id"]: k for k, x in enumerate(out)}
+                i, j = place[a], place[b]
+                if i > j:
+                    continue
+                if all(place[k] < i for k in nodes[b]["pre"]):
+                    new = out[:i] + [out[j]] + out[i:j] + out[j + 1:]
+                elif all(place[k] > j for k in nodes[a]["post"]):
+                    new = out[:i] + out[i + 1:j + 1] + [out[i]] + out[j + 1:]
+                else:
+                    continue
+                m = others(new)
+                if m < mark + HEAT * (1 - n / SWAPS) * rng.exponential():
+                    out, mark = new, m
+                    if m < best[0]:
+                        best = (m, new)
+            ORDER.extend(x["id"] for x in best[1])
         return [nodes[k] for k in ORDER]
 
     def finish():
@@ -212,9 +288,8 @@ def helpers(topo, cores, rank):
     return [[c for c in free if topo.die(c) != topo.die(me)][0], [c for c in free if topo.die(c) == topo.die(me)][0]]
 
 
-def inner(topo, cores, rank, helper, t):
-    out = topo.engines(cores[rank], cores[rank - 1]) if t > 3 else []
-    return [e for e in topo.engines(cores[rank], helper) if e not in out]
+def carrier(t, q):
+    return q % 2 if t > 1 else q // 3
 
 
 def hand_on(g, core, T, topo):
@@ -226,9 +301,9 @@ def hand_on(g, core, T, topo):
         for t in range(1, 4):
             dst = T.cores[(rank - 1 - t % 3) % 4]
             rid, pid, _se = topo.addr(dst)
-            for q in range(two.index(core), 4, 2):
+            for q in [q for q in range(4) if two[carrier(t, q)] == core]:
                 x = T["FT%d" % t][:, 1024 * q:1024 * q + 1024]
-                g.wait_ge(T.sem["h%d%d" % (t, q)], len(inner(topo, T.cores, rank, core, t)))
+                g.wait_ge(T.sem["h%d%d" % (t, q)], len(topo.engines(T.cores[rank], core)))
                 g.remote_dma(x, x, T.sem["sn%d" % t], T.sem["hl"], pid, rid, topo.mask(core, dst))
                 n += len(topo.engines(core, dst))
         g.wait_ge(T.sem["hl"], n)
@@ -258,24 +333,24 @@ def rank_program(g, core, T, topo):
 
     def snapshot(t, quarters=range(4), lsem=None):
         for n, q in enumerate(quarters):
-            put(("FT%d" % t, 1024 * q, 1024 * q + 1024), ("TAB", 1024 * q, 1024 * q + 1024), mine[q % 2], "h%d%d" % (t, q), lsem or "loc%d" % t,
-                inner(topo, cores, rank, mine[q % 2], t), [("EHT", 0, 192)] if t == 1 else [], 2.5 + 1.5 * n)
+            put(("FT%d" % t, 1024 * q, 1024 * q + 1024), ("TAB", 1024 * q, 1024 * q + 1024), mine[carrier(t, q)], "h%d%d" % (t, q), lsem or "loc%d" % t,
+                None, [("EHT", 0, 192)] if t == 1 else [], 2.5 + 1.0 * n)
 
     def w(n, a=0, b=16):
         return ("WF", WIDX[n] + a, WIDX[n] + b)
 
-    pc = ("PC", 0, 16)
+    pc = ("PC", 0, 17)
 
     def P(n):
         return T.PC[:, PCOL[n]:PCOL[n] + 1]
 
-    def cost(out, sides, each):
+    def cost(out, sides, each, fix=FIX):
         n = 1
         for k in out.shape[1:]:
             n *= k
         if each is None:
             each = 0.5 if all(SCRATCH[x[0]][2] in (B16, F16, U16) for x in sides) else 1.0
-        return CYC * max(64, n * each)
+        return CYC * max(LEAST, n * each) + fix
 
     def ts(o, i, s1, o0, s2=None, o1=None, ia=None, oa=None, more=(), part=None):
         rd = [i] + list(more)
@@ -290,11 +365,11 @@ def rank_program(g, core, T, topo):
         if lst:
             ia, more = A(a).indirect(A(lst)), [lst]
         op("v", [a, b] + list(more), [o], lambda e: e.tensor_tensor(out, A(a) if ia is None else ia, A(b) if ib is None else ib, f),
-           0.055 + cost(out, [], GATHER) if lst else cost(out, [], 2.0))
+           (cost(out, [], GATHER, 0.05), 0.7 * cost(out, [], GATHER)) if lst else cost(out, [], 1.0 if SCRATCH[a[0]][0] != SB else 2.0))
 
     def act(o, i, f, ia=None, oa=None, more=(), part=None, price=None, **k):
         src, out = A(i) if ia is None else ia, A(o) if oa is None else oa
-        op("s", [i] + list(more), [o], lambda e: e.activation(out, src, f, **k), price or cost(out, [], 1.0), part)
+        op("s", [i] + list(more), [o], lambda e: e.activation(out, src, f, **k), price or cost(out, [], 1.0, SFIX), part)
 
     def cp(o, i, ia=None, oa=None, more=(), e="v", bias=None, part=None, price=None):
         src, out = A(i) if ia is None else ia, A(o) if oa is None else oa
@@ -305,18 +380,24 @@ def rank_program(g, core, T, topo):
         else:
             act(o, i, AF.Identity, ia, oa, more, part, price, bias=bias)
 
+    def lin(o, i, a, b, e, ia=None):
+        if e == "v":
+            ts(o, i, a, OP.mult, b, OP.add, ia=ia)
+        else:
+            act(o, i, AF.Identity, ia=ia, scale=a, bias=b)
+
     def gather(o, win, lst, e="v", bias=None):
-        cp(o, win, ia=A(win).indirect(A(lst)), more=[lst], e=e, bias=bias, price=0.07 + cost(A(o), [], GATHER))
+        cp(o, win, ia=A(win).indirect(A(lst)), more=[lst], e=e, bias=bias, price=(cost(A(o), [], GATHER, 0.06), 0.7 * cost(A(o), [], GATHER)))
 
     def scatter(win, lst, i):
-        cp(win, i, oa=A(win).indirect(A(lst)), more=[lst], price=0.055 + cost(A(i), [], SCATTER))
+        cp(win, i, oa=A(win).indirect(A(lst)), more=[lst], price=(cost(A(i), [], SCATTER, 0.05), 0.85 * cost(A(i), [], SCATTER)))
 
     def scan(o, d0, d1, init, o0, o1):
         op("v", [d0, d1], [o], lambda e: e.tensor_tensor_scan(A(o), A(d0), A(d1), init, o0, o1), cost(A(o), [o, d0, d1], None))
 
     def mm(o, l, r, start, stop, oa=None, la=None, ra=None):
         out = A(o) if oa is None else oa
-        op("p", [l, r], [o], lambda e: e.matmul(out, A(l) if la is None else la, A(r) if ra is None else ra, start, stop), cost(out, [], 1.0) * PE / CYC)
+        op("p", [l, r], [o], lambda e: e.matmul(out, A(l) if la is None else la, A(r) if ra is None else ra, start, stop), max(64 * CYC, cost(out, [], 1.0, 0.0)) * PE / CYC)
 
     def iota(o, pattern, base, cm=0):
         op("g", [], [o], lambda e: e.iota(A(o), pattern, base, cm, allow_small_or_imprecise_dtypes=True), 0.14 + 2 * CYC * (o[2] - o[1]))
@@ -330,25 +411,25 @@ def rank_program(g, core, T, topo):
     queued = [1.8]
 
     def load(n, dst, lo, hi, src, a, b, after=None):
-        queued[0] = (1.8 if after else queued[0]) + 0.2 + (hi - lo) * (2 if SCRATCH[dst][2] == B16 else 4) / 1750
+        queued[0] = (1.8 if after else queued[0]) + 0.2 + (hi - lo) * (2 if SCRATCH[dst][2] == B16 else 4) / RATE
         dma("y", "ld%d" % n, [], [(dst, lo, hi)], lambda e: e.dma_start(T[dst][:, lo:hi], T[src][:, a:b]), queued[0], after)
     load(0, "EFT", 192, 448, "ef", 0, 256)
     load(1, "ZFT", 192, 448, "zf", 0, 256)
-    load(2, "TAB", 0, 2048, "tab", 0, 2048)
     load(4, "EHT", 192, 448, "eh", 0, 256)
+    load(2, "TAB", 0, 2048, "tab", 0, 2048)
     load(3, "TAB", 2048, 4096, "tab", 2048, 4096)
     far = len(topo.engines(asker(0), core))
-    land("qu", far, "QE", 0, 256, "qu", 2.0)
-    land("qu", far, "QZ", 0, 256, "qu", 2.0)
+    land("qu", far, "QE", 0, 256, "qu", 2.5)
+    land("qu", far, "QZ", 0, 256, "qu", 2.5)
     land("rp", len(topo.engines(cores[seen(0)], core)), "RP", 0, 16, "rp", 1.5)
     for t in range(1, 4):
         a, n = 192 - 64 * t, len(topo.engines(cores[seen(t)], core))
         land("qf%d" % t, len(topo.engines(asker(t), core)), "QF", a, a + 64, "qf%d" % t, HOP)
-        land("qf%d" % t, len(topo.engines(asker(t), core)), "QY", a, a + 64, "qf%d" % t, HOP)
+        land("qf%d" % t, len(topo.engines(asker(t), core)), "QY", a, a + 64, "qf%d" % t, HOP + 1 if t == 1 else 2 * HOP)
         land("rq%d" % t, n, "SF%d" % t, 0, 64, "rq%d" % t, HOP)
-        land("sn%d" % t, sum(2 * len(topo.engines(h, core)) for h in helpers(topo, cores, seen(t))), "FT%d" % t, 0, 4096, "h%d3" % t, 9.0)
+        land("sn%d" % t, sum(len(topo.engines(helpers(topo, cores, seen(t))[carrier(t, q)], core)) for q in range(4)), "FT%d" % t, 0, 4096, "h%d3" % t, 9.0)
         land("rz%d" % t, n, "RZ%d" % t, 0, 256, "rz%d" % t, HOP)
-        land("rl%d" % t, n, "RL%d" % t, 0, 16, "rl%d" % t, HOP)
+        land("rl%d" % t, n, "RL%d" % t, 0, 16, "rl%d" % t, LIST)
 
     z0 = ("ZFT", 192, 448)
     iota(("PJ", 0, 1), [[0, 1]], 0, 1)
@@ -361,7 +442,7 @@ def rank_program(g, core, T, topo):
     memset(("HF", 0, 1), 200.0)
     memset(("ST", 0, 1024), 0.0)
     for k in range(8):
-        cp(("OCC", 512 * k, 512 * k + 512), ("ST", 0, 512), e="s", bias=-1.0)
+        cp(("OCC", 512 * k, 512 * k + 512), ("ST", 0, 512), e="s", bias=0.4)
 
     def c(n):
         return ("PC", PCOL[n], PCOL[n] + 1)
@@ -379,8 +460,9 @@ def rank_program(g, core, T, topo):
     col("EV", "P32", 16.0, OP.is_lt)
     col("OD", "P32", 16.0, OP.is_ge)
     col("SG", "I", -400.0, OP.mult, -200.0, OP.add)
-    col("F0", "M0", 832.0, OP.mult)
-    col("F1", "M0", -192.0, OP.mult)
+    col("F0", "M0", 832 * FINE, OP.mult, -512 * FINE, OP.add)
+    col("F1", "M0", -192 * FINE, OP.mult, -512 * FINE, OP.add)
+    col("MN", "M0", -1.0, OP.mult)
     col("WP", "M1", -2048.0, OP.mult, P("M0"), OP.add)
     col("WD", "M1", -128.0, OP.mult, P("M0"), OP.add)
     col("N1", "I", 1.0, OP.not_equal)
@@ -407,11 +489,13 @@ def rank_program(g, core, T, topo):
     tt(("TRI", 0, 128), ("T1", 0, 128), ("BO8", 0, 128), OP.mult)
     memset(("RS", 0, 256), -20000.0)
     ts(("RS", 0, 256), ("CI", 0, 16), P("I"), OP.add, LOOK - OFF, OP.add, oa=T.RS[:, 0:256:16], more=[pc])
-    ts(("AB", 0, 768), ("ST", 0, 768), P("N1"), OP.add, more=[pc])
+    if SEARCH > 1:
+        ts(("AB", 0, 256 * SEARCH - 256), ("ST", 0, 256 * SEARCH - 256), P("N1"), OP.add, more=[pc])
     ts(("DW", 0, 48), ("CI", 0, 48), P("I"), OP.add, 768.0 - 2047.0, OP.add, more=[pc])
     memset(("DB", 0, 256), 0.0)
     memset(("KD", 0, 256), -W1 / 2)
-    for n, f in (("X0", "M0"), ("XO", "M1"), ("XP", "WP"), ("XD", "WD")):
+    ts(("NIH", 0, 128), qx, P("P"), OP.is_equal, -1.0, OP.mult, more=[pc])
+    for n, f in (("X0", "M0"), ("XN", "MN"), ("XO", "M1"), ("XP", "WP"), ("XD", "WD")):
         ts((n, 0, 144), ("QX", 0, 144), P("G"), OP.is_equal, P(f), OP.mult, more=[pc])
     ts(("BO0", 0, 128), ("Q4", 0, 128), P("G"), OP.is_equal, P("M0"), OP.mult, more=[pc])
     ts(("MB", 0, 192), ("JM", 0, 192), P("I"), OP.is_equal, 60000.0, OP.mult, more=[pc])
@@ -429,15 +513,12 @@ def rank_program(g, core, T, topo):
         ask(cores[seen(t)], ("SEF", a, a + 64), ("QF", a, a + 64), ("ZFT", a, a + 64), ("QY", a, a + 64), "qf%d" % t, "loc7", 2.0)
     cp(("EFO", 0, 256), ("EFT", 192, 448))
     ask(cores[seen(0)], ("EFO", 0, 256), ("QE", 0, 256), z0, ("QZ", 0, 256), "qu", "loc0", 6.5)
-    for k, (o, i) in enumerate((("EFT", "ef"), ("ZFT", "zf"), ("EHT", "eh"))):
-        load(5 + k, o, 0, 192, i, 832, 1024, "loc0" if k == 0 else None)
-    for k, (o, i) in enumerate((("ZFT", "zf"), ("EHT", "eh"), ("EFT", "ef"))):
-        load(8 + k, o, 448, 1024, i, 256, 832)
     iota(("IOT", 0, 1024), [[1, 1024]], 0)
     iota(("JR", 0, 192), [[1, 192]], 0)
-    cp(("FN", 0, 192), ("IOT", 0, 192), e="s", bias=P("F0"), more=[pc])
-    for a in (192, 608):
-        cp(("FN", a, a + 416), ("IOT", a, a + 416), e="s", bias=P("F1"), more=[pc])
+    for k, (o, i) in enumerate((("EFT", "ef"), ("ZFT", "zf"), ("EHT", "eh"))):
+        load(5 + k, o, 0, 192, i, 832, 1024, "loc0" if k == 0 else None)
+    for (a, b, f) in ((0, 192, "F0"), (192, 608, "F1"), (608, 1024, "F1")):
+        act(("FN", a, b), ("IOT", a, b), AF.Identity, more=[pc], scale=FINE, bias=P(f))
     cp(("SEH", 0, 192), ("EHT", 0, 192))
     cp(("SEF", 0, 192), ("EFT", 0, 192))
 
@@ -462,11 +543,7 @@ def rank_program(g, core, T, topo):
         mm(d, (zt, 0, 128), ("EX", 0, 512), True, False, la=T[zt][row:row + 16 * n, :], ra=T.EX[row:row + 16 * n, 0:256 * n])
         gather(gb, win, (lst, col0, col0 + 16 * n), e="s")
         mm(d, ("NID", 0, 128), gb, False, True)
-        batch(True)
-        for h in range(n):
-            act((dst, 256 * (m + h), 256 * (m + h) + 256), d, AF.Sigmoid, ia=T[d[0]][:, 256 * h:256 * h + 256], oa=T[dst][:, m + h, :],
-                more=[("HF", 0, 1)], bias=T.HF[:, 0:1], scale=400.0)
-        batch(False)
+        act((dst, 256 * m, 256 * (m + n)), d, AF.Sigmoid, oa=T[dst][:, m:m + n, :], more=[("HF", 0, 1)], bias=T.HF[:, 0:1], scale=400.0)
 
     def v_block(dst, m, win, lst, col0, zx, b):
         tt((dst, 256 * m, 256 * m + 256), win, (zx, 256 * b, 256 * b + 256), OP.is_le, oa=T[dst][:, m, :], lst=(lst, col0, col0 + 16))
@@ -487,7 +564,7 @@ def rank_program(g, core, T, topo):
         for (src, b0, b1, h) in parts:
             ts(ep, src, -2048.0, OP.add, oa=T.EP[:, b0:b1, 16 * h:16 * h + 16])
         batch(False)
-        op("v", [ep], [tr], lambda e: e.transpose(T.TR[:, :, :], T.EP[:, :, :]), 128 * CYC)
+        op("v", [ep], [tr], lambda e: e.transpose(T.TR[:, :, :], T.EP[:, :, :]), 128 * CYC + FIX)
 
     def slots_mm():
         batch(True)
@@ -501,10 +578,10 @@ def rank_program(g, core, T, topo):
             mm(("PA", 0, 256), ("RO", 128 * k, 128 * k + 128), src, start, start or (stop and k == 15), oa=T.PA[:, k:256:16])
         batch(False)
 
-    def pick(x, src, n):
+    def pick(x, src, a, start, stop):
         batch(True)
         for k in range(16):
-            mm(("PB", 0, n), (x, 16 - k, 144 - k), src, k == 0, k == 15, ra=T[src[0]][:, src[1] + k:src[2]:16])
+            mm(("PB", a, a + (src[2] - src[1]) // 16), (x, 16 - k, 144 - k), src, start and k == 0, stop and k == 15, ra=T[src[0]][:, src[1] + k:src[2]:16])
         batch(False)
 
     def slot(t):
@@ -524,23 +601,24 @@ def rank_program(g, core, T, topo):
         if t == 0:
             return
         cp(("SL", 0, 16), ("IW", 16, 32))
-        gather(("OG", 0, 256), ("OCC", 0, 4096), ("SL", 0, 16), e=ON["OG"])
-        pick("XO", ("OG", 0, 256), 16)
-        cp(("BL", 0, 16), ("PB", 0, 16))
-        ts(w("OC"), ("PB", 0, 16), 0.0, OP.is_ge)
-        tt(w("Y0"), ("PB", 0, 16), w("FW"), OP.subtract)
-        tt(w("Y"), w("Y0"), w("OC"), OP.mult)
-        gather(("DB", 256, 512), ("ST", 0, 1024), ("BL", 0, 16), e="s", bias=-127.0)
-        pick("X0", ("DB", 0, 512), 32)
-        ts(w("X0"), ("PB", 0, 16), 128.0, OP.add)
-        tt(w("X1"), ("PB", 16, 32), w("X0"), OP.subtract)
-        tt(w("X2"), w("X1"), w("OC"), OP.mult)
-        ts(w("X"), w("X2"), 128.0, OP.add)
+        occ, sl, og = ("OCC", 0, 4096), ("SL", 0, 16), ("OG", 0, 256)
+        act(og, occ, AF.Identity, ia=A(occ).indirect(A(sl)), more=[sl], price=(0.4, 0.25), scale=4 / FINE, bias=1536 - 2 / FINE)
+        pick("XO", og, 0, True, True)
+        pick("XO", og, 16, True, False)
+        mm(("PB", 16, 32), ("NIH", 0, 128), ("FW", 0, 16), False, True)
+        lin(("BL", 0, 16), ("PB", 0, 16), 1.0, -1024.0, ON["BL"])
+        ts(w("OC"), ("PB", 0, 16), 1024.0, OP.is_ge, 1 / 128, OP.mult)
+        tt(w("Y"), ("PB", 16, 32), w("OC"), OP.mult)
+        gather(("DB", 256, 512), ("ST", 0, 1024), ("BL", 0, 16), e="s", bias=-255.0)
+        pick("X0", ("DB", 256, 512), 32, True, False)
+        pick("XN", ("DB", 0, 256), 32, False, True)
+        tt(w("X"), ("PB", 32, 48), w("OC"), OP.mult)
 
     def mark(t):
         cp(("PM", 0, 192), ("DB", 64, 256), e="s", bias=128.0)
-        memset(("ST", 192 - 64 * t, 256 - 64 * t), 128.0)
-        scatter(("ST", 0, 1024), ("FL", 0, 12), ("PM", 0, 192))
+        cp(("ST", 192 - 64 * t, 256 - 64 * t), ("DB", 0, 64), e="s", bias=128.0)
+        for k in range(0, 12, 12 // PIECES[1]):
+            scatter(("ST", 0, 1024), ("FL", k, k + 12 // PIECES[1]), ("PM", 16 * k, 16 * k + 192 // PIECES[1]))
 
     def lanes(t):
         return z0 if t == 0 else ("ZL%d" % t, 0, 256)
@@ -549,38 +627,38 @@ def rank_program(g, core, T, topo):
         wl = ("WL%d" % t, 0, 16)
         if t:
             sf, far = ("SF%d" % t, 0, 256), ends("SF%d" % t)
-            scan((sf[0], 64, 256), ("SCM", 64, 256), ("KF", 64, 256), 0.0, OP.mult, OP.max)
         else:
             sf, far = ("RP", 0, 16), T.RP[:, :]
-        for m in range(16):
+        turns = [m + k for m in ([0] + fours(4, SPLIT[1]) if t else range(0, 16, 4)) for k in range(4)]
+        for m in turns:
             n, x = 256 - 16 * m, 16 * m + 15 if t else m
             ts(("EE", 256 * m, 256 * m + n), ("SR", 16 * m, 256), A(w("SW", m, m + 1)), OP.subtract, T[sf[0]][:, x:x + 1], OP.is_equal,
                oa=T.EE[:, m, 0:n], more=[w("SW"), (sf[0], x, x + 1)])
             if m < 15:
                 mm(("CN", 16 * m + 16, 256), ("BO8", 0, 128), ("EE", 256 * m, 256 * m + n), False, False, ra=T.EE[:, m, 16:n])
             if m % 4 == 3:
-                mm(("CN", 16 * m - 48, 16 * m + 16), ("TRI", 0, 128), ("EE", 256 * m - 768, 256 * m + 256), False, m == 15, ra=T.EE[:, m - 3:m + 1, 0:16])
-        ts(w("FA"), sf, 1 / W1, OP.mult, 8.0, OP.add, ia=far)
+                mm(("CN", 16 * m - 48, 16 * m + 16), ("TRI", 0, 128), ("EE", 256 * m - 768, 256 * m + 256), False, m == turns[-1], ra=T.EE[:, m - 3:m + 1, 0:16])
+        lin(w("FA"), sf, 1 / W1, 8.0, "s", far)
         tt(w("FC"), w("FA"), sf, OP.min, ib=far)
         tt(("WH", 32, 48), w("FC"), w("HN"), OP.max)
         spread(("WH", 32, 48), False, False)
         cs = ("CS", 0, 256)
         scan(cs, ("RS", 0, 256), ("CN", 0, 256), -20000.0, OP.max, OP.min)
-        ts(wl, cs, OFF, OP.add, ia=ends("CS"))
+        lin(wl, cs, 1.0, OFF, ON["WL"], ends("CS"))
+        win = ("WH", 16, 32)
+        ts(win, cs, 4096.0 - OFF, OP.is_lt, 128.0, OP.mult, ia=ends("CS"))
+        spread(win, False, t == 0)
         if t:
-            ts(w("WIN"), cs, 4096.0 - OFF, OP.is_lt, ia=ends("CS"))
-            tt(("WH", 16, 32), w("WIN"), w("X"), OP.mult)
-            tt(w("T2"), w("WIN"), w("Y"), OP.mult)
-            tt(w("TF"), w("T2"), w("FW"), OP.add)
-            cp(("TL", 0, 16), w("TF"))
-        else:
-            ts(("WH", 16, 32), cs, 4096.0 - OFF, OP.is_lt, 128.0, OP.mult, ia=ends("CS"))
-        spread(("WH", 16, 32), False, True)
+            tt(("WH", 48, 64), win, w("X"), OP.mult)
+            spread(("WH", 48, 64), False, True)
+            tt(w("T2"), win, w("Y"), OP.mult)
+            tt(w("TF"), w("T2"), ("FW", 0, 16), OP.add)
+            lin(("TL", 0, 16), w("TF"), 1.0, -1024.0, ON["TL"])
         if t < 3:
             put(("RL%d" % (t + 1), 0, 16), wl, asker(t + 1), "rl%d" % (t + 1), "loc%d" % (8 + t))
         scatter(("TAB", 0, WT), wl, lanes(t))
         if t < 3:
-            cp(("TAB", 4096, LOOK), ("TAB", 0, LOOK - 4096))
+            cp(("TAB", 4096, LOOK), ("TAB", 0, LOOK - 4096), e="s")
         if t < 2:
             snapshot(t + 2)
         if t:
@@ -588,7 +666,7 @@ def rank_program(g, core, T, topo):
             scatter(("ST", 0, 1024), ("TL", 0, 16), ("STN", 0, 256))
         else:
             cp(("ST", 192, 448), ("PA", 0, 256), e="s")
-        scatter(("OCC", 0, WT), wl, ("FR%d" % t, 0, 256) if t else ("FN", 192, 448))
+        act(("OCC", 0, WT), ("FR%d" % t, 0, 256) if t else ("FN", 192, 448), AF.Sigmoid, oa=T.OCC[:, :].indirect(A(wl)), more=[wl], price=(0.87, 0.7))
 
     def fresh(t):
         a = 192 - 64 * t
@@ -606,10 +684,12 @@ def rank_program(g, core, T, topo):
 
     def select(t):
         U, lo, n = 256 * t, 256 - 64 * t, 16 * t
+        if t >= SEARCH:
+            return search(t, lo, U + 192)
         ts(("FB", 0, U), ("ST", lo, lo + U), 128.0, OP.is_lt)
         scan(("VB", 0, U), ("AB", 0, U), ("FB", 0, U), 0.0, OP.mult, OP.add)
         mm(("PA", 0, 1), ("BO0", 0, 128), ("VB", U - 1, U), True, True)
-        pick("XP", ("VB", 0, U), n)
+        pick("XP", ("VB", 0, U), 0, True, True)
         ts(("LW", 0, 192), ("JR", 0, 192), T.PA[:, 0:1], OP.subtract, float(lo + U), OP.add, more=[("PA", 0, 1)])
         tt(("LF", 0, n), ("PB", 0, n), ("DW", 0, n), OP.min)
         ts(("LU", 0, n), ("LF", 0, n), 2047.0, OP.add)
@@ -617,52 +697,86 @@ def rank_program(g, core, T, topo):
         scan(("WS", 0, 192), ("MB", 0, 192), ("LW", 0, 192), 0.0, OP.max, OP.min)
         cp(("FL", 0, 12), ("WS", 0, 192), ia=ends("WS", 192))
 
+    def search(t, lo, R):
+        jr, mb, n = ("JR", 0, 192), ("MB", 0, 192), 16 * t + 16
+        memset(("VB", R, R + 64), 2000.0)
+        ts(("FB", 0, R), ("ST", lo, lo + R), 128.0, OP.is_lt)
+        scan(("VB", 0, R), ("FB", 0, R), ("FB", 0, R), 0.0, OP.add, OP.max)
+        op("v", [("MB", 0, n), ("VB", 0, R + 64)], [("LF", 0, n)],
+           lambda e: e.tensor_tensor_scan(T.LF[:, 0:n], T.MB[:, 0:n], T.VB[:, 15:R + 64:16], 0.0, OP.max, OP.min), 64 * CYC + FIX)
+        pick("XO", ("VB", 0, R), 0, True, True)
+        cp(("LW", 0, R // 16), ("PB", 0, R // 16))
+        for k in range(t + 1):
+            ts(("YA", 192 * k, 192 * k + 192), jr, T.LF[:, 16 * k + 15:16 * k + 16], OP.is_ge, 16.0, OP.mult, more=[("LF", 0, n)])
+            mm(("PA", 0, 192), ("BO", 0, 128), ("YA", 192 * k, 192 * k + 192), k == 0, k == t)
+        for k in range(t + 1):
+            mm(("CN", 0, 192), ("BO", 0, 128), ("YA", 192 * k, 192 * k + 192), k == 0, False)
+        scan(("WS", 0, 192), mb, ("PA", 0, 192), 0.0, OP.max, OP.min)
+        ts(("LU", 0, 12), ("WS", 0, 192), 1 / 16, OP.mult, ia=ends("WS", 192))
+        tt(("STN", 0, 192), ("LW", 0, R // 16), jr, OP.is_le, lst=("LU", 0, 12))
+        mm(("CN", 0, 192), ("BO", 0, 128), ("STN", 0, 192), False, True)
+        scan(("WS", 0, 192), mb, ("CN", 0, 192), 0.0, OP.max, OP.min)
+        ts(("FL", 0, 12), ("WS", 0, 192), float(lo), OP.add, ia=ends("WS", 192))
+
     def entries(tab, a, o):
         tt((a, 0, 192), (tab, 0, 1024), ("DB", 64, 256), OP.add, lst=("FL", 0, 12))
         cp((o, 0, 192), (a, 0, 192))
 
-    def blocks(dst, key, first, split, win, lst, col0, zt, zx, zx0):
+    def blocks(dst, key, first, split, win, lst, col0, zt, zx, zx0, out=None):
         for m in range(first, split, 2):
             s_unit(dst, m, win, lst, 16 * (m - col0), *zt(m), min(2, split - m))
         for m in range(15, split - 1, -1):
             v_block(dst, m, win, lst, 16 * (m - col0), zx, m - zx0)
-        low, high = first, 16
-        while high - low > 4:
+        for n, m in enumerate(fours(first, split)):
+            if out:
+                bank = (key, "ZP")[n % 2]
+                key_open(bank, 16 * m, 16 * m + 64)
+                sums(bank, dst, m, m + 4, True)
+                scan((out, 16 * m, 16 * m + 64), ("SCM", 0, 64), (bank, 16 * m, 16 * m + 64), 0.0, OP.mult, OP.max)
+            else:
+                sums(key, dst, m, m + 4, n == 3 - first // 4)
+
+    def fours(low, split):
+        high, out = 16, []
+        while high > low:
             if split - low >= high - split:
-                sums(key, dst, low, low + 4)
+                out.append(low)
                 low += 4
             else:
-                sums(key, dst, high - 4, high)
                 high -= 4
-        sums(key, dst, low, high, True)
+                out.append(high)
+        return out
 
     def penalties(t):
         ft, fl, zl, a = "FT%d" % t, ("FL", 0, 12), "ZL%d" % t, 192 - 64 * t
-        gather(("DB", 64, 256), ("ST", 0, 1024), fl, e=ON["DL"])
-        gather((zl, 64, 256), ("ZFT", 0, 1024), fl, e="s")
+        gather(("DB", 64, 256), ("ST", 0, 1024), fl, e=ON["DL"][t - 1])
+        gather((zl, 64, 256), ("ZFT", 0, 1024), fl, e=ON["ZL"][t - 1])
         if t < 3:
             put(("RZ%d" % (t + 1), 0, 256), (zl, 0, 256), asker(t + 1), "rz%d" % (t + 1), "loc%d" % (4 + t))
         scan(("SQ", 0, 64), ("SCM", 0, 64), ("KF", 0, 64), 0.0, OP.mult, OP.max)
         put(("SF%d" % t, 0, 64), ("SQ", 0, 64), asker(t), "rq%d" % t, "loc%d" % (11 + t))
+        if t == 1:
+            ask_fresh(2)
+            ask_fresh(3)
         entries("EHT", "EI", "EHO")
         entries("EFT", "FI", "EFO")
         ts(("EM", 0, 192), ("EI", 0, 192), 4095, OP.bitwise_and)
         expand("ZX", (zl, 16 * min(SPLIT), 256), ZS)
         turn("ZT", (zl, 64, min(192, 16 * max(SPLIT))))
         if max(SPLIT) > 12:
-            turn("ZU", (zl, 192, 16 * max(SPLIT)))
-        key_open("KF", 64, 256)
-        scatter((ft, 0, WT), ("RL%d" % t, 0, 16), ("RZ%d" % t, 0, 256))
-        cp((ft, 4096, LOOK), (ft, 0, LOOK - 4096))
+            turn("ZTQ", (zl, 192, 16 * max(SPLIT)))
+        for k in range(0, 16, 16 // PIECES[0]):
+            scatter((ft, 0, WT), ("RL%d" % t, k, k + 16 // PIECES[0]), ("RZ%d" % t, 16 * k, 16 * k + 256 // PIECES[0]))
+        cp((ft, 4096, LOOK), (ft, 0, LOOK - 4096), e=ON["FT"])
         slots_in(((("EHT", a, a + 64), 0, 4, 0), (("EM", 0, 64), 4, 8, 0), (("EM", 64, 192), 0, 8, 1)))
         slots_mm()
 
         def zt(m):
-            return ("ZT", 16 * m - 64) if m < 12 else ("ZU", 16 * m - 192)
+            return ("ZT", 16 * m - 64) if m < 12 else ("ZTQ", 16 * m - 192)
         blocks("CH", "KH", 4, SPLIT[0], ("TAB", 0, LOOK), "EHO", 4, zt, "ZX", min(SPLIT))
-        blocks("CF", "KF", 4, SPLIT[1], (ft, 0, LOOK), "EFO", 4, zt, "ZX", min(SPLIT))
-        cp(w("FW", 4, 16), ("WS", 0, 192), ia=ends("WS", 192))
-        ts(w("FW", 0, 4), ("CI", 0, 4), P("I"), OP.add, float(a), OP.add, more=[pc])
+        blocks("CF", "KF", 4, SPLIT[1], (ft, 0, LOOK), "EFO", 4, zt, "ZX", min(SPLIT), "SF%d" % t)
+        lin(("FW", 4, 16), ("WS", 0, 192), 1.0, 1024.0 + (a + 64 if t >= SEARCH else 0), ON["FW"], ends("WS", 192))
+        lin(("FW", 0, 4), ("DW", 0, 4), 1.0, a + 1024.0 + 2047.0 - 768.0, ON["FW"])
         gather(("FR%d" % t, 64, 256), ("FN", 0, 1024), fl, e="s")
         slot(t)
         if t < 3:
@@ -674,13 +788,13 @@ def rank_program(g, core, T, topo):
         expand("ZX", ("ZFT", 192 + 16 * h, 448), 16)
         cp(("EHO", 0, 256), ("EHT", 192, 448))
         slots_in(((("EHT", 192, 320), 0, 8, 0), (("EHT", 320, 448), 0, 8, 1)))
-        snapshot(1, (0, 2))
         ask_fresh(1)
+        snapshot(1, range(EARLY))
         key_open("KH")
         key_open("KF")
         slots_mm()
         turn("ZTQ", ("QZ", 0, 16 * f))
-        expand("ZXQ", ("QZ", 16 * f, 256), 0)
+        expand("ZXQ", ("QZ", 16 * f, 256), ZQ)
         for m in range(0, 4, 2):
             s_unit("CH", m, tab, "EHO", 16 * m, "ZT", 16 * m)
         sums("KH", "CH", 0, 4)
@@ -689,10 +803,10 @@ def rank_program(g, core, T, topo):
         scan(("SF", 0, 256), ("SCM", 0, 256), ("KF", 0, 256), 0.0, OP.mult, OP.max)
         cp(("SP", 0, 16), ("SF", 0, 256), ia=ends("SF"))
         put(("RP", 0, 16), ("SP", 0, 16), asker(0), "rp", "loc11")
-        snapshot(1, (1, 3), "loc15")
+        snapshot(1, range(EARLY, 4), "loc15")
+        for k, (o, i) in enumerate((("ZFT", "zf"), ("EHT", "eh"), ("EFT", "ef"))):
+            load(8 + k, o, 448, 1024, i, 256, 832, "loc11" if k == 0 else None)
         put(("RZ1", 0, 256), z0, asker(1), "rz1", "loc4")
-        ask_fresh(2)
-        ask_fresh(3)
         slot(0)
 
     penalties_0()
@@ -704,16 +818,19 @@ def rank_program(g, core, T, topo):
         claims(t)
     def store(e, n, o, oa, i, ia, dur):
         dma(e, "out%d" % n, [i], [o], lambda q: q.dma_start(oa, ia), dur)
+    store("s", 4, ("SF", 0, 256), T.SF[:, :], ("OCC", 0, 4096), T.OCC[0:128:16, 0:4096], 2.5)
+    lin(("OG", 0, 256), ("SF", 0, 256), 4 / FINE, 1536 - 2 / FINE, "s")
+    ts(("SF1", 0, 256), ("OG", 0, 256), -1024.0, OP.add, -1.0, OP.max)
     for h in range(2):
         a, b = 2048 * h, 2048 * h + 2048
-        store("y", h, ("yt", a, b), T.yt[:, a:b], ("TAB", a, b), T.TAB[:, a:b], 4.2 + 2.4 * h)
+        store("y", h, ("yt", a, b), T.yt[:, a:b], ("TAB", a, b), T.TAB[:, a:b], 3.6 + 1.9 * h)
     ts(("YA", 0, 1024), ("ST", 0, 1024), P("LO"), OP.max, P("HI"), OP.min, more=[pc])
     batch(True)
     for k in range(16):
         a = (64 * k + 192) % 1024
         mm(("PB", 0, 64), ("XD", 16 - k, 144 - k), ("YA", a, a + 64), k == 0, k == 15)
     batch(False)
-    store("y", 2, ("yo", 0, 4096), T.yo[:, :], ("OCC", 0, 4096), T.OCC[0:128:16, 0:4096], 2.5)
+    store("y", 2, ("yo", 0, 4096), T.yo[:, :], ("SF1", 0, 256), T.SF1[:, :], 2.5)
     cp(("YD", 0, 64), ("PB", 0, 64), e="s", bias=16256.0)
-    store("s", 3, ("yd", 0, 1024), T.yd[:, :], ("YD", 0, 64), T.YD[:, :], 2.0)
+    store("s", 3, ("yd", 0, 1024), T.yd[:, :], ("YD", 0, 64), T.YD[:, :], 2.5)
     finish()

import numpy as np
from concourse.mybir import AluOpType, ActivationFunctionType
from concourse.bass import DstId, RemoteDMATransfer

OP = AluOpType
AF = ActivationFunctionType
W1 = 65536.0
BIG = 8192.0
OFF = 2048.0 + BIG
LOOK = 4096 + 64
WT = LOOK + 256
ON = {"SR": "s", "DL": "sss", "ZL": "sss", "BL": "s", "WL": "v", "TL": "v", "FW": "s", "FT": "s"}
FINE = 1 / 8192
EARLY = 3
SPLIT0, SPLIT = (7, 7), (9, 9)
ZS, ZQ = 7, 4
CYC, PE, GATHER, SCATTER, WAKE, WAKE_SAME, FILL, HOP = 0.00085, 0.00035, 1.56, 3.8, 0.18, 0.2, 1.0, 5.0
FIX, LEAST, SFIX, RATE = 0.0, 64, 0.03, 2200
CASES = ((0.15, 0.3, -0.03, 0.0, 1.0, 1.0), (0.15, 0.15, 0.035, 0.0, 0.75, 1.0), (0.2, 0.2, 0.0, 1.0, 1.0, 0.7), (0.2, 0.2, 0.0, 0.4, 1.4, 0.8))
LIST, SEARCH, PIECES = 5.0, 2, (1, 3)
ROUNDS, TRIES, SWAPS, HEAT, ORDER = 4, 200, 4000, 0.12, []
SB = "sbuf"
F32, B16, F16, I32, U16 = "float32", "bfloat16", "float16", "int32", "uint16"
SCRATCH = {}
for _names, _w, _d in (
        ("TAB FT1 FT2 FT3", WT, B16), ("OCC", WT, F32), ("ST ZFT YA", 1024, B16), ("EHT EFT", 1024, I32), ("IOT FN", 1024, F32),
        ("PJ", 4, I32), ("PC", 24, F32), ("CI", 48, F32), ("QX", 160, F32), ("Q4 T1 T2", 128, F32), ("JM RS SCM SH SF CS FR1 FR2 FR3", 256, F32),
        ("MB WS", 192, F32), ("JR", 192, B16), ("DW", 48, F32), ("HF", 8, F32), ("EX EXI GB0 GB1 DB", 512, B16), ("KC KD CM STN QZ PM", 256, B16),
        ("XV X0 XN XD", 144, B16), ("NIH", 128, F16), ("FW", 16, F16), ("XP XO", 144, F16), ("BE BD", 160, F16), ("BO BO8 TRI NID PID ZT ZTF ZTQ", 128, B16), ("BO0 PIH BOH", 128, F16),
        ("RO", 2048, F16), ("ZX ZXQ", 2560, B16), ("SR OG", 256, F16), ("AB FB VB", 1024, F16), ("LW", 1536, F32),
        ("EHO EFO QE", 256, U16), ("SEH SEF", 192, U16), ("EI EM FI", 192, I32), ("IW", 64, I32), ("WF", 256, F32), ("WH", 64, F16),
        ("RP SP", 16, F32), ("LF", 64, F32), ("LU", 48, U16), ("SL BL TL FL", 16, U16), ("YD", 64, F32),
        ("SF1 SF2 SF3", 256, F32), ("SQ", 64, F32), ("QF", 192, U16), ("QY", 192, B16), ("ZTG TU", 128, B16),
        ("ZL1 ZL2 ZL3 RZ1 RZ2 RZ3", 256, B16), ("WL0 WL1 WL2 WL3 RL1 RL2 RL3", 16, U16)):
    for _n in _names.split():
        SCRATCH[_n] = (SB, [128, _w], _d)
for _n in ("CH", "CF", "EE"):
    SCRATCH[_n] = (SB, [128, 16, 256], B16)
for _n in ("EP", "TR"):
    SCRATCH[_n] = (SB, [128, 8, 32], F16)
for _n in ("KH", "KF", "D0", "D1", "ZP", "PA", "PB", "CN"):
    SCRATCH[_n] = ("psum", [128, 512], F32)
SEMAPHORES = ["cv", "cs", "cp", "cg", "qu", "rp", "hl"] + ["ld%d" % _i for _i in range(12)] + ["loc%d" % _i for _i in range(16)]
SEMAPHORES += ["%s%d" % (_s, _t) for _s in ("sn", "qf", "rq", "rz", "rl") for _t in range(1, 4)] + ["out%d" % _i for _i in range(5)]
SEMAPHORES += ["h%d%d" % (_t, _q) for _t in range(1, 4) for _q in range(4)]
WIDX = {n: 16 * i for i, n in enumerate("SW HG HN FA FC WIN T2 OC X0 X1 X Y0 Y FW TF X2".split())}
PCOL = {n: i for i, n in enumerate("I P G P32 M0 M1 EV OD WP WD N1 F0 F1 LO HI SG MN".split())}


def make(g, T):
    eng = {"v": g.vector, "s": g.scalar, "p": g.tensor, "g": g, "y": g.sync}
    sem = {"v": "cv", "s": "cs", "p": "cp", "g": "cg"}
    nodes, acc, total, sender, last, open_batch = [], {}, {}, {}, {}, [None]

    def psum(b):
        return b in SCRATCH and SCRATCH[b][0] == "psum"

    def add(e, own, reads, writes, fns, hold, dur, s=None, part=None):
        me = {"id": len(nodes), "e": e, "own": own, "fns": fns, "hold": hold, "dur": dur, "s": s, "part": part, "pre": {}, "more": 0.0, "name": writes[0][0] if writes else s}
        nodes.append(me)
        link(me, reads, writes)
        if e in "gy":
            if e in last:
                me["pre"].setdefault(last[e], False)
            last[e] = me["id"]
        return me

    def link(me, reads, writes):
        for mode, lst in (("r", reads), ("w", writes)):
            for (b, lo, hi) in lst:
                ps = psum(b)
                for (l2, h2, m2, k) in acc.get(b, []):
                    x = nodes[k]
                    if x is me or (not ps and (h2 <= lo or hi <= l2)) or (mode == m2 == "r" and (not ps or x["own"] == me["own"])):
                        continue
                    if me["part"] and mode == m2 == "w" and x["part"] == me["part"]:
                        continue
                    wait = not (x["own"] == me["own"] == "p" and mode == "w")
                    me["pre"][k] = wait or me["pre"].get(k, False)
        for (b, lo, hi) in writes:
            lst = acc.setdefault(b, [])
            lst[:] = [x for x in lst if not (psum(b) or (lo <= x[0] and x[1] <= hi)) or (me["part"] and nodes[x[3]]["part"] == me["part"])]
            lst.append((lo, hi, "w", me["id"]))
        for (b, lo, hi) in reads:
            acc.setdefault(b, []).append((lo, hi, "r", me["id"]))

    def op(e, reads, writes, fn, cost, part=None):
        b = open_batch[0]
        cost, more = cost if isinstance(cost, tuple) else (cost, 0.4 * cost)
        if b is not None and e in b:
            me = b[e]
            me["fns"].append(fn)
            me["hold"] += cost
            me["dur"] += cost
            link(me, reads, writes)
        else:
            me = add(e, e, reads, writes, [fn], cost, cost, sem[e], part)
            if b is not None:
                b[e] = me
        me["more"] += more

    def batch(on):
        open_batch[0] = {} if on else None

    def dma(e, s, reads, writes, fn, dur, after=None):
        me = add(e, "dma" + s, reads, writes, [fn], 0.1, dur, s)
        total[s] = 16
        if after:
            me["pre"][sender[after]] = True

    def send(s, n, reads, fn, lands, dur):
        me = add("g", "rem" + s, reads, [], [fn], 0.5 if sender else 2.5, dur, s)
        total[s] = total.get(s, 0) + n
        sender[s] = sender[lands] = me["id"]

    def land(s, n, b, lo, hi, like, lag):
        me = add("n", "net" + s, [], [(b, lo, hi)], [], 0.0, lag, s)
        me["like"] = like
        total[s] = n

    def order():
        for x in nodes:
            x["post"] = []
            if "like" in x:
                x["pre"][sender[x["like"]]] = False
        for x in nodes:
            for k in x["pre"]:
                nodes[k]["post"].append(x["id"])

        def step(a, b):
            if b["e"] == "n":
                return a["dur"]
            return a["dur"] + (WAKE_SAME if a["e"] == b["e"] else WAKE) if b["pre"][a["id"]] else a["hold"]

        def run(way, back):
            pre, post = ("post", "pre") if back else ("pre", "post")
            left = [len(x[pre]) for x in nodes]
            ready = [x["dur"] - x["hold"] if back else 0.0 for x in nodes]
            free = {e: 0.0 for e in "vspgyn"}
            cand = {e: [x for x in nodes if x["e"] == e and not x[pre]] for e in free}
            out, start = [], [0.0] * len(nodes)
            while len(out) < len(nodes):
                best = None
                for e, lst in cand.items():
                    if not lst:
                        continue
                    lst.sort(key=lambda x: (-way[x["id"]], x["id"]))
                    pick = lst[0]
                    r = ready[pick["id"]]
                    if e == "n":
                        pick = min(lst, key=lambda x: ready[x["id"]])
                    elif r > free[e]:
                        for y in lst[1:]:
                            at = max(free[e], ready[y["id"]])
                            if at < r and at + y["hold"] - r < FILL * (r - at) + max(0.0, y["hold"] - way[pick["id"]] + way[y["id"]]):
                                pick = y
                                break
                    at = max(free[e], ready[pick["id"]])
                    if best is None or at < best[0]:
                        best = (at, pick)
                at, x = best
                cand[x["e"]].remove(x)
                free[x["e"]] = at + x["hold"]
                start[x["id"]] = at
                out.append(x)
                for k in x[post]:
                    y = nodes[k]
                    ready[k] = max(ready[k], at + (x["hold"] + step(y, x) - y["hold"] if back else step(x, y)))
                    left[k] -= 1
                    if not left[k]:
                        cand[y["e"]].append(y)
            return out, [start[x["id"]] + x["hold"] for x in nodes], max(start[x["id"]] + x["dur"] for x in nodes)
        if not ORDER:
            cases = []
            for (wake, same, call, slow, link_time, weight) in CASES:
                hold = [x["hold"] + slow * x["more"] + (call * len(x["fns"]) if x["own"] == "s" else 0.0) for x in nodes]
                dur = [h if x["own"] == x["e"] else x["dur"] * link_time for x, h in zip(nodes, hold)]
                edge = [[(k, dur[k] if x["e"] == "n" else dur[k] + (same if nodes[k]["e"] == x["e"] else wake) if wait else hold[k])
                         for k, wait in x["pre"].items()] for x in nodes]
                cases.append((hold, dur, edge, weight))

            def others(out):
                mark = 0.0
                for (hold, dur, edge, weight) in cases:
                    free, start, end = {e: 0.0 for e in "vspgyn"}, [0.0] * len(nodes), 0.0
                    for x in out:
                        j = x["id"]
                        at = free[x["e"]]
                        for k, d in edge[j]:
                            if start[k] + d > at:
                                at = start[k] + d
                        start[j], free[x["e"]] = at, at + hold[j]
                        end = max(end, at + dur[j])
                    mark += weight * end
                return mark
            ends, best, rng = [float(x["id"]) for x in nodes], None, np.random.RandomState(1)
            for n in range(ROUNDS + TRIES):
                if n < ROUNDS:
                    way = run(ends, True)[1]
                else:
                    a, size = rng.uniform(-3.0, best[4]), rng.choice([0.15, 0.4, 1.0])
                    way = [v + size * float(rng.randn()) if a < e < a + 6.0 else v for v, e in zip(best[2], best[3])]
                out, ends, end = run(way, False)
                mark = end + others(out)
                if best is None or mark <= best[0]:
                    best = (mark, [x["id"] for x in out], way, ends, end)
            cases.append(([x["hold"] for x in nodes], [x["dur"] for x in nodes], [[(k, step(nodes[k], x)) for k in x["pre"]] for x in nodes], 1.0))

            def queued(out, case):
                hold, dur, edge, _w = case
                lastq, start, why = {}, [0.0] * len(nodes), {}
                for x in out:
                    j, q = x["id"], lastq.get(x["e"])
                    at, by = (start[q] + hold[q], (q, True)) if q is not None else (0.0, None)
                    for k, d in edge[j]:
                        if start[k] + d >= at:
                            at, by = start[k] + d, (k, False)
                    start[j], why[j], lastq[x["e"]] = at, by, j
                j, pairs = max(range(len(nodes)), key=lambda k: start[k] + dur[k]), []
                while why[j]:
                    if why[j][1] and nodes[j]["e"] in "vsp":
                        pairs.append((why[j][0], j))
                    j = why[j][0]
                return pairs
            out = [nodes[k] for k in best[1]]
            mark = others(out)
            best = (mark, out)
            for n in range(SWAPS):
                if n % 4 == 0:
                    pairs = queued(out, cases[rng.randint(len(cases))])
                a, b = pairs[rng.randint(len(pairs))]
                place = {x["id"]: k for k, x in enumerate(out)}
                i, j = place[a], place[b]
                if i > j:
                    continue
                if all(place[k] < i for k in nodes[b]["pre"]):
                    new = out[:i] + [out[j]] + out[i:j] + out[j + 1:]
                elif all(place[k] > j for k in nodes[a]["post"]):
                    new = out[:i] + out[i + 1:j + 1] + [out[i]] + out[j + 1:]
                else:
                    continue
                m = others(new)
                if m < mark + HEAT * (1 - n / SWAPS) * rng.exponential():
                    out, mark = new, m
                    if m < best[0]:
                        best = (m, new)
            ORDER.extend(x["id"] for x in best[1])
        return [nodes[k] for k in ORDER]

    def finish():
        know = {e: {} for e in eng}
        cnt = {e: 0 for e in sem}
        for x in order():
            e = x["e"]
            if e == "n":
                x["tok"] = (x["s"], total[x["s"]], {})
                continue
            toks = [nodes[k]["tok"] for k, wait in x["pre"].items() if wait]
            for tok in sorted(toks, key=lambda y: (-len(y[2]), -y[1])):
                if know[e].get(tok[0], 0) < tok[1]:
                    top = max([y for y in toks if y[0] == tok[0]], key=lambda y: y[1])
                    eng[e].wait_ge(T.sem[top[0]], top[1])
                    for k, v in list(top[2].items()) + [top[:2]]:
                        know[e][k] = max(v, know[e].get(k, 0))
            for fn in x["fns"]:
                if x["own"] == e:
                    cnt[e] += 1
                    fn(eng[e]).then_inc(T.sem[sem[e]], 1)
                    total[sem[e]] = cnt[e]
                elif x["own"].startswith("dma"):
                    fn(eng[e]).then_inc(T.sem[x["s"]], 16)
                else:
                    fn(eng[e])
            x["tok"] = (x["s"], total[x["s"]], dict(know[e]))
        for s, v in total.items():
            if know["g"].get(s, 0) < v:
                g.wait_ge(T.sem[s], v)
    return op, batch, dma, send, land, finish


def bits(engines):
    return sum(1 << e for e in engines)


def helpers(topo, cores, rank):
    me = cores[rank]
    free = [c for c in topo.cores_of(me) if c != me and all(topo.may_write(c, o) for o in cores if o != me)]
    return [[c for c in free if topo.die(c) != topo.die(me)][0], [c for c in free if topo.die(c) == topo.die(me)][0]]


def carrier(t, q):
    return q % 2 if t > 1 else q // 3


def hand_on(g, core, T, topo):
    for rank in range(4):
        two = helpers(topo, T.cores, rank)
        if core not in two:
            continue
        n = 0
        for t in range(1, 4):
            dst = T.cores[(rank - 1 - t % 3) % 4]
            rid, pid, _se = topo.addr(dst)
            for q in [q for q in range(4) if two[carrier(t, q)] == core]:
                x = T["FT%d" % t][:, 1024 * q:1024 * q + 1024]
                g.wait_ge(T.sem["h%d%d" % (t, q)], len(topo.engines(T.cores[rank], core)))
                g.remote_dma(x, x, T.sem["sn%d" % t], T.sem["hl"], pid, rid, topo.mask(core, dst))
                n += len(topo.engines(core, dst))
        g.wait_ge(T.sem["hl"], n)


def rank_program(g, core, T, topo):
    rank = T.rank_of(core)
    if rank is None:
        return hand_on(g, core, T, topo)
    op, batch, dma, send, land, finish = make(g, T)
    cores = T.cores
    mine = helpers(topo, cores, rank)

    def A(x):
        return T[x[0]][:, x[1]:x[2]]

    def put(o, i, dst, rsem, lsem, en=None, more=(), dur=1.5):
        rid, pid, _se = topo.addr(dst)
        en = en or topo.engines(core, dst)
        send(lsem, len(en), [i] + list(more), lambda e: e.remote_dma(A(o), A(i), T.sem[rsem], T.sem[lsem], pid, rid, bits(en)), rsem, dur)

    def asker(t):
        return cores[(rank - 1 - t % 3) % 4]

    def seen(t):
        return (rank + 1 + t % 3) % 4

    def snapshot(t, quarters=range(4), lsem=None):
        for n, q in enumerate(quarters):
            put(("FT%d" % t, 1024 * q, 1024 * q + 1024), ("TAB", 1024 * q, 1024 * q + 1024), mine[carrier(t, q)], "h%d%d" % (t, q), lsem or "loc%d" % t,
                None, [("EHT", 0, 192)] if t == 1 else [], 2.5 + 1.0 * n)

    def w(n, a=0, b=16):
        return ("WF", WIDX[n] + a, WIDX[n] + b)

    pc = ("PC", 0, 17)

    def P(n):
        return T.PC[:, PCOL[n]:PCOL[n] + 1]

    def cost(out, sides, each, fix=FIX):
        n = 1
        for k in out.shape[1:]:
            n *= k
        if each is None:
            each = 0.5 if all(SCRATCH[x[0]][2] in (B16, F16, U16) for x in sides) else 1.0
        return CYC * max(LEAST, n * each) + fix

    def ts(o, i, s1, o0, s2=None, o1=None, ia=None, oa=None, more=(), part=None):
        rd = [i] + list(more)
        src, out = A(i) if ia is None else ia, A(o) if oa is None else oa
        if o1 is None:
            op("v", rd, [o], lambda e: e.tensor_scalar(out, src, s1, None, o0), cost(out, [o, i], None), part)
        else:
            op("v", rd, [o], lambda e: e.tensor_scalar(out, src, s1, s2, o0, o1), cost(out, [o, i], None), part)

    def tt(o, a, b, f, ia=None, ib=None, more=(), oa=None, lst=None):
        out = A(o) if oa is None else oa
        if lst:
            ia, more = A(a).indirect(A(lst)), [lst]
        op("v", [a, b] + list(more), [o], lambda e: e.tensor_tensor(out, A(a) if ia is None else ia, A(b) if ib is None else ib, f),
           (cost(out, [], GATHER, 0.05), 0.7 * cost(out, [], GATHER)) if lst else cost(out, [], 1.0 if SCRATCH[a[0]][0] != SB else 2.0))

    def act(o, i, f, ia=None, oa=None, more=(), part=None, price=None, **k):
        src, out = A(i) if ia is None else ia, A(o) if oa is None else oa
        op("s", [i] + list(more), [o], lambda e: e.activation(out, src, f, **k), price or cost(out, [], 1.0, SFIX), part)

    def cp(o, i, ia=None, oa=None, more=(), e="v", bias=None, part=None, price=None):
        src, out = A(i) if ia is None else ia, A(o) if oa is None else oa
        if e == "v":
            op("v", [i] + list(more), [o], lambda e: e.tensor_copy(out, src), price or cost(out, [o, i], None), part)
        elif bias is None:
            act(o, i, AF.Copy, ia, oa, more, part, price)
        else:
            act(o, i, AF.Identity, ia, oa, more, part, price, bias=bias)

    def lin(o, i, a, b, e, ia=None):
        if e == "v":
            ts(o, i, a, OP.mult, b, OP.add, ia=ia)
        else:
            act(o, i, AF.Identity, ia=ia, scale=a, bias=b)

    def gather(o, win, lst, e="v", bias=None):
        cp(o, win, ia=A(win).indirect(A(lst)), more=[lst], e=e, bias=bias, price=(cost(A(o), [], GATHER, 0.06), 0.7 * cost(A(o), [], GATHER)))

    def scatter(win, lst, i):
        cp(win, i, oa=A(win).indirect(A(lst)), more=[lst], price=(cost(A(i), [], SCATTER, 0.05), 0.85 * cost(A(i), [], SCATTER)))

    def scan(o, d0, d1, init, o0, o1):
        op("v", [d0, d1], [o], lambda e: e.tensor_tensor_scan(A(o), A(d0), A(d1), init, o0, o1), cost(A(o), [o, d0, d1], None))

    def mm(o, l, r, start, stop, oa=None, la=None, ra=None):
        out = A(o) if oa is None else oa
        op("p", [l, r], [o], lambda e: e.matmul(out, A(l) if la is None else la, A(r) if ra is None else ra, start, stop), max(64 * CYC, cost(out, [], 1.0, 0.0)) * PE / CYC)

    def iota(o, pattern, base, cm=0):
        op("g", [], [o], lambda e: e.iota(A(o), pattern, base, cm, allow_small_or_imprecise_dtypes=True), 0.14 + 2 * CYC * (o[2] - o[1]))

    def memset(o, v):
        op("v", [], [o], lambda e: e.memset(A(o), v), cost(A(o), [o], None))

    def ends(b, n=256):
        return T[b][:, 15:n:16]

    queued = [1.8]

    def load(n, dst, lo, hi, src, a, b, after=None):
        queued[0] = (1.8 if after else queued[0]) + 0.2 + (hi - lo) * (2 if SCRATCH[dst][2] == B16 else 4) / RATE
        dma("y", "ld%d" % n, [], [(dst, lo, hi)], lambda e: e.dma_start(T[dst][:, lo:hi], T[src][:, a:b]), queued[0], after)
    load(0, "EFT", 192, 448, "ef", 0, 256)
    load(1, "ZFT", 192, 448, "zf", 0, 256)
    load(4, "EHT", 192, 448, "eh", 0, 256)
    load(2, "TAB", 0, 2048, "tab", 0, 2048)
    load(3, "TAB", 2048, 4096, "tab", 2048, 4096)
    far = len(topo.engines(asker(0), core))
    land("qu", far, "QE", 0, 256, "qu", 2.5)
    land("qu", far, "QZ", 0, 256, "qu", 2.5)
    land("rp", len(topo.engines(cores[seen(0)], core)), "RP", 0, 16, "rp", 1.5)
    for t in range(1, 4):
        a, n = 192 - 64 * t, len(topo.engines(cores[seen(t)], core))
        land("qf%d" % t, len(topo.engines(asker(t), core)), "QF", a, a + 64, "qf%d" % t, HOP)
        land("qf%d" % t, len(topo.engines(asker(t), core)), "QY", a, a + 64, "qf%d" % t, HOP + 1 if t == 1 else 2 * HOP)
        land("rq%d" % t, n, "SF%d" % t, 0, 64, "rq%d" % t, HOP)
        land("sn%d" % t, sum(len(topo.engines(helpers(topo, cores, seen(t))[carrier(t, q)], core)) for q in range(4)), "FT%d" % t, 0, 4096, "h%d3" % t, 9.0)
        land("rz%d" % t, n, "RZ%d" % t, 0, 256, "rz%d" % t, HOP)
        land("rl%d" % t, n, "RL%d" % t, 0, 16, "rl%d" % t, LIST)

    z0 = ("ZFT", 192, 448)
    iota(("PJ", 0, 1), [[0, 1]], 0, 1)
    iota(("QX", 0, 160), [[1, 160]], -16)
    iota(("EXI", 0, 512), [[1, 32], [0, 16]], 0)
    iota(("Q4", 0, 128), [[16, 8], [0, 16]], 0)
    iota(("KC", 0, 256), [[0, 16], [-256, 16]], 3968)
    iota(("JM", 0, 256), [[0, 16], [1, 16]], 0)
    iota(("CI", 0, 48), [[16, 48]], 0)
    memset(("HF", 0, 1), 200.0)
    memset(("ST", 0, 1024), 0.0)
    for k in range(8):
        cp(("OCC", 512 * k, 512 * k + 512), ("ST", 0, 512), e="s", bias=0.4)

    def c(n):
        return ("PC", PCOL[n], PCOL[n] + 1)

    def col(n, i, s1, o0, s2=None, o1=None):
        ts(c(n), c(i), s1, o0, s2, o1, more=[c("M0")] if n in ("WP", "WD") else [])
    ts(("PJ", 1, 2), ("PJ", 0, 1), 15, OP.bitwise_and)
    ts(("PJ", 2, 3), ("PJ", 0, 1), 31, OP.bitwise_and)
    cp(c("P"), ("PJ", 0, 1))
    cp(c("I"), ("PJ", 1, 2))
    cp(c("P32"), ("PJ", 2, 3))
    tt(c("G"), c("P"), c("I"), OP.subtract)
    col("M0", "I", 0.0, OP.is_equal)
    col("M1", "I", 1.0, OP.is_equal)
    col("EV", "P32", 16.0, OP.is_lt)
    col("OD", "P32", 16.0, OP.is_ge)
    col("SG", "I", -400.0, OP.mult, -200.0, OP.add)
    col("F0", "M0", 832 * FINE, OP.mult, -512 * FINE, OP.add)
    col("F1", "M0", -192 * FINE, OP.mult, -512 * FINE, OP.add)
    col("MN", "M0", -1.0, OP.mult)
    col("WP", "M1", -2048.0, OP.mult, P("M0"), OP.add)
    col("WD", "M1", -128.0, OP.mult, P("M0"), OP.add)
    col("N1", "I", 1.0, OP.not_equal)
    col("LO", "M1", 127.0, OP.mult)
    col("HI", "M1", -128.0, OP.mult, 256.0, OP.add)
    qx = ("QX", 16, 144)
    ts(("PID", 0, 128), qx, P("P"), OP.is_equal, more=[pc])
    ts(("NID", 0, 128), qx, P("P"), OP.is_equal, -1.0, OP.mult, more=[pc])
    ts(("XV", 0, 144), ("QX", 0, 144), P("G"), OP.is_equal, W1, OP.mult, more=[pc])
    for n, f in (("BE", "EV"), ("BD", "OD")):
        ts((n, 0, 160), ("QX", 0, 160), P("P"), OP.is_equal, P(f), OP.mult, more=[pc])
    ts(("EX", 0, 512), ("EXI", 0, 512), P("P32"), OP.is_equal, more=[pc])
    ts(("BO", 0, 128), ("Q4", 0, 128), P("G"), OP.is_equal, more=[pc])
    ts(("BOH", 0, 128), ("Q4", 0, 128), P("G"), OP.is_equal, more=[pc])
    act(("TU", 0, 128), ("JM", 0, 128), AF.Sigmoid, more=[pc], price=1.5, bias=P("SG"), scale=400.0)
    ts(("SCM", 0, 256), ("JM", 0, 256), 0.5, OP.is_gt)
    ts(("T2", 0, 128), ("JM", 0, 128), P("I"), OP.is_equal, more=[pc])
    for k in range(16):
        ts(("RO", 128 * k, 128 * k + 128), ("BOH", 0, 128), T.T2[:, k:k + 1], OP.mult, more=[("T2", 0, 128)])
    ts(("PIH", 0, 128), qx, P("P"), OP.is_equal, more=[pc])
    ts(("BO8", 0, 128), ("BO", 0, 128), BIG, OP.mult)
    tt(("T1", 0, 128), ("TU", 0, 128), ("T2", 0, 128), OP.subtract)
    ts(("CM", 0, 256), ("JM", 0, 256), P("I"), OP.not_equal, 131072.0, OP.mult, more=[pc])
    tt(("TRI", 0, 128), ("T1", 0, 128), ("BO8", 0, 128), OP.mult)
    memset(("RS", 0, 256), -20000.0)
    ts(("RS", 0, 256), ("CI", 0, 16), P("I"), OP.add, LOOK - OFF, OP.add, oa=T.RS[:, 0:256:16], more=[pc])
    if SEARCH > 1:
        ts(("AB", 0, 256 * SEARCH - 256), ("ST", 0, 256 * SEARCH - 256), P("N1"), OP.add, more=[pc])
    ts(("DW", 0, 48), ("CI", 0, 48), P("I"), OP.add, 768.0 - 2047.0, OP.add, more=[pc])
    memset(("DB", 0, 256), 0.0)
    memset(("KD", 0, 256), -W1 / 2)
    ts(("NIH", 0, 128), qx, P("P"), OP.is_equal, -1.0, OP.mult, more=[pc])
    for n, f in (("X0", "M0"), ("XN", "MN"), ("XO", "M1"), ("XP", "WP"), ("XD", "WD")):
        ts((n, 0, 144), ("QX", 0, 144), P("G"), OP.is_equal, P(f), OP.mult, more=[pc])
    ts(("BO0", 0, 128), ("Q4", 0, 128), P("G"), OP.is_equal, P("M0"), OP.mult, more=[pc])
    ts(("MB", 0, 192), ("JM", 0, 192), P("I"), OP.is_equal, 60000.0, OP.mult, more=[pc])

    def ask(dst, e_from, e_to, z_from, z_to, rsem, lsem, dur):
        rid, pid, _se = topo.addr(dst)
        en = topo.engines(core, dst)
        parts = ((en[:len(en) // 2], e_from, e_to), (en[len(en) // 2:], z_from, z_to))
        send(lsem, len(en), [e_from, z_from], lambda e: e.remote_dma_fused(
            [RemoteDMATransfer(dst_ids=[DstId(rid=rid, pnc=pid)], dma_engine_mask=bits(m), remote_sem=T.sem[rsem], src=A(i), dst=A(o)) for (m, i, o) in parts],
            local_sem=T.sem[lsem]), rsem, dur)

    def ask_fresh(t):
        a = 192 - 64 * t
        ask(cores[seen(t)], ("SEF", a, a + 64), ("QF", a, a + 64), ("ZFT", a, a + 64), ("QY", a, a + 64), "qf%d" % t, "loc7", 2.0)
    cp(("EFO", 0, 256), ("EFT", 192, 448))
    ask(cores[seen(0)], ("EFO", 0, 256), ("QE", 0, 256), z0, ("QZ", 0, 256), "qu", "loc0", 6.5)
    iota(("IOT", 0, 1024), [[1, 1024]], 0)
    iota(("JR", 0, 192), [[1, 192]], 0)
    for k, (o, i) in enumerate((("EFT", "ef"), ("ZFT", "zf"), ("EHT", "eh"))):
        load(5 + k, o, 0, 192, i, 832, 1024, "loc0" if k == 0 else None)
    for (a, b, f) in ((0, 192, "F0"), (192, 608, "F1"), (608, 1024, "F1")):
        act(("FN", a, b), ("IOT", a, b), AF.Identity, more=[pc], scale=FINE, bias=P(f))
    cp(("SEH", 0, 192), ("EHT", 0, 192))
    cp(("SEF", 0, 192), ("EFT", 0, 192))

    def turn(o, z):
        n = z[2] - z[1]
        mm(("ZP", 0, 128), z, ("PID", 0, 128), True, True, oa=T.ZP[0:n, 0:128])
        cp((o, 0, 128), ("ZP", 0, 128), ia=T.ZP[0:n, 0:128], oa=T[o][0:n, :], e="s")

    def expand(o, z, on_s):
        n = 16 * (z[2] - z[1])
        batch(True)
        for k in range(16):
            cp((o, 0, n), z, oa=T[o][:, k:n:16], e="s" if k < on_s else "v", part=(o,) + z)
        batch(False)

    units, tab = [0], ("TAB", 0, 4096)

    def s_unit(dst, m, win, lst, col0, zt, row, n=2):
        u = units[0] % 2
        units[0] += 1
        d, gb = ("D%d" % u, 0, 256 * n), ("GB%d" % u, 0, 256 * n)
        mm(d, (zt, 0, 128), ("EX", 0, 512), True, False, la=T[zt][row:row + 16 * n, :], ra=T.EX[row:row + 16 * n, 0:256 * n])
        gather(gb, win, (lst, col0, col0 + 16 * n), e="s")
        mm(d, ("NID", 0, 128), gb, False, True)
        act((dst, 256 * m, 256 * (m + n)), d, AF.Sigmoid, oa=T[dst][:, m:m + n, :], more=[("HF", 0, 1)], bias=T.HF[:, 0:1], scale=400.0)

    def v_block(dst, m, win, lst, col0, zx, b):
        tt((dst, 256 * m, 256 * m + 256), win, (zx, 256 * b, 256 * b + 256), OP.is_le, oa=T[dst][:, m, :], lst=(lst, col0, col0 + 16))

    def key_open(key, a=0, b=256):
        mm((key, a, b), ("BO", 0, 128), ("KC" if key == "KH" else "KD", a, b), True, False)

    def sums(key, src, m0, m1, last=False):
        batch(True)
        for k in range(16):
            mm((key, 16 * m0, 16 * m1), ("XV", 0, 144), (src, 256 * m0, 256 * m1), False, last and k == 15,
               la=T.XV[:, 16 - k:144 - k], ra=T[src][:, m0:m1, 16 * k:16 * k + 16])
        batch(False)

    def slots_in(parts):
        ep, tr = ("EP", 0, 256), ("TR", 0, 256)
        batch(True)
        for (src, b0, b1, h) in parts:
            ts(ep, src, -2048.0, OP.add, oa=T.EP[:, b0:b1, 16 * h:16 * h + 16])
        batch(False)
        op("v", [ep], [tr], lambda e: e.transpose(T.TR[:, :, :], T.EP[:, :, :]), 128 * CYC + FIX)

    def slots_mm():
        batch(True)
        for (h2, h, l, a) in ((0, 0, "BE", 16), (0, 1, "BE", 0), (1, 1, "BD", 16), (1, 0, "BD", 32)):
            mm(("KH", 128 * h2, 128 * h2 + 128), (l, a, a + 128), ("TR", 0, 256), False, False, ra=T.TR[:, :, 16 * h:16 * h + 16])
        batch(False)

    def spread(src, start, stop):
        batch(True)
        for k in range(16):
            mm(("PA", 0, 256), ("RO", 128 * k, 128 * k + 128), src, start, start or (stop and k == 15), oa=T.PA[:, k:256:16])
        batch(False)

    def pick(x, src, a, start, stop):
        batch(True)
        for k in range(16):
            mm(("PB", a, a + (src[2] - src[1]) // 16), (x, 16 - k, 144 - k), src, start and k == 0, stop and k == 15, ra=T[src[0]][:, src[1] + k:src[2]:16])
        batch(False)

    def slot(t):
        scan(("SH", 0, 256), ("SCM", 0, 256), ("KH", 0, 256), 0.0, OP.mult, OP.max)
        cp(("IW", 0, 16), ("SH", 0, 256), ia=ends("SH"))
        ts(("IW", 16, 32), ("IW", 0, 16), 4095, OP.bitwise_and)
        ts(("WH", 0, 16), ("IW", 16, 32), -2048.0, OP.add)
        ts(w("HG"), ("SH", 0, 256), 9 * W1, OP.is_ge, 2 * BIG, OP.mult, ia=ends("SH"))
        tt(w("SW"), ("WH", 0, 16), w("HG"), OP.add)
        ts(("IW", 32, 48), ("IW", 0, 16), 16, OP.arith_shift_right)
        tt(w("HN"), ("IW", 32, 48), w("HG"), OP.min)
        spread(("WH", 0, 16), True, True)
        cp(("SR", 0, 256), ("PA", 0, 256), e=ON["SR"])
        mm(("CN", 0, 256), ("PID", 0, 128), ("CM", 0, 256), True, False)
        mm(("CN", 0, 256), ("PIH", 0, 128), ("SR", 0, 256), False, False)
        mm(("PA", 0, 256), ("PID", 0, 128), ("DB", 0, 256), True, False)
        if t == 0:
            return
        cp(("SL", 0, 16), ("IW", 16, 32))
        occ, sl, og = ("OCC", 0, 4096), ("SL", 0, 16), ("OG", 0, 256)
        act(og, occ, AF.Identity, ia=A(occ).indirect(A(sl)), more=[sl], price=(0.4, 0.25), scale=4 / FINE, bias=1536 - 2 / FINE)
        pick("XO", og, 0, True, True)
        pick("XO", og, 16, True, False)
        mm(("PB", 16, 32), ("NIH", 0, 128), ("FW", 0, 16), False, True)
        lin(("BL", 0, 16), ("PB", 0, 16), 1.0, -1024.0, ON["BL"])
        ts(w("OC"), ("PB", 0, 16), 1024.0, OP.is_ge, 1 / 128, OP.mult)
        tt(w("Y"), ("PB", 16, 32), w("OC"), OP.mult)
        gather(("DB", 256, 512), ("ST", 0, 1024), ("BL", 0, 16), e="s", bias=-255.0)
        pick("X0", ("DB", 256, 512), 32, True, False)
        pick("XN", ("DB", 0, 256), 32, False, True)
        tt(w("X"), ("PB", 32, 48), w("OC"), OP.mult)

    def mark(t):
        cp(("PM", 0, 192), ("DB", 64, 256), e="s", bias=128.0)
        cp(("ST", 192 - 64 * t, 256 - 64 * t), ("DB", 0, 64), e="s", bias=128.0)
        for k in range(0, 12, 12 // PIECES[1]):
            scatter(("ST", 0, 1024), ("FL", k, k + 12 // PIECES[1]), ("PM", 16 * k, 16 * k + 192 // PIECES[1]))

    def lanes(t):
        return z0 if t == 0 else ("ZL%d" % t, 0, 256)

    def claims(t):
        wl = ("WL%d" % t, 0, 16)
        if t:
            sf, far = ("SF%d" % t, 0, 256), ends("SF%d" % t)
        else:
            sf, far = ("RP", 0, 16), T.RP[:, :]
        turns = [m + k for m in ([0] + fours(4, SPLIT[1]) if t else range(0, 16, 4)) for k in range(4)]
        for m in turns:
            n, x = 256 - 16 * m, 16 * m + 15 if t else m
            ts(("EE", 256 * m, 256 * m + n), ("SR", 16 * m, 256), A(w("SW", m, m + 1)), OP.subtract, T[sf[0]][:, x:x + 1], OP.is_equal,
               oa=T.EE[:, m, 0:n], more=[w("SW"), (sf[0], x, x + 1)])
            if m < 15:
                mm(("CN", 16 * m + 16, 256), ("BO8", 0, 128), ("EE", 256 * m, 256 * m + n), False, False, ra=T.EE[:, m, 16:n])
            if m % 4 == 3:
                mm(("CN", 16 * m - 48, 16 * m + 16), ("TRI", 0, 128), ("EE", 256 * m - 768, 256 * m + 256), False, m == turns[-1], ra=T.EE[:, m - 3:m + 1, 0:16])
        lin(w("FA"), sf, 1 / W1, 8.0, "s", far)
        tt(w("FC"), w("FA"), sf, OP.min, ib=far)
        tt(("WH", 32, 48), w("FC"), w("HN"), OP.max)
        spread(("WH", 32, 48), False, False)
        cs = ("CS", 0, 256)
        scan(cs, ("RS", 0, 256), ("CN", 0, 256), -20000.0, OP.max, OP.min)
        lin(wl, cs, 1.0, OFF, ON["WL"], ends("CS"))
        win = ("WH", 16, 32)
        ts(win, cs, 4096.0 - OFF, OP.is_lt, 128.0, OP.mult, ia=ends("CS"))
        spread(win, False, t == 0)
        if t:
            tt(("WH", 48, 64), win, w("X"), OP.mult)
            spread(("WH", 48, 64), False, True)
            tt(w("T2"), win, w("Y"), OP.mult)
            tt(w("TF"), w("T2"), ("FW", 0, 16), OP.add)
            lin(("TL", 0, 16), w("TF"), 1.0, -1024.0, ON["TL"])
        if t < 3:
            put(("RL%d" % (t + 1), 0, 16), wl, asker(t + 1), "rl%d" % (t + 1), "loc%d" % (8 + t))
        scatter(("TAB", 0, WT), wl, lanes(t))
        if t < 3:
            cp(("TAB", 4096, LOOK), ("TAB", 0, LOOK - 4096), e="s")
        if t < 2:
            snapshot(t + 2)
        if t:
            cp(("STN", 0, 256), ("PA", 0, 256), e="s")
            scatter(("ST", 0, 1024), ("TL", 0, 16), ("STN", 0, 256))
        else:
            cp(("ST", 192, 448), ("PA", 0, 256), e="s")
        act(("OCC", 0, WT), ("FR%d" % t, 0, 256) if t else ("FN", 192, 448), AF.Sigmoid, oa=T.OCC[:, :].indirect(A(wl)), more=[wl], price=(0.87, 0.7))

    def fresh(t):
        a = 192 - 64 * t
        turn("ZTG", ("QY", a, a + 64))
        turn("ZTF", ("ZFT", a, a + 64))
        cp(("ZL%d" % t, 0, 64), ("ZFT", a, a + 64), e="s")
        cp(("FR%d" % t, 0, 64), ("FN", a, a + 64), e="s")
        for (dst, lst, zt) in (("CF", "QF", "ZTG"), ("CH", "SEH", "ZTF")):
            for u in range(2):
                s_unit(dst, 2 * u, tab, lst, a + 32 * u, zt, 32 * u)
        key_open("KF", 0, 64)
        sums("KF", "CF", 0, 4, True)
        key_open("KH")
        sums("KH", "CH", 0, 4)

    def select(t):
        U, lo, n = 256 * t, 256 - 64 * t, 16 * t
        if t >= SEARCH:
            return search(t, lo, U + 192)
        ts(("FB", 0, U), ("ST", lo, lo + U), 128.0, OP.is_lt)
        scan(("VB", 0, U), ("AB", 0, U), ("FB", 0, U), 0.0, OP.mult, OP.add)
        mm(("PA", 0, 1), ("BO0", 0, 128), ("VB", U - 1, U), True, True)
        pick("XP", ("VB", 0, U), 0, True, True)
        ts(("LW", 0, 192), ("JR", 0, 192), T.PA[:, 0:1], OP.subtract, float(lo + U), OP.add, more=[("PA", 0, 1)])
        tt(("LF", 0, n), ("PB", 0, n), ("DW", 0, n), OP.min)
        ts(("LU", 0, n), ("LF", 0, n), 2047.0, OP.add)
        scatter(("LW", 0, 1536), ("LU", 0, n), ("IOT", lo, lo + U))
        scan(("WS", 0, 192), ("MB", 0, 192), ("LW", 0, 192), 0.0, OP.max, OP.min)
        cp(("FL", 0, 12), ("WS", 0, 192), ia=ends("WS", 192))

    def search(t, lo, R):
        jr, mb, n = ("JR", 0, 192), ("MB", 0, 192), 16 * t + 16
        memset(("VB", R, R + 64), 2000.0)
        ts(("FB", 0, R), ("ST", lo, lo + R), 128.0, OP.is_lt)
        scan(("VB", 0, R), ("FB", 0, R), ("FB", 0, R), 0.0, OP.add, OP.max)
        op("v", [("MB", 0, n), ("VB", 0, R + 64)], [("LF", 0, n)],
           lambda e: e.tensor_tensor_scan(T.LF[:, 0:n], T.MB[:, 0:n], T.VB[:, 15:R + 64:16], 0.0, OP.max, OP.min), 64 * CYC + FIX)
        pick("XO", ("VB", 0, R), 0, True, True)
        cp(("LW", 0, R // 16), ("PB", 0, R // 16))
        for k in range(t + 1):
            ts(("YA", 192 * k, 192 * k + 192), jr, T.LF[:, 16 * k + 15:16 * k + 16], OP.is_ge, 16.0, OP.mult, more=[("LF", 0, n)])
            mm(("PA", 0, 192), ("BO", 0, 128), ("YA", 192 * k, 192 * k + 192), k == 0, k == t)
        for k in range(t + 1):
            mm(("CN", 0, 192), ("BO", 0, 128), ("YA", 192 * k, 192 * k + 192), k == 0, False)
        scan(("WS", 0, 192), mb, ("PA", 0, 192), 0.0, OP.max, OP.min)
        ts(("LU", 0, 12), ("WS", 0, 192), 1 / 16, OP.mult, ia=ends("WS", 192))
        tt(("STN", 0, 192), ("LW", 0, R // 16), jr, OP.is_le, lst=("LU", 0, 12))
        mm(("CN", 0, 192), ("BO", 0, 128), ("STN", 0, 192), False, True)
        scan(("WS", 0, 192), mb, ("CN", 0, 192), 0.0, OP.max, OP.min)
        ts(("FL", 0, 12), ("WS", 0, 192), float(lo), OP.add, ia=ends("WS", 192))

    def entries(tab, a, o):
        tt((a, 0, 192), (tab, 0, 1024), ("DB", 64, 256), OP.add, lst=("FL", 0, 12))
        cp((o, 0, 192), (a, 0, 192))

    def blocks(dst, key, first, split, win, lst, col0, zt, zx, zx0, out=None):
        for m in range(first, split, 2):
            s_unit(dst, m, win, lst, 16 * (m - col0), *zt(m), min(2, split - m))
        for m in range(15, split - 1, -1):
            v_block(dst, m, win, lst, 16 * (m - col0), zx, m - zx0)
        for n, m in enumerate(fours(first, split)):
            if out:
                bank = (key, "ZP")[n % 2]
                key_open(bank, 16 * m, 16 * m + 64)
                sums(bank, dst, m, m + 4, True)
                scan((out, 16 * m, 16 * m + 64), ("SCM", 0, 64), (bank, 16 * m, 16 * m + 64), 0.0, OP.mult, OP.max)
            else:
                sums(key, dst, m, m + 4, n == 3 - first // 4)

    def fours(low, split):
        high, out = 16, []
        while high > low:
            if split - low >= high - split:
                out.append(low)
                low += 4
            else:
                high -= 4
                out.append(high)
        return out

    def penalties(t):
        ft, fl, zl, a = "FT%d" % t, ("FL", 0, 12), "ZL%d" % t, 192 - 64 * t
        gather(("DB", 64, 256), ("ST", 0, 1024), fl, e=ON["DL"][t - 1])
        gather((zl, 64, 256), ("ZFT", 0, 1024), fl, e=ON["ZL"][t - 1])
        if t < 3:
            put(("RZ%d" % (t + 1), 0, 256), (zl, 0, 256), asker(t + 1), "rz%d" % (t + 1), "loc%d" % (4 + t))
        scan(("SQ", 0, 64), ("SCM", 0, 64), ("KF", 0, 64), 0.0, OP.mult, OP.max)
        put(("SF%d" % t, 0, 64), ("SQ", 0, 64), asker(t), "rq%d" % t, "loc%d" % (11 + t))
        if t == 1:
            ask_fresh(2)
            ask_fresh(3)
        entries("EHT", "EI", "EHO")
        entries("EFT", "FI", "EFO")
        ts(("EM", 0, 192), ("EI", 0, 192), 4095, OP.bitwise_and)
        expand("ZX", (zl, 16 * min(SPLIT), 256), ZS)
        turn("ZT", (zl, 64, min(192, 16 * max(SPLIT))))
        if max(SPLIT) > 12:
            turn("ZTQ", (zl, 192, 16 * max(SPLIT)))
        for k in range(0, 16, 16 // PIECES[0]):
            scatter((ft, 0, WT), ("RL%d" % t, k, k + 16 // PIECES[0]), ("RZ%d" % t, 16 * k, 16 * k + 256 // PIECES[0]))
        cp((ft, 4096, LOOK), (ft, 0, LOOK - 4096), e=ON["FT"])
        slots_in(((("EHT", a, a + 64), 0, 4, 0), (("EM", 0, 64), 4, 8, 0), (("EM", 64, 192), 0, 8, 1)))
        slots_mm()

        def zt(m):
            return ("ZT", 16 * m - 64) if m < 12 else ("ZTQ", 16 * m - 192)
        blocks("CH", "KH", 4, SPLIT[0], ("TAB", 0, LOOK), "EHO", 4, zt, "ZX", min(SPLIT))
        blocks("CF", "KF", 4, SPLIT[1], (ft, 0, LOOK), "EFO", 4, zt, "ZX", min(SPLIT), "SF%d" % t)
        lin(("FW", 4, 16), ("WS", 0, 192), 1.0, 1024.0 + (a + 64 if t >= SEARCH else 0), ON["FW"], ends("WS", 192))
        lin(("FW", 0, 4), ("DW", 0, 4), 1.0, a + 1024.0 + 2047.0 - 768.0, ON["FW"])
        gather(("FR%d" % t, 64, 256), ("FN", 0, 1024), fl, e="s")
        slot(t)
        if t < 3:
            mark(t)

    def penalties_0():
        h, f = SPLIT0
        turn("ZT", ("ZFT", 192, 192 + 16 * h))
        expand("ZX", ("ZFT", 192 + 16 * h, 448), 16)
        cp(("EHO", 0, 256), ("EHT", 192, 448))
        slots_in(((("EHT", 192, 320), 0, 8, 0), (("EHT", 320, 448), 0, 8, 1)))
        ask_fresh(1)
        snapshot(1, range(EARLY))
        key_open("KH")
        key_open("KF")
        slots_mm()
        turn("ZTQ", ("QZ", 0, 16 * f))
        expand("ZXQ", ("QZ", 16 * f, 256), ZQ)
        for m in range(0, 4, 2):
            s_unit("CH", m, tab, "EHO", 16 * m, "ZT", 16 * m)
        sums("KH", "CH", 0, 4)
        blocks("CF", "KF", 0, f, tab, "QE", 0, lambda m: ("ZTQ", 16 * m), "ZXQ", f)
        blocks("CH", "KH", 4, h, tab, "EHO", 0, lambda m: ("ZT", 16 * m), "ZX", h)
        scan(("SF", 0, 256), ("SCM", 0, 256), ("KF", 0, 256), 0.0, OP.mult, OP.max)
        cp(("SP", 0, 16), ("SF", 0, 256), ia=ends("SF"))
        put(("RP", 0, 16), ("SP", 0, 16), asker(0), "rp", "loc11")
        snapshot(1, range(EARLY, 4), "loc15")
        for k, (o, i) in enumerate((("ZFT", "zf"), ("EHT", "eh"), ("EFT", "ef"))):
            load(8 + k, o, 448, 1024, i, 256, 832, "loc11" if k == 0 else None)
        put(("RZ1", 0, 256), z0, asker(1), "rz1", "loc4")
        slot(0)

    penalties_0()
    for t in range(4):
        if t:
            fresh(t)
            select(t)
            penalties(t)
        claims(t)
    def store(e, n, o, oa, i, ia, dur):
        dma(e, "out%d" % n, [i], [o], lambda q: q.dma_start(oa, ia), dur)
    store("s", 4, ("SF", 0, 256), T.SF[:, :], ("OCC", 0, 4096), T.OCC[0:128:16, 0:4096], 2.5)
    lin(("OG", 0, 256), ("SF", 0, 256), 4 / FINE, 1536 - 2 / FINE, "s")
    ts(("SF1", 0, 256), ("OG", 0, 256), -1024.0, OP.add, -1.0, OP.max)
    for h in range(2):
        a, b = 2048 * h, 2048 * h + 2048
        store("y", h, ("yt", a, b), T.yt[:, a:b], ("TAB", a, b), T.TAB[:, a:b], 3.6 + 1.9 * h)
    ts(("YA", 0, 1024), ("ST", 0, 1024), P("LO"), OP.max, P("HI"), OP.min, more=[pc])
    batch(True)
    for k in range(16):
        a = (64 * k + 192) % 1024
        mm(("PB", 0, 64), ("XD", 16 - k, 144 - k), ("YA", a, a + 64), k == 0, k == 15)
    batch(False)
    store("y", 2, ("yo", 0, 4096), T.yo[:, :], ("SF1", 0, 256), T.SF1[:, :], 2.5)
    cp(("YD", 0, 64), ("PB", 0, 64), e="s", bias=16256.0)
    store("s", 3, ("yd", 0, 1024), T.yd[:, :], ("YD", 0, 64), T.YD[:, :], 2.5)
    finish()
